import numpy as np, ml_dtypes
CORES = [3,11,19,27,35,43,51,59]
N = 8
import mx_ref
BF = ml_dtypes.bfloat16
def gentries(a):
    return np.ascontiguousarray(a.reshape(8, 16, -1).transpose(0, 2, 1)).reshape(8, -1)
def gtable(e):
    e = np.asarray(e); return np.ascontiguousarray(e.reshape(8, -1, 16).transpose(0, 2, 1)).reshape(128, -1).astype(np.int32)
def cols(t, e):
    v = np.concatenate([t.reshape(128, -1, 4), np.zeros((128, 1, 4), BF)], axis=1)
    return np.ascontiguousarray(v[:, e]).reshape(128, -1)
def gcols(t, e):
    v = np.concatenate([t.reshape(8, 16, -1, 4), np.zeros((8, 16, 1, 4), BF)], axis=2)
    return np.ascontiguousarray(np.stack([v[g][:, e[g]] for g in range(8)])).reshape(128, -1)
def tile(rs):
    return np.stack(rs, axis=2).reshape(128, -1).astype(BF)
def cut(t, i, w=512):
    return t[:, w * i:w * i + w]
def pick(q, e):
    c = np.concatenate([q[0].reshape(128, -1, 4), np.zeros((128, 1, 4), np.uint8)], axis=1); s = np.concatenate([q[1], np.ones((16, 1), np.uint8)], axis=1)
    return (np.ascontiguousarray(c[:, e].reshape(128, -1)), np.ascontiguousarray(s[:, e]))
def join(*qs):
    return (np.concatenate([q[0] for q in qs], axis=1), np.concatenate([q[1] for q in qs], axis=1))
def put(q, e, v):
    c, s = q[0].reshape(128, -1, 4).copy(), q[1].copy(); c[:, e] = v[0].reshape(128, -1, 4); s[:, e] = v[1]
    return (c.reshape(128, -1), s)
def pk(c, s):
    return (np.ascontiguousarray(c), mx_ref.live(s))
def emit(q):
    return q[0], q[1]
def packed(v, rng):
    q = [mx_ref.quantize(np.ascontiguousarray(v[r])) for r in range(N)]
    return np.stack([a for a, b in q]), np.stack([mx_ref.plane(b, rng) for a, b in q])
def values_of_codes():
    e, c = np.zeros((128, 128, 4), np.float32), np.zeros((128, 2, 4), np.uint8)
    e[np.arange(128), np.arange(128), 0] = 1
    c[:127, :, 0] = np.arange(256).reshape(2, 128).T[:127]
    return mx_ref.matmul(mx_ref.quantize(e.reshape(128, 512).astype(BF)), (c.reshape(128, 8), np.full((16, 2), 127, np.uint8))).T.reshape(-1).astype(np.float64)
CODE_VALUE, SCALE_VALUE = values_of_codes(), 2.0 ** (np.arange(256) - 127.0)
def decode(q):
    return (CODE_VALUE[q[0]].reshape(16, 8, -1, 4) * SCALE_VALUE[q[1]][:, None, :, None] + 0.0).reshape(128, -1).astype(np.float32)
def f(rng, *shape):
    return mx_ref.flush((rng.standard_normal(shape, dtype=np.float32) * np.exp2(rng.integers(-2, 3, shape[:-1] + (1,)))).astype(BF))
def wide(rng, *shape, cols=0):
    v = rng.standard_normal(shape, dtype=np.float32) * np.exp2(rng.integers(-12, 13, shape)).astype(np.float32)
    if cols: v *= np.repeat(np.exp2(rng.integers(-cols, cols + 1, shape[:-2] + (1, shape[-1] // 4))) * (rng.random(shape[:-2] + (1, shape[-1] // 4)) > 0.0625), 4, axis=-1).astype(np.float32)
    return mx_ref.flush(v.astype(BF))
MC, P, A, K, R = 1024, 512, 256, 48, 3
def numbers_of(rng):
    return {"m": np.array(f(rng, N, 128, 4 * MC)), "x": np.array(f(rng, N, 128, 4 * P)), "u": np.array(f(rng, N, 128, 512)), "v": np.array(f(rng, N, 128, 512))}
def weights(rng, w):
    c, p = packed(w, rng)
    return {"wc": c, "ws": p}
def still(rng):
    w = np.zeros((N, 128, 4, 128, 4), np.float32)
    i = np.arange(128)
    for b in range(4): w[:, i, b, i, b] = 32
    return weights(rng, w.reshape(N, 128, 2048).astype(BF))
def signs(rng):
    return np.stack([rng.permutation(8) % 2 * 2.0 - 1.0 for r in range(N)])
def mixed(rng, t):
    n = rng.integers(0, 2 * K + 1, (R, 8))
    n[0] = rng.permutation(np.concatenate([[0, K - 1, K, K + 1, 2 * K], n[0, :3]]))
    o = []
    for g in range(8):
        known = t[g]
        for i in range(R):
            new = np.setdiff1d(np.arange(MC), known)
            e = rng.permutation(np.concatenate([rng.choice(known, A - n[i, g], replace=False), rng.choice(new, n[i, g], replace=False)]))
            o.append(e)
            known = np.union1d(known, e)
    return np.stack(o).reshape(8, R * A)
def exact(rng, t, n):
    o, sure, out = [], t, np.setdiff1d(np.arange(MC), t)
    for i in range(R):
        e = rng.permutation(np.concatenate([rng.choice(sure, A - n, replace=False), rng.choice(out, n, replace=False)]))
        miss = np.isin(e, out)
        served = e[miss][:K]
        sure = np.concatenate([e[~miss], served])
        out = np.setdiff1d(out, served)
        o.append(e)
    return np.concatenate(o)
def draw_tags(rng):
    return np.stack([np.stack([rng.permutation(MC)[:P] for g in range(8)]) for r in range(N)])
def lists_of(rng):
    t = draw_tags(rng)
    return {"tg": np.stack([gtable(t[r]) for r in range(N)]), "ad": np.stack([gtable(mixed(rng, t[r])) for r in range(N)])}
def held(l, r):
    t, a = gentries(l["tg"][r]), gentries(l["ad"][r])[:, :A]
    return np.stack([np.isin(t[g], a[g]) for g in range(8)])
def fine(rng, v, s):
    v = v.astype(np.float32).reshape(N, 8, 16, -1, 4)
    g = ((s[..., None] >> np.arange(8)) & 1) * np.exp2(np.arange(8) - 23.0)
    v[:, :, 0] = 0
    v[:, :, 0, :, 0] = 1
    v[:, :, 8] = g[..., :4]
    v[:, :, 9] = g[..., 4:]
    a = v[:, :, 10:].shape
    v[:, :, 10:] = rng.integers(4, 8, a) * rng.choice([-1.0, 1.0], a) * 2.0 ** -20
    return v.reshape(N, 128, -1).astype(BF)
def setup_inputs(rng):
    return {**numbers_of(rng), **weights(rng, f(rng, N, 128, 2048)), **lists_of(rng)}
def setup_inputs_full(rng):
    d = {**numbers_of(rng), **weights(rng, f(rng, N, 128, 2048))}
    t = draw_tags(rng)
    e = rng.permutation(N)
    ad = []
    for r in range(N):
        kind = rng.permutation(8)
        o = []
        for g in range(8):
            if r == e[0]: o.append(exact(rng, t[r, g], A))
            elif r == e[1]: o.append(exact(rng, t[r, g], 0))
            elif kind[g] < 6: o.append(exact(rng, t[r, g], [0, 1, K - 1, K, K + 1, A][kind[g]]))
            elif kind[g] == 6: o.append(rng.permutation(MC)[:R * A])
            else: o.append(np.concatenate([rng.choice(np.setdiff1d(np.arange(MC), t[r, g]), A, replace=False)] + [rng.choice(t[r, g], A, replace=False) for i in range(R - 1)]))
        ad.append(gtable(np.stack(o)))
    return {**d, "tg": np.stack([gtable(t[r]) for r in range(N)]), "ad": np.stack(ad)}
def setup_inputs_ties(rng):
    d = setup_inputs(rng)
    e = rng.permutation(N)
    for r in range(N):
        k = np.zeros(P, int) if r == e[0] else rng.permutation(P) % 3
        d["x"][r] = cols(d["x"][r], np.where(k == 2, -1, k))
    o = (e[0] + 1) % N
    d["m"][o] = cols(d["m"][o], np.zeros(MC, int))
    d["x"][e[1]] = 0
    return d
def setup_inputs_near(rng):
    d = numbers_of(rng)
    l = lists_of(rng)
    g = signs(rng)
    down = (P - 1 - np.arange(P)) // 2
    s = np.tile(down, (N, 8, 1))
    r = int(rng.integers(N))
    hit = held(l, r)
    for i in range(8): s[r, i, np.argsort(hit[i], kind="stable")] = down
    u = d["u"].reshape(N, 128, 128, 4)
    u[:, :, ::16] = 0
    for h in range(0, 128, 16):
        u[:, h, h, 0] = g[:, h // 16].astype(BF)
        u[:, h + 8:h + 10, h] = 1
    return {"m": fine(rng, d["m"], rng.integers(0, P // 2, (N, 8, MC))), "x": fine(rng, d["x"], s), "u": u.reshape(N, 128, 512), "v": d["v"], **still(rng), **l}
def setup_inputs_huge(rng):
    d = numbers_of(rng)
    l = lists_of(rng)
    g = signs(rng)
    m = 2.0 ** 30 * (0.6 + 0.4 * rng.random((N, 128, 4 * MC), dtype=np.float32))
    x = 2.0 ** 30 * (0.6 + 0.4 * rng.random((N, 128, 4 * P), dtype=np.float32))
    a = 2.0 ** 30 * (1 - 0.25 * rng.random((N, 128, 8, 4)))
    c = np.stack([rng.permutation(P) % 2 * 2.0 - 1.0 for r in range(N)])
    e = rng.permutation(N)
    c[e[:N // 2]] = 1
    r = e[-1]
    hit = held(l, r)
    k = int(np.argmax(np.sum(hit, axis=1) == A - K))
    c[r] = np.where(hit[k], -g[r, k], g[r, k])
    x[r] = 2.0 ** 30
    a[r] = 2.0 ** 30
    x = x * np.repeat(c, 4, axis=1)[:, None, :]
    u = d["u"].reshape(N, 128, 128, 4)
    a = a * g[:, None, :, None]
    u[:, :, ::16] = a.astype(np.float32).astype(BF)
    return {"m": m.astype(np.float32).astype(BF), "x": x.astype(np.float32).astype(BF), "u": u.reshape(N, 128, 512), "v": d["v"], **still(rng), **l}
def setup_inputs_spread(rng):
    d = setup_inputs(rng)
    d["m"] = np.array(wide(rng, N, 128, 4 * MC, cols=6))
    d["x"] = np.array(wide(rng, N, 128, 4 * P, cols=6))
    r = int(rng.integers(N))
    t, a = gentries(d["tg"][r]), gentries(d["ad"][r])[:, :A]
    g = int(np.argmax([np.sum(~np.isin(a[i], t[i])) for i in range(8)]))
    size = np.full(P, 2.0 ** -24)
    size[rng.choice(np.flatnonzero(~np.isin(t[g], a[g])), 16, replace=False)] = 2.0 ** 20
    v = f(rng, 128, 4 * P).astype(np.float32) * np.repeat(size, 4).astype(np.float32)
    d["x"][r] = mx_ref.flush(v.astype(BF))
    return d
def check_inputs(d):
    b = []
    for k in ("m", "x", "u", "v"):
        a = np.abs(d[k].astype(np.float32))
        if not (np.isfinite(a).all() and ((a == 0) | (a >= 2.0 ** -30) & (a <= 2.0 ** 30)).all()): b.append("a value of " + k)
    t = np.stack([gentries(a) for a in d["tg"]])
    if (t < 0).any() or (t >= MC).any(): b.append("a tag out of range")
    if (np.diff(np.sort(t, axis=-1), axis=-1) == 0).any(): b.append("a tag twice in a cache")
    a = np.stack([gentries(a) for a in d["ad"]]).reshape(N, 8, R, A)
    if (a < 0).any() or (a >= MC).any(): b.append("an address out of range")
    if (np.diff(np.sort(a, axis=-1), axis=-1) == 0).any(): b.append("an address twice in a round of a cache")
    return b
def reference(m, x, u, v, wc, ws, tg, ad):
    qu = [mx_ref.quantize(u[r]) for r in range(N)]
    lay = [pk(wc[r], ws[r]) for r in range(N)]
    now = [x[r] for r in range(N)]
    tags = [np.array(gentries(tg[r])) for r in range(N)]
    acc = [gentries(ad[r]).reshape(8, R, A) for r in range(N)]
    for t in range(R):
        source, target, fetched = [], [], []
        for r in range(N):
            marks = mx_ref.matmul(qu[r], mx_ref.quantize(now[r]))[::16] + np.float32(0.0)
            ask = np.full((8, K), -1)
            src = np.full((8, A), -1)
            dst = np.full((8, A), -1)
            for g in range(8):
                want = acc[r][g, t]
                at = np.full(MC, -1)
                at[tags[r][g]] = np.arange(P)
                place = at[want]
                miss = np.flatnonzero(place < 0)[:K]
                n = len(miss)
                order = np.argsort(marks[g], kind="stable")
                victims = order[~np.isin(order, place)][:n]
                ask[g, :n] = want[miss]
                src[g] = place
                src[g, miss] = P + np.arange(n)
                dst[g] = place
                dst[g, miss] = victims
                tags[r][g, victims] = want[miss]
            source.append(src)
            target.append(dst)
            fetched.append(mx_ref.quantize(gcols(m[(r + 1) % N], ask)))
        came = decode(join(*fetched)).astype(BF)
        for r in range(N):
            z = mx_ref.quantize(gcols(np.concatenate([now[r], cut(came, r, 4 * K)], axis=1), source[r]))
            h = tile([np.maximum(mx_ref.matmul(pick(lay[r], np.arange(128 * b, 128 * b + 128)), z), np.float32(0.0)) * np.float32(0.03125) for b in range(4)])
            e = np.tile(np.arange(P), (8, 1))
            g, j = np.nonzero(target[r] >= 0)
            e[g, target[r][g, j]] = P + j
            now[r] = gcols(np.concatenate([now[r], h], axis=1), e)
    y, ot = np.zeros((N, 128, P), np.float32), np.zeros((N, 8, P), np.float32)
    oc, osc = np.zeros((N, 128, 4 * P), np.uint8), np.zeros((N, 16, P), np.uint8)
    for r in range(N):
        q = mx_ref.quantize(now[r])
        y[r] = mx_ref.matmul(mx_ref.quantize(v[r]), q)
        ot[r] = tags[r]
        oc[r], osc[r] = emit(q)
    return {"y": y, "ot": ot, "oc": oc, "osc": osc}

@@ -1,0 +1,434 @@
+from concourse.mybir import dt, AluOpType, AxisListType, ActivationFunctionType
+
+MC, P, A, K, R = 1024, 512, 256, 48, 3
+BIG = 1.0e29
+LIFT = 2048.0
+UP = 2.0 ** 71
+N1, N2 = P // 4, 4 * K
+W2 = N2 + 16
+S1, S2 = N1 // 16, N2 // 16
+QF = [0, 0, -1]
+QZ = [(2, 4), (2, 4), (0, 1)]
+SA = [6, 6, 0]
+HALF = [32, 32, 128]
+XO, CO, ZO, XW = 4 * A, 4 * (A + P), 4 * (A + P + K), 4 * (A + P + A)
+LAND = [0, K + 128, 2 * K + 128]
+LW = 3 * K + 128
+
+F32, BF, I32, U16, X4, U8 = "float32", "bfloat16", "int32", "uint16", "float8_e4m3fn_x4", "uint8"
+SCRATCH = {}
+
+
+def _sb(name, n, dtype):
+    SCRATCH[name] = ("sbuf", [128, n], dtype)
+
+
+for _n, _w, _d in [
+    ("tgi", 32, I32), ("adi", 48, I32), ("tg16", 32, U16), ("ad16", 48, U16),
+    ("mm", 4 * (MC + K), BF), ("uu", 512, BF), ("vv", 512, BF),
+    ("qu", 128, X4), ("su", 128, U8), ("qu2", 128, X4), ("su2", 128, U8), ("qv", 128, X4), ("sv", 128, U8),
+    ("qw", 512, X4), ("sw", 512, U8), ("qx", 512, X4), ("sx", 512, U8), ("qz", 256, X4), ("sz", 256, U8),
+    ("eb", 2048, BF), ("qe", 512, X4), ("se", 512, U8), ("zt", 512, BF),
+    ("lq", LW, X4), ("ls", LW, U8), ("ft", 512, BF), ("zz", 4 * A, BF), ("hv", 4 * K, BF),
+    ("pidx", 4, I32), ("pint", 4, I32), ("io16", 16, F32), ("io1", MC, F32), ("sc", 16, F32), ("kk", 4, BF),
+    ("pa", 32, F32), ("p16x", 16, F32), ("pcl", 16, F32), ("p4", 24, F32),
+    ("l16", 16, U16), ("l4", 32, U16), ("ul", 8, U16), ("ol", 8, U16),
+    ("c16x", A, F32), ("c4x", P, F32), ("c4m", P, F32), ("cl", N2, F32), ("cr", N2, F32),
+    ("ramp0", N1, BF), ("ramp1", 3 * N1, BF), ("ramp2", S2 * W2, BF), ("missrow", K, F32),
+    ("at", MC + K, F32), ("tgr", P + K, F32), ("tgo", P + K, F32), ("a0", K, F32),
+    ("adr", A + K, F32), ("flg", A, F32), ("cum", A, F32), ("src1", A, F32), ("sA", A, F32), ("sB", A, F32), ("src16", 16, U16), ("src4", 64, U16),
+    ("sE", P, F32), ("e4", 128, U16), ("sJ", K, F32), ("j16", 4, U16), ("sR", K, F32), ("hv4", 12, U16),
+    ("a1", K, F32), ("a16", 4, U16), ("iv0", K, F32), ("inv", K, F32),
+    ("hm", P, F32), ("k0", P, F32), ("k1", P, F32),
+    ("ra1", N1, F32), ("ow1", N1, F32), ("dg", N1, BF), ("dc", N1, BF), ("mx1", S1 * N1, BF), ("rk1", S1, F32), ("rk16", S1, U16),
+    ("fl", N1, BF), ("cm", N1, BF), ("mx3", 3 * N1, BF), ("cm3", 3 * N1, BF), ("id16", 4, U16), ("idr", K, F32), ("c4", 12, U16),
+    ("ra2", W2, F32), ("rb2", W2, F32), ("r2", W2, F32), ("ow2", N2, F32), ("mx2", S2 * W2, BF), ("cm2", S2 * W2, BF),
+    ("rk2f", S2, F32), ("rk2", S2, U16),
+    ("plr", N2, F32), ("vr", N2, F32), ("vr1", K, F32), ("v16", 4, U16), ("v4", 12, U16),
+    ("old", K, F32), ("so", K, F32), ("o16", 4, U16), ("ys", P, F32),
+]:
+    _sb(_n, _w, _d)
+for _t in range(R):
+    _sb("ee%d" % _t, P + A, F32)
+    _sb("req%d" % _t, 12, U16)
+    _sb("rql%d" % _t, 12, U16)
+    _sb("qf%d" % _t, 128, X4)
+    _sb("sf%d" % _t, 128, U8)
+for _t in range(R + 1):
+    _sb("xb%d" % _t, XW, BF)
+SCRATCH["ps"] = ("psum", [128, 4096], F32)
+
+SEMAPHORES = (["cv", "ca", "ct", "cg", "sent"] + ["d%d" % i for i in range(24)]
+              + ["rq%d" % t for t in range(R)] + ["fa%d" % t for t in range(R)])
+
+AL = AluOpType
+AF = ActivationFunctionType
+
+
+def rank_program(g, core, T, topo):
+    rank = T.rank_of(core)
+    if rank is None:
+        return
+    n = len(T.cores)
+    nxt, prv = T.cores[(rank + 1) % n], T.cores[(rank - 1) % n]
+    Q = {"v": g.vector, "a": g.scalar, "t": g.tensor, "g": g, "s": g.sync}
+    OWN = {"v": "cv", "a": "ca", "t": "ct", "g": "cg"}
+    known = {q: {} for q in Q}
+    count, wrote, readers = {}, {}, {}
+    ndma = [0]
+
+    def need(q, tok):
+        sem, val, clock = tok
+        if known[q].get(sem, 0) < val:
+            Q[q].wait_ge(T.sem[sem], val)
+            for s, x in clock.items():
+                if known[q].get(s, 0) < x:
+                    known[q][s] = x
+
+    def before(q, rd, wr):
+        toks = [wrote[k] for k in rd + wr if k in wrote]
+        for k in wr:
+            toks += readers.get(k, [])
+        for tok in sorted(toks, key=lambda z: -z[1]):
+            need(q, tok)
+
+    def after(q, sem, inc, rd, wr):
+        count[sem] = count.get(sem, 0) + inc
+        clock = dict(known[q])
+        clock[sem] = count[sem]
+        tok = (sem, count[sem], clock)
+        for k in rd:
+            readers.setdefault(k, []).append(tok)
+        for k in wr:
+            wrote[k] = tok
+            readers[k] = []
+
+    def op(q, rd, wr, fn):
+        rd, wr = rd.split(), wr.split()
+        before(q, rd, wr)
+        fn().then_inc(T.sem[OWN[q]], 1)
+        after(q, OWN[q], 1, rd, wr)
+
+    def dma(q, rd, wr, out, in_):
+        rd, wr = rd.split(), wr.split()
+        before(q, rd, wr)
+        sem = "d%d" % ndma[0]
+        ndma[0] += 1
+        Q[q].dma_start(out, in_).then_inc(T.sem[sem], 16)
+        after(q, sem, 16, rd, wr)
+
+    def send(dst, rd, out, in_, sem):
+        before("g", rd.split(), [])
+        rid, pid, _ = topo.addr(dst)
+        g.remote_dma(out, in_, T.sem[sem], T.sem.sent, pid, rid, topo.mask(core, dst))
+        count["sent"] = count.get("sent", 0) + len(topo.engines(core, dst))
+
+    def lands(key, sem, src, writes):
+        count[sem] = writes * len(topo.engines(src, core))
+        wrote[key] = (sem, count[sem], {sem: count[sem]})
+
+    V, S = g.vector, g.scalar
+
+    def ts(rd, wr, out, in0, s1, op0, s2=None, op1=None):
+        if op1 is None:
+            op("v", rd, wr, lambda: V.tensor_scalar(out, in0, s1, None, op0))
+        else:
+            op("v", rd, wr, lambda: V.tensor_scalar(out, in0, s1, s2, op0, op1))
+
+    def tt(rd, wr, out, in0, in1, o):
+        op("v", rd, wr, lambda: V.tensor_tensor(out, in0, in1, o))
+
+    def cp(rd, wr, out, in_):
+        op("v", rd, wr, lambda: V.tensor_copy(out, in_))
+
+    def ms(wr, out, c):
+        op("v", "", wr, lambda: V.memset(out, c))
+
+    def scan(rd, wr, out, d0, d1, init, op0, op1):
+        op("v", rd, wr, lambda: V.tensor_tensor_scan(out, d0, d1, init, op0, op1))
+
+    def act(rd, wr, out, in_, func=AF.Copy, **kw):
+        op("a", rd, wr, lambda: S.activation(out, in_, func, **kw))
+
+    def fill(wr, out, w, c):
+        act("zt", wr, out, T.zt[:, 0:w], AF.Identity, bias=c)
+
+    def quant(rd, wr, q, s, in_):
+        op("v", rd, wr, lambda: V.quantize_mx(q, s, in_))
+
+    def mm(rd, bank, w, lq, ls, rq, rs):
+        op("t", rd, "ps%d" % bank, lambda: g.tensor.matmul_mx(T.ps[:, 512 * bank:512 * bank + w], lq, ls, rq, rs, True, True))
+
+    def iota(wr, out, pattern, base):
+        op("g", "", wr, lambda: g.iota(out, pattern, base, 0, allow_small_or_imprecise_dtypes=True))
+
+    def col(i):
+        return T.sc[:, i:i + 1]
+    LANE, LANE1, LANE2, CLS1, T0, TM4, F16, F4 = range(8)
+
+    def lane16(rd, tmp, wr, row, w):
+        scan(rd + " c16x", tmp, T[tmp][:, 0:w], T.c16x[:, 0:w], row, 0.0, AL.mult, AL.max)
+        ts(tmp + " f16", wr, T[wr][:, 0:w // 16], T[tmp][:, 15:w:16], col(F16), AL.mult, -1.0, AL.add)
+
+    def lane4(rd, tmp, wr, row, w):
+        scan(rd + " c4x", tmp, T[tmp][:, 0:w], T.c4x[:, 0:w], row, 0.0, AL.mult, AL.max)
+        ts(tmp + " f4 tm4", wr, T[wr][:, 0:w // 4], T[tmp][:, 3:w:4], col(F4), AL.mult, col(TM4), AL.add)
+
+    for t in range(R):
+        lands("rql%d" % t, "rq%d" % t, prv, 1)
+        lands("land%d" % t, "fa%d" % t, nxt, 2)
+
+    dma("s", "", "tgi", T.tgi[:], T.tg[:])
+    dma("a", "", "adi", T.adi[:], T.ad[:])
+    dma("s", "", "uu", T.uu[:], T.u[:])
+    dma("s", "", "X0", T.xb0[:, XO:CO], T.x[:])
+    dma("s", "", "mm", T.mm[:, 0:4 * MC], T.m[:])
+    dma("s", "", "qw", T.qw[:].bitcast(dt.uint8), T.wc[:])
+    dma("s", "", "sw", T.sw[:], T.ws[:])
+    dma("s", "", "vv", T.vv[:], T.v[:])
+
+    p4x, p4m, p4g = T.p4[:, 0:4], T.p4[:, 8:12], T.p4[:, 16:20]
+    op("g", "", "pidx", lambda: g.iota(T.pidx[:, 0:1], [[0, 1]], 0, 1))
+    iota("io16", T.io16[:], [[1, 16]], 1)
+    iota("ioa", T.io1[:, 0:P], [[1, P]], 1)
+    iota("iob", T.io1[:, P:MC], [[1, MC - P]], P + 1)
+    iota("ramp0", T.ramp0[:], [[0, S1], [1, 16]], 0)
+    ms("zt", T.zt[:], 0.0)
+    fill("at0", T.at[:, 0:P], P, LIFT)
+    fill("at1", T.at[:, P:MC], P, LIFT)
+    fill("at2", T.at[:, MC:MC + K], K, LIFT)
+    ts("pidx", "lanei", T.pint[:, 0:1], T.pidx[:, 0:1], 15, AL.bitwise_and)
+    ts("pidx", "ti", T.pint[:, 1:2], T.pidx[:, 0:1], 3, AL.bitwise_and)
+    ts("pidx", "clsi", T.pint[:, 2:3], T.pidx[:, 0:1], 2, AL.arith_shift_right, 3, AL.bitwise_and)
+    cp("lanei", "lane", col(LANE), T.pint[:, 0:1])
+    ts("lanei", "lane1", col(LANE1), T.pint[:, 0:1], 1.0, AL.add)
+    ts("lanei", "lane2", col(LANE2), T.pint[:, 0:1], 2.0, AL.add)
+    cp("ti", "t0", col(T0), T.pint[:, 1:2])
+    ts("clsi", "cls1", col(CLS1), T.pint[:, 2:3], 1.0, AL.add)
+    ts("io16 lane", "l16", T.l16[:], T.io16[:], 0.0, AL.mult, col(LANE), AL.add)
+    ts("io16 lane1", "pa", T.pa[:, 0:16], T.io16[:], col(LANE1), AL.is_gt)
+    ts("io16 lane2", "pb", T.pa[:, 16:32], T.io16[:], col(LANE2), AL.is_equal, LIFT, AL.mult)
+    ts("io16 cls1", "p4x", p4x, T.io16[:, 0:4], col(CLS1), AL.is_gt, LIFT, AL.mult)
+    ts("io16 t0", "l4a", T.l4[:, 0:16], T.io16[:], 0.0, AL.mult, col(T0), AL.add)
+    ts("io16 t0", "l4b", T.l4[:, 16:32], T.io16[:], 0.0, AL.mult, col(T0), AL.add)
+    tt("pa pb", "p16x", T.p16x[:], T.pa[:, 0:16], T.pa[:, 16:32], AL.max)
+    ts("lanei", "f16", col(F16), T.pint[:, 0:1], 15.0, AL.is_equal, 1.0 - 1.0 / LIFT, AL.mult)
+    ts("p4x", "p4g", p4g, p4x, (1.0 / LIFT - 1.0) / LIFT, AL.mult, 1.0, AL.add)
+    ts("ti", "tm4", col(TM4), T.pint[:, 1:2], -4.0, AL.add)
+    ts("f16", "f16", col(F16), col(F16), 1.0 / LIFT, AL.add)
+    op("v", "p4g", "f4", lambda: V.tensor_reduce(col(F4), p4g, AxisListType.X, AL.mult))
+    ts("pa", "pcl", T.pcl[:], T.pa[:, 0:16], -0.5, AL.add, 2.0 * BIG, AL.mult)
+    ts("io16", "p4m", p4m, T.io16[:, 0:4], 1.5, AL.is_lt, -0.5, AL.add)
+    ts("f4", "f4", col(F4), col(F4), 4.0, AL.mult)
+    ts("io16", "ul", T.ul[:], T.io16[:, 0:8], -1.0, AL.add, 16.0, AL.mult)
+    cp("tgi", "tg16", T.tg16[:], T.tgi[:])
+    cp("adi", "ad16", T.ad16[:], T.adi[:])
+    cp("ioa tg16", "at at0 at1 at2", T.at[:].indirect(T.tg16[:]), T.io1[:, 0:P])
+
+    def addresses(t):
+        act("ioa iob ad16", "adr", T.adr[:, 0:A], T.io1[:].indirect(T.ad16[:, 16 * t:16 * t + 16]))
+
+    def flags(t):
+        act("at ad16", "flg", T.flg[:], T.at[:].indirect(T.ad16[:, 16 * t:16 * t + 16]), AF.Relu, scale=2.0 / LIFT, bias=-1.0)
+
+    def lists(t):
+        e, ek = T["ee%d" % t], "ee%d eeb%d" % (t, t)
+        scan("flg", "cum", T.cum[:], T.flg[:], T.flg[:], float(P), AL.add, AL.max)
+        tt("at ad16 cum", "src1", T.src1[:], T.at[:].indirect(T.ad16[:, 16 * t:16 * t + 16]), T.cum[:], AL.min)
+        lane16("src1", "sA", "src16", T.src1[:], A)
+        cp("ioa src16", ek, e[:].indirect(T.src16[:]), T.io1[:, 0:A])
+        act(ek, "hm", T.hm[:], e[:, 0:P], AF.Identity, scale=-UP, bias=(A + 0.5) * UP)
+        lane16(ek, "sJ", "j16", e[:, P:P + K], K)
+        cp("adr adrb j16", "a1", T.a1[:], T.adr[:].indirect(T.j16[:, 0:3]))
+        lane4("a1", "sR", "req%d" % t, T.a1[:], K)
+        send(nxt, "req%d" % t, T["rql%d" % t][:], T["req%d" % t][:], "rq%d" % t)
+
+    def zeros(t):
+        act("zt", "Za%d" % t, T["xb%d" % t][:, ZO:ZO + 512], T.zt[:])
+        act("zt", "Zb%d" % t, T["xb%d" % t][:, ZO + 512:XW], T.zt[:, 0:XW - ZO - 512])
+
+    def unit(b):
+        op("g", "zt", "eb%d" % b, lambda: g.affine_select(T.eb[:, 512 * b:512 * b + 512], T.zt[:], [[-1, 512]], AL.not_equal, 1.0, b, 4))
+
+    act("p16x l16", "c16x", T.c16x[:], T.p16x[:].indirect(T.l16[:]))
+    act("ioa", "ee0", T.ee0[:, 0:P], T.io1[:, 0:P], AF.Identity, bias=float(A))
+    act("ioa", "eeb0", T.ee0[:, P:P + A], T.io1[:, 0:A], AF.Identity, bias=float(A))
+    act("p4x l4a l4b", "c4x", T.c4x[:], p4x.indirect(T.l4[:]))
+    flags(0)
+    act("ioa", "adrb", T.adr[:, A:A + K], T.io1[:, 0:K], AF.Identity, bias=float(MC))
+    addresses(0)
+    unit(0)
+    unit(1)
+    unit(2)
+    quant("uu", "qu", T.qu[:], T.su[:], T.uu[:])
+    cp("qu ul", "qu2", T.qu2[:].bitcast(dt.uint32), T.qu[:].bitcast(dt.uint32).indirect(T.ul[:]))
+    ts("ul", "ol", T.ol[:], T.ul[:], 15.0, AL.add)
+    ts("ul lane", "kk", T.kk[:, 0:3], T.ul[:, 0:3], col(LANE), AL.add)
+    act("qu ul", "su2", T.su2[:], T.su[:].indirect(T.ul[:]))
+    act("p4m l4a l4b", "c4m", T.c4m[:], p4m.indirect(T.l4[:]), AF.Identity, scale=2.0 * BIG)
+    lists(0)
+    unit(3)
+    act("pcl l16", "cl", T.cl[:], T.pcl[:].indirect(T.l16[:, 0:S2]))
+    act("cl", "cr", T.cr[:], T.cl[:], AF.Identity, scale=-1.0)
+    act("zt", "ftz", T.ft[:, 4 * K:512], T.zt[:, 4 * K:512])
+    act("zt", "mmz", T.mm[:, 4 * MC:4 * (MC + K)], T.zt[:, 0:4 * K])
+    fill("ra2p", T.ra2[:, N2:W2], 16, BIG)
+    fill("rb2p", T.rb2[:, 0:16], 16, BIG)
+    fill("missrow", T.missrow[:], K, LIFT)
+
+    banks = [[5, 6, 7, 0], [1, 2, 3, 4]]
+    for t in range(R):
+        xb, xn, e = T["xb%d" % t], T["xb%d" % (t + 1)], T["ee%d" % t]
+        ek, X, Xn = "ee%d eeb%d" % (t, t), "X%d" % t, "X%d" % (t + 1)
+        H = " ".join("H%d_%d" % (t, b) for b in range(8))
+        came = " ".join("C%d_%d" % (t, b) for b in range(4))
+        camen = " ".join("C%d_%d" % (t + 1, b) for b in range(4))
+        last, half, sa = t == R - 1, HALF[t], SA[t]
+
+        def serve():
+            act("mm mmz rql%d" % t, "ft", T.ft[:, 0:4 * K], T.mm[:].indirect(T["rql%d" % t][:]))
+            qf, sf = T["qf%d" % t], T["sf%d" % t]
+            quant("ft ftz", "qf%d" % t, qf[:], sf[:], T.ft[:])
+            send(prv, "qf%d" % t, T.lq[:, LAND[t]:LAND[t] + K].bitcast(dt.uint8), qf[:, 0:K].bitcast(dt.uint8), "fa%d" % t)
+            send(prv, "qf%d" % t, T.ls[:, LAND[t]:LAND[t] + K], sf[:, 0:K], "fa%d" % t)
+            if t == 0:
+                iota("ramp1", T.ramp1[:], [[0, 3], [1, N1]], 0)
+                iota("ramp2", T.ramp2[:], [[0, S2], [1, W2]], 0)
+            if not last:
+                iota("ee%d" % (t + 1), T["ee%d" % (t + 1)][:, 0:P], [[1, P]], A + 1)
+                iota("eeb%d" % (t + 1), T["ee%d" % (t + 1)][:, P:P + A], [[1, A]], A + 1)
+
+        def layer(i):
+            c = slice(128 * i, 128 * i + 128)
+            quant("zz%d" % i, "qz%d" % i, T.qz[:, c], T.sz[:, c], T.zz[:, 512 * i:512 * i + 512])
+            for b in range(4):
+                mm("qw sw qz%d" % i, banks[i][b], 128, T.qw[:, 128 * b:128 * b + 128], T.sw[:, 128 * b:128 * b + 128], T.qz[:, c], T.sz[:, c])
+
+        def relu(i):
+            for b in range(4):
+                o = 512 * banks[i][b]
+                act("ps%d" % banks[i][b], "H%d_%d" % (t, 4 * i + b), xb[:, 512 * i + b:512 * i + 512:4], T.ps[:, o:o + 128], AF.Relu, scale=0.03125)
+
+        quant(X, "qx", T.qx[:], T.sx[:], xb[:, XO:CO])
+        mm("qu2 su2 qx", 0, P, T.qu2[:], T.su2[:], T.qx[:], T.sx[:])
+        lane4("src1", "sB", "src4", T.src1[:], A)
+        ts("iob cum", "iv0", T.iv0[:], T.io1[:, P:P + K], T.cum[:, A - 1:A], AL.is_gt)
+        lane4(ek, "sR", "hv4", e[:, P:P + K], K)
+        tt("iv0 iob", "inv", T.inv[:], T.iv0[:], T.io1[:, P:P + K], AL.mult)
+        zeros(t)
+        if not last:
+            addresses(t + 1)
+        else:
+            act("tgr tgrb", "tgo", T.tgo[:], T.tgr[:], AF.Identity, bias=-1.0)
+            act("a1", "a0", T.a0[:], T.a1[:], AF.Identity, bias=-1.0)
+        tt("ps0 hm", "k0", T.k0[:], T.ps[:, 0:P], T.hm[:], AL.max)
+        scan("k0 c4m", "k1", T.k1[:], T.c4m[:], T.k0[:], BIG, AL.max, AL.min)
+        tt("k1 cl", "ra1", T.ra1[:], T.k1[:, 3:P:4], T.cl[:, 0:N1], AL.max)
+        if QF[t] < 0:
+            serve()
+        scan("ra1 cr", "ow1", T.ow1[:], T.cr[:, 0:N1], T.ra1[:], BIG, AL.max, AL.min)
+        tt("ow1 ol ra1", "dg", T.dg[:], T.ow1[:].indirect(T.ol[:]), T.ra1[:], AL.is_equal)
+        for s in range(S1):
+            if QF[t] == s:
+                serve()
+            c, o, row = 16 * s, T.ow1[:, 16 * s + 15:16 * s + 16], T.mx1[:, N1 * s:N1 * s + N1]
+            if s:
+                ts("k1 ow1", "mx1a%d" % s, row[:, 0:c], T.k1[:, 3:4 * c:4], o, AL.is_le)
+            ts("k1 ow1", "mx1b%d" % s, row[:, c:N1], T.k1[:, 4 * c + 3:P:4], o, AL.is_lt)
+            if s == 0:
+                scan("dg ramp0", "dc", T.dc[:], T.ramp0[:], T.dg[:], 0.0, AL.min, AL.add)
+            act("dc", "mx1a%d mx1b%d rk1_%d" % (s, s, s), row, row, AF.Identity, scale=float(N1), bias=T.dc[:, c + 15:c + 16], accum_out=T.rk1[:, s:s + 1])
+        if t == 0:
+            quant("zt", "lz", T.lq[:, K:K + 128], T.ls[:, K:K + 128], T.zt[:])
+            quant("eb0 eb1 eb2 eb3", "qe", T.qe[:], T.se[:], T.eb[:])
+        lane4(ek, "sE", "e4", e[:, 0:P], P)
+        if not last:
+            lane16("a1", "so", "a16", T.a1[:], K)
+        else:
+            quant("vv", "qv", T.qv[:], T.sv[:], T.vv[:])
+        ts(" ".join("rk1_%d" % s for s in range(S1)), "rk16", T.rk16[:], T.rk1[:], 1.0 / N1, AL.mult)
+        ts("ioa rk16", "fl", T.fl[:], T.io1[:, 0:P].indirect(T.rk16[:]), K + 1.0, AL.is_le)
+        scan("fl", "cm", T.cm[:], T.fl[:], T.fl[:], 0.0, AL.add, AL.max)
+        for s in range(3):
+            ts("cm kk", "mx3_%d" % s, T.mx3[:, N1 * s:N1 * s + N1], T.cm[:], T.kk[:, s:s + 1], AL.is_le)
+        scan("mx3_0 mx3_1 mx3_2 ramp1", "cm3", T.cm3[:], T.ramp1[:], T.mx3[:], 0.0, AL.min, AL.add)
+        cp("cm3", "id16", T.id16[:, 0:3], T.cm3[:, N1 - 1:3 * N1:N1])
+        cp("ioa id16", "idr", T.idr[:], T.io1[:, 0:P].indirect(T.id16[:, 0:3]))
+        lane4("idr", "sR", "c4", T.idr[:], K)
+        lo = LAND[t] + K - 128 if t else 0
+        for b in range(4):
+            mm("qe lz " + " ".join("land%d" % i for i in range(t + 1)), 1 + b, 128, T.qe[:, 128 * b:128 * b + 128], T.se[:, 128 * b:128 * b + 128],
+               T.lq[:, lo:lo + 128], T.ls[:, lo:lo + 128])
+            o = 512 * (1 + b) + LAND[t] - lo
+            act("ps%d" % (1 + b), "C%d_%d" % (t, b), xb[:, CO + b:ZO:4], T.ps[:, o:o + K])
+        for i in range(2):
+            act("%s %s Za%d Zb%d src4" % (X, came, t, t), "zz%d" % i, T.zz[:, 512 * i:512 * i + 512], xb[:, XO:XW].indirect(T.src4[:, 32 * i:32 * i + 32]))
+        act("ioa c4", "plr", T.plr[:], T.io1[:, 0:P].indirect(T.c4[:]))
+        tt("k0 c4 cl", "ra2", T.ra2[:, 0:N2], T.k0[:].indirect(T.c4[:]), T.cl[:], AL.max)
+        tt("k0 c4 cr", "rb2", T.rb2[:, 16:W2], T.k0[:].indirect(T.c4[:]), T.cr[:], AL.max)
+        scan("ra2 cr", "ow2", T.ow2[:], T.cr[:], T.ra2[:, 0:N2], BIG, AL.max, AL.min)
+        tt("ra2 rb2 ra2p rb2p", "r2", T.r2[:], T.ra2[:], T.rb2[:], AL.min)
+        for s in range(S2):
+            if s == QZ[t][0]:
+                layer(0)
+                if not sa:
+                    relu(0)
+            if s == QZ[t][1]:
+                layer(1)
+            if s == max(QZ[t][1], sa):
+                if sa:
+                    relu(0)
+                relu(1)
+                if t == 0:
+                    act("ioa iob tg16", "tgr", T.tgr[:, 0:P], T.io1[:].indirect(T.tg16[:]))
+                    act("ioa", "tgrb", T.tgr[:, P:P + K], T.io1[:, 0:K], AF.Identity, bias=float(MC))
+                act("%s %s hv4" % (H, X), "hv", T.hv[:], xb[:, 0:CO].indirect(T.hv4[:]))
+                act("%s %s e4" % (H, X), Xn + "a", xn[:, XO:XO + 16 * half], xb[:, 0:CO].indirect(T.e4[:, 0:half]))
+            c, row = 16 * s + 16, T.mx2[:, W2 * s:W2 * s + W2]
+            ts("r2 ow2", "mx2a%d" % s, row[:, 0:c], T.r2[:, 0:c], T.ow2[:, c - 1:c], AL.is_le)
+            ts("r2 ow2", "mx2b%d" % s, row[:, c:W2], T.r2[:, c:W2], T.ow2[:, c - 1:c], AL.is_lt)
+            if s < sa:
+                act("", "mx2a%d mx2b%d rk2_%d" % (s, s, s), row, row, AF.Identity, accum_out=T.rk2f[:, s:s + 1])
+        scan(" ".join("mx2a%d mx2b%d" % (s, s) for s in range(sa, S2)) + " ramp2", "cm2", T.cm2[:, sa * W2:S2 * W2], T.ramp2[:, sa * W2:S2 * W2],
+             T.mx2[:, sa * W2:S2 * W2], 0.0, AL.min, AL.add)
+        if sa:
+            ts(" ".join("rk2_%d" % s for s in range(sa)), "rk2a", T.rk2[:, 0:sa], T.rk2f[:, 0:sa], -1.0, AL.add)
+        ts("cm2", "rk2", T.rk2[:, sa:S2], T.cm2[:, sa * W2 + W2 - 1:S2 * W2:W2], -1.0, AL.add)
+        cp("plr rk2 rk2a", "vr", T.vr[:].indirect(T.rk2[:]), T.plr[:])
+        tt("vr inv", "vr1", T.vr1[:], T.vr[:, 0:K], T.inv[:], AL.max)
+        if not last:
+            lane16("vr1", "sJ", "v16", T.vr1[:], K)
+            cp("tgr tgrb v16", "old", T.old[:], T.tgr[:].indirect(T.v16[:, 0:3]))
+            cp("vr1 a16", "at", T.at[:].indirect(T.a16[:, 0:3]), T.vr1[:])
+            lane16("old", "so", "o16", T.old[:], K)
+            cp("missrow o16", "at", T.at[:].indirect(T.o16[:, 0:3]), T.missrow[:])
+            flags(t + 1)
+            if half < 128:
+                act("%s %s e4" % (H, X), Xn + "b", xn[:, XO + 16 * half:CO], xb[:, 0:CO].indirect(T.e4[:, half:128]))
+            lane4("vr1", "sR", "v4", T.vr1[:], K)
+            cp("a1 v16", "tgr tgrb", T.tgr[:].indirect(T.v16[:, 0:3]), T.a1[:])
+            lists(t + 1)
+        else:
+            lane4("vr1", "sR", "v4", T.vr1[:], K)
+            if half < 128:
+                cp("%s %s e4" % (H, X), Xn + "b", xn[:, XO + 16 * half:CO], xb[:, 0:CO].indirect(T.e4[:, half:128]))
+        cp("hv v4", "%s %sa %sb %s" % (Xn, Xn, Xn, camen), xn[:, XO:ZO].indirect(T.v4[:]), T.hv[:])
+
+    xb, X = T["xb%d" % R], "X%d" % R
+    h = P // 2
+    for i in range(2):
+        quant(X, ("qx " if i == 0 else "") + "qx%d" % i, T.qx[:, h * i:h * i + h], T.sx[:, h * i:h * i + h], xb[:, XO + 4 * h * i:XO + 4 * h * (i + 1)])
+        mm("qv qx%d" % i, 2 + i, h, T.qv[:], T.sv[:], T.qx[:, h * i:h * i + h], T.sx[:, h * i:h * i + h])
+    lane16("vr1", "sJ", "v16", T.vr1[:], K)
+    cp("a0 v16", "tgo", T.tgo[:].indirect(T.v16[:, 0:3]), T.a0[:])
+    dma("s", "qx0 qx1", "oc", T.oc[:], T.qx[:].bitcast(dt.uint8))
+    act("ps2", "ys0", T.ys[:, 0:h], T.ps[:, 1024:1024 + h])
+    dma("a", "ys0", "y0", T.y[:, 0:h], T.ys[:, 0:h])
+    cp("ps3", "ys1", T.ys[:, h:P], T.ps[:, 1536:1536 + h])
+    for k in range(4):
+        dma("s", "qx0 qx1", "osc%d" % k, T.osc[4 * k:4 * k + 4, :], T.sx[32 * k:32 * k + 4, :])
+    dma("s", "tgo", "ot", T.ot[:], T.tgo[0:128:16, 0:P])
+    dma("a", "ys1", "y1", T.y[:, h:P], T.ys[:, h:P])
+    for sem in sorted(count):
+        if known["g"].get(sem, 0) < count[sem]:
+            g.wait_ge(T.sem[sem], count[sem])

@@ -7,10 +7,11 @@ UP = 2.0 ** 71
 N1, N2 = P // 4, 4 * K
 W2 = N2 + 16
 S1, S2 = N1 // 16, N2 // 16
-QF = [0, 0, -1]
-QZ = [(2, 4), (2, 4), (0, 1)]
-SA = [6, 6, 0]
-HALF = [32, 32, 128]
+QF = [0, -1, -1]
+QZ = [(5, 7), (5, 7), (0, 1)]
+S1A = [6, 5, 8]
+SC = [3, 3, 0]
+SA = [3, 3, 0]
 XO, CO, ZO, XW = 4 * A, 4 * (A + P), 4 * (A + P + K), 4 * (A + P + A)
 LAND = [0, K + 128, 2 * K + 128]
 LW = 3 * K + 128
@@ -35,17 +36,18 @@ for _n, _w, _d in [
     ("l16", 16, U16), ("l4", 32, U16), ("ul", 8, U16), ("ol", 8, U16),
     ("c16x", A, F32), ("c4x", P, F32), ("c4m", P, F32), ("cl", N2, F32), ("cr", N2, F32),
     ("ramp0", N1, BF), ("ramp1", 3 * N1, BF), ("ramp2", S2 * W2, BF), ("missrow", K, F32),
-    ("at", MC + K, F32), ("tgr", P + K, F32), ("tgo", P + K, F32), ("a0", K, F32),
-    ("adr", A + K, F32), ("flg", A, F32), ("cum", A, F32), ("src1", A, F32), ("sA", A, F32), ("sB", A, F32), ("src16", 16, U16), ("src4", 64, U16),
+    ("at", MC + K, F32), ("tgr", P + K, F32), ("tgo", P + K, F32), ("jk", K, F32),
+    ("adr", A + K, F32), ("flg", A, F32), ("cum", A, F32), ("src1", A, F32), ("sA", A, F32), ("src16", 16, U16), ("src4", 64, U16),
     ("sE", P, F32), ("e4", 128, U16), ("sJ", K, F32), ("j16", 4, U16), ("sR", K, F32), ("hv4", 12, U16),
     ("a1", K, F32), ("a16", 4, U16), ("iv0", K, F32), ("inv", K, F32),
     ("hm", P, F32), ("k0", P, F32), ("k1", P, F32),
-    ("ra1", N1, F32), ("ow1", N1, F32), ("dg", N1, BF), ("dc", N1, BF), ("mx1", S1 * N1, BF), ("rk1", S1, F32), ("rk16", S1, U16),
+    ("ra1", N1, F32), ("ow1", N1, F32), ("dg", N1, BF), ("dc", N1, BF), ("mx1", S1 * N1, BF), ("cm1", S1 * N1, BF),
+    ("rk1", S1, F32), ("rk16", S1, U16),
     ("fl", N1, BF), ("cm", N1, BF), ("mx3", 3 * N1, BF), ("cm3", 3 * N1, BF), ("id16", 4, U16), ("idr", K, F32), ("c4", 12, U16),
     ("ra2", W2, F32), ("rb2", W2, F32), ("r2", W2, F32), ("ow2", N2, F32), ("mx2", S2 * W2, BF), ("cm2", S2 * W2, BF),
-    ("rk2f", S2, F32), ("rk2", S2, U16),
+    ("rk2f", 3 * S2, F32), ("rk2", S2, U16),
     ("plr", N2, F32), ("vr", N2, F32), ("vr1", K, F32), ("v16", 4, U16), ("v4", 12, U16),
-    ("old", K, F32), ("so", K, F32), ("o16", 4, U16), ("ys", P, F32),
+    ("old", K, F32), ("so", K, F32), ("o16", 4, U16),
 ]:
     _sb(_n, _w, _d)
 for _t in range(R):
@@ -205,6 +207,8 @@ def rank_program(g, core, T, topo):
     ts("lanei", "lane2", col(LANE2), T.pint[:, 0:1], 2.0, AL.add)
     cp("ti", "t0", col(T0), T.pint[:, 1:2])
     ts("clsi", "cls1", col(CLS1), T.pint[:, 2:3], 1.0, AL.add)
+    ts("lanei", "f16", col(F16), T.pint[:, 0:1], 15.0, AL.is_equal, 1.0 - 1.0 / LIFT, AL.mult)
+    ts("ti", "tm4", col(TM4), T.pint[:, 1:2], -4.0, AL.add)
     ts("io16 lane", "l16", T.l16[:], T.io16[:], 0.0, AL.mult, col(LANE), AL.add)
     ts("io16 lane1", "pa", T.pa[:, 0:16], T.io16[:], col(LANE1), AL.is_gt)
     ts("io16 lane2", "pb", T.pa[:, 16:32], T.io16[:], col(LANE2), AL.is_equal, LIFT, AL.mult)
@@ -212,18 +216,12 @@ def rank_program(g, core, T, topo):
     ts("io16 t0", "l4a", T.l4[:, 0:16], T.io16[:], 0.0, AL.mult, col(T0), AL.add)
     ts("io16 t0", "l4b", T.l4[:, 16:32], T.io16[:], 0.0, AL.mult, col(T0), AL.add)
     tt("pa pb", "p16x", T.p16x[:], T.pa[:, 0:16], T.pa[:, 16:32], AL.max)
-    ts("lanei", "f16", col(F16), T.pint[:, 0:1], 15.0, AL.is_equal, 1.0 - 1.0 / LIFT, AL.mult)
     ts("p4x", "p4g", p4g, p4x, (1.0 / LIFT - 1.0) / LIFT, AL.mult, 1.0, AL.add)
-    ts("ti", "tm4", col(TM4), T.pint[:, 1:2], -4.0, AL.add)
     ts("f16", "f16", col(F16), col(F16), 1.0 / LIFT, AL.add)
-    op("v", "p4g", "f4", lambda: V.tensor_reduce(col(F4), p4g, AxisListType.X, AL.mult))
-    ts("pa", "pcl", T.pcl[:], T.pa[:, 0:16], -0.5, AL.add, 2.0 * BIG, AL.mult)
-    ts("io16", "p4m", p4m, T.io16[:, 0:4], 1.5, AL.is_lt, -0.5, AL.add)
-    ts("f4", "f4", col(F4), col(F4), 4.0, AL.mult)
-    ts("io16", "ul", T.ul[:], T.io16[:, 0:8], -1.0, AL.add, 16.0, AL.mult)
     cp("tgi", "tg16", T.tg16[:], T.tgi[:])
-    cp("adi", "ad16", T.ad16[:], T.adi[:])
+    op("v", "p4g", "f4", lambda: V.tensor_reduce(col(F4), p4g, AxisListType.X, AL.mult))
     cp("ioa tg16", "at at0 at1 at2", T.at[:].indirect(T.tg16[:]), T.io1[:, 0:P])
+    cp("adi", "ad16", T.ad16[:], T.adi[:])
 
     def addresses(t):
         act("ioa iob ad16", "adr", T.adr[:, 0:A], T.io1[:].indirect(T.ad16[:, 16 * t:16 * t + 16]))
@@ -260,14 +258,17 @@ def rank_program(g, core, T, topo):
     unit(0)
     unit(1)
     unit(2)
+    ts("io16", "ul", T.ul[:], T.io16[:, 0:8], -1.0, AL.add, 16.0, AL.mult)
     quant("uu", "qu", T.qu[:], T.su[:], T.uu[:])
+    ts("io16", "p4m", p4m, T.io16[:, 0:4], 1.5, AL.is_lt, -0.5, AL.add)
     cp("qu ul", "qu2", T.qu2[:].bitcast(dt.uint32), T.qu[:].bitcast(dt.uint32).indirect(T.ul[:]))
-    ts("ul", "ol", T.ol[:], T.ul[:], 15.0, AL.add)
-    ts("ul lane", "kk", T.kk[:, 0:3], T.ul[:, 0:3], col(LANE), AL.add)
+    ts("pa", "pcl", T.pcl[:], T.pa[:, 0:16], -0.5, AL.add, 2.0 * BIG, AL.mult)
+    ts("f4", "f4", col(F4), col(F4), 4.0, AL.mult)
     act("qu ul", "su2", T.su2[:], T.su[:].indirect(T.ul[:]))
     act("p4m l4a l4b", "c4m", T.c4m[:], p4m.indirect(T.l4[:]), AF.Identity, scale=2.0 * BIG)
     lists(0)
     unit(3)
+    iota("ramp1", T.ramp1[:], [[0, 3], [1, N1]], 0)
     act("pcl l16", "cl", T.cl[:], T.pcl[:].indirect(T.l16[:, 0:S2]))
     act("cl", "cr", T.cr[:], T.cl[:], AF.Identity, scale=-1.0)
     act("zt", "ftz", T.ft[:, 4 * K:512], T.zt[:, 4 * K:512])
@@ -282,8 +283,7 @@ def rank_program(g, core, T, topo):
         ek, X, Xn = "ee%d eeb%d" % (t, t), "X%d" % t, "X%d" % (t + 1)
         H = " ".join("H%d_%d" % (t, b) for b in range(8))
         came = " ".join("C%d_%d" % (t, b) for b in range(4))
-        camen = " ".join("C%d_%d" % (t + 1, b) for b in range(4))
-        last, half, sa = t == R - 1, HALF[t], SA[t]
+        last, s1a, sc, sa = t == R - 1, S1A[t], SC[t], SC[t] + SA[t]
 
         def serve():
             act("mm mmz rql%d" % t, "ft", T.ft[:, 0:4 * K], T.mm[:].indirect(T["rql%d" % t][:]))
@@ -292,7 +292,6 @@ def rank_program(g, core, T, topo):
             send(prv, "qf%d" % t, T.lq[:, LAND[t]:LAND[t] + K].bitcast(dt.uint8), qf[:, 0:K].bitcast(dt.uint8), "fa%d" % t)
             send(prv, "qf%d" % t, T.ls[:, LAND[t]:LAND[t] + K], sf[:, 0:K], "fa%d" % t)
             if t == 0:
-                iota("ramp1", T.ramp1[:], [[0, 3], [1, N1]], 0)
                 iota("ramp2", T.ramp2[:], [[0, S2], [1, W2]], 0)
             if not last:
                 iota("ee%d" % (t + 1), T["ee%d" % (t + 1)][:, 0:P], [[1, P]], A + 1)
@@ -311,43 +310,53 @@ def rank_program(g, core, T, topo):
 
         quant(X, "qx", T.qx[:], T.sx[:], xb[:, XO:CO])
         mm("qu2 su2 qx", 0, P, T.qu2[:], T.su2[:], T.qx[:], T.sx[:])
-        lane4("src1", "sB", "src4", T.src1[:], A)
         ts("iob cum", "iv0", T.iv0[:], T.io1[:, P:P + K], T.cum[:, A - 1:A], AL.is_gt)
-        lane4(ek, "sR", "hv4", e[:, P:P + K], K)
+        lane4("src1", "sA", "src4", T.src1[:], A)
         tt("iv0 iob", "inv", T.inv[:], T.iv0[:], T.io1[:, P:P + K], AL.mult)
-        zeros(t)
+        if last:
+            lane4(ek, "sR", "hv4", e[:, P:P + K], K)
+        else:
+            lane16("a1", "so", "a16", T.a1[:], K)
+            act(ek, "jk", T.jk[:], e[:, P:P + K])
+        if t == 0:
+            ts("ul", "ol", T.ol[:], T.ul[:], 15.0, AL.add)
         if not last:
             addresses(t + 1)
-        else:
-            act("tgr tgrb", "tgo", T.tgo[:], T.tgr[:], AF.Identity, bias=-1.0)
-            act("a1", "a0", T.a0[:], T.a1[:], AF.Identity, bias=-1.0)
         tt("ps0 hm", "k0", T.k0[:], T.ps[:, 0:P], T.hm[:], AL.max)
         scan("k0 c4m", "k1", T.k1[:], T.c4m[:], T.k0[:], BIG, AL.max, AL.min)
         tt("k1 cl", "ra1", T.ra1[:], T.k1[:, 3:P:4], T.cl[:, 0:N1], AL.max)
+        if t == 0:
+            quant("zt", "lz", T.lq[:, K:K + 128], T.ls[:, K:K + 128], T.zt[:])
+        scan("ra1 cr", "ow1", T.ow1[:], T.cr[:, 0:N1], T.ra1[:], BIG, AL.max, AL.min)
+        if t == 0:
+            quant("eb0 eb1 eb2 eb3", "qe", T.qe[:], T.se[:], T.eb[:])
+        zeros(t)
         if QF[t] < 0:
             serve()
-        scan("ra1 cr", "ow1", T.ow1[:], T.cr[:, 0:N1], T.ra1[:], BIG, AL.max, AL.min)
         tt("ow1 ol ra1", "dg", T.dg[:], T.ow1[:].indirect(T.ol[:]), T.ra1[:], AL.is_equal)
         for s in range(S1):
-            if QF[t] == s:
-                serve()
             c, o, row = 16 * s, T.ow1[:, 16 * s + 15:16 * s + 16], T.mx1[:, N1 * s:N1 * s + N1]
             if s:
                 ts("k1 ow1", "mx1a%d" % s, row[:, 0:c], T.k1[:, 3:4 * c:4], o, AL.is_le)
             ts("k1 ow1", "mx1b%d" % s, row[:, c:N1], T.k1[:, 4 * c + 3:P:4], o, AL.is_lt)
             if s == 0:
                 scan("dg ramp0", "dc", T.dc[:], T.ramp0[:], T.dg[:], 0.0, AL.min, AL.add)
-            act("dc", "mx1a%d mx1b%d rk1_%d" % (s, s, s), row, row, AF.Identity, scale=float(N1), bias=T.dc[:, c + 15:c + 16], accum_out=T.rk1[:, s:s + 1])
+            if QF[t] == s:
+                serve()
+            if s < s1a:
+                act("dc", "mx1a%d mx1b%d rk1_%d" % (s, s, s), row, row, AF.Identity, scale=float(N1), bias=T.dc[:, c + 15:c + 16], accum_out=T.rk1[:, s:s + 1])
+        for s in range(s1a, S1):
+            row = T.mx1[:, N1 * s:N1 * s + N1]
+            scan("dc mx1a%d mx1b%d" % (s, s), "cm1_%d" % s, T.cm1[:, N1 * s:N1 * s + N1], row, row, T.dc[:, 16 * s + 15:16 * s + 16], AL.add, AL.max)
         if t == 0:
-            quant("zt", "lz", T.lq[:, K:K + 128], T.ls[:, K:K + 128], T.zt[:])
-            quant("eb0 eb1 eb2 eb3", "qe", T.qe[:], T.se[:], T.eb[:])
-        lane4(ek, "sE", "e4", e[:, 0:P], P)
-        if not last:
-            lane16("a1", "so", "a16", T.a1[:], K)
-        else:
+            ts("ul lane", "kk", T.kk[:, 0:3], T.ul[:, 0:3], col(LANE), AL.add)
+        if last:
+            lane4(ek, "sE", "e4", e[:, 0:P], P)
             quant("vv", "qv", T.qv[:], T.sv[:], T.vv[:])
-        ts(" ".join("rk1_%d" % s for s in range(S1)), "rk16", T.rk16[:], T.rk1[:], 1.0 / N1, AL.mult)
-        ts("ioa rk16", "fl", T.fl[:], T.io1[:, 0:P].indirect(T.rk16[:]), K + 1.0, AL.is_le)
+        ts(" ".join("rk1_%d" % s for s in range(s1a)), "rk16", T.rk16[:, 0:s1a], T.rk1[:, 0:s1a], 1.0 / N1, AL.mult)
+        if s1a < S1:
+            cp(" ".join("cm1_%d" % s for s in range(s1a, S1)), "rk16b", T.rk16[:, s1a:S1], T.cm1[:, N1 * s1a + N1 - 1:N1 * S1:N1])
+        ts("ioa rk16 rk16b", "fl", T.fl[:], T.io1[:, 0:P].indirect(T.rk16[:]), K + 1.0, AL.is_le)
         scan("fl", "cm", T.cm[:], T.fl[:], T.fl[:], 0.0, AL.add, AL.max)
         for s in range(3):
             ts("cm kk", "mx3_%d" % s, T.mx3[:, N1 * s:N1 * s + N1], T.cm[:], T.kk[:, s:s + 1], AL.is_le)
@@ -363,56 +372,72 @@ def rank_program(g, core, T, topo):
             act("ps%d" % (1 + b), "C%d_%d" % (t, b), xb[:, CO + b:ZO:4], T.ps[:, o:o + K])
         for i in range(2):
             act("%s %s Za%d Zb%d src4" % (X, came, t, t), "zz%d" % i, T.zz[:, 512 * i:512 * i + 512], xb[:, XO:XW].indirect(T.src4[:, 32 * i:32 * i + 32]))
-        act("ioa c4", "plr", T.plr[:], T.io1[:, 0:P].indirect(T.c4[:]))
+        if last:
+            act("ioa c4", "plr", T.plr[:], T.io1[:, 0:P].indirect(T.c4[:]))
         tt("k0 c4 cl", "ra2", T.ra2[:, 0:N2], T.k0[:].indirect(T.c4[:]), T.cl[:], AL.max)
         tt("k0 c4 cr", "rb2", T.rb2[:, 16:W2], T.k0[:].indirect(T.c4[:]), T.cr[:], AL.max)
         scan("ra2 cr", "ow2", T.ow2[:], T.cr[:], T.ra2[:, 0:N2], BIG, AL.max, AL.min)
         tt("ra2 rb2 ra2p rb2p", "r2", T.r2[:], T.ra2[:], T.rb2[:], AL.min)
-        for s in range(S2):
+        for s in range(sc):
+            c, row, ks = 16 * s + 16, T.mx2[:, W2 * s:W2 * s + W2], "mx2a%d mx2b%d" % (s, s)
+            act("r2 ow2", ks, row, T.r2[:], AF.Sign, scale=-1.0, bias=T.ow2[:, c - 1:c])
+        for s in range(sc):
+            c, row = 16 * s + 16, T.mx2[:, W2 * s:W2 * s + W2]
+            act("", "mx2a%d rkl%d" % (s, s), row[:, 0:c], row[:, 0:c], AF.Sign, bias=0.5, accum_out=T.rk2f[:, S2 + s:S2 + s + 1])
+            act("", "mx2b%d rkr%d" % (s, s), row[:, c:W2], row[:, c:W2], AF.Sign, bias=-0.5, accum_out=T.rk2f[:, 2 * S2 + s:2 * S2 + s + 1])
+        for s in range(sc, S2):
             if s == QZ[t][0]:
                 layer(0)
-                if not sa:
+                if last:
                     relu(0)
             if s == QZ[t][1]:
                 layer(1)
-            if s == max(QZ[t][1], sa):
-                if sa:
-                    relu(0)
-                relu(1)
-                if t == 0:
-                    act("ioa iob tg16", "tgr", T.tgr[:, 0:P], T.io1[:].indirect(T.tg16[:]))
-                    act("ioa", "tgrb", T.tgr[:, P:P + K], T.io1[:, 0:K], AF.Identity, bias=float(MC))
-                act("%s %s hv4" % (H, X), "hv", T.hv[:], xb[:, 0:CO].indirect(T.hv4[:]))
-                act("%s %s e4" % (H, X), Xn + "a", xn[:, XO:XO + 16 * half], xb[:, 0:CO].indirect(T.e4[:, 0:half]))
+                if last:
+                    relu(1)
+                    act("%s %s hv4" % (H, X), "hv", T.hv[:], xb[:, 0:CO].indirect(T.hv4[:]))
+                    act("%s %s e4" % (H, X), Xn, xn[:, XO:CO], xb[:, 0:CO].indirect(T.e4[:]))
+                    act("tgr tgrb", "tgo", T.tgo[:], T.tgr[:], AF.Identity, bias=-1.0)
+                    act("a1", "old", T.old[:], T.a1[:], AF.Identity, bias=-1.0)
             c, row = 16 * s + 16, T.mx2[:, W2 * s:W2 * s + W2]
             ts("r2 ow2", "mx2a%d" % s, row[:, 0:c], T.r2[:, 0:c], T.ow2[:, c - 1:c], AL.is_le)
             ts("r2 ow2", "mx2b%d" % s, row[:, c:W2], T.r2[:, c:W2], T.ow2[:, c - 1:c], AL.is_lt)
             if s < sa:
                 act("", "mx2a%d mx2b%d rk2_%d" % (s, s, s), row, row, AF.Identity, accum_out=T.rk2f[:, s:s + 1])
+        if not last:
+            act("ioa c4", "plr", T.plr[:], T.io1[:, 0:P].indirect(T.c4[:]))
+            if t == 0:
+                act("ioa iob tg16", "tgr", T.tgr[:, 0:P], T.io1[:].indirect(T.tg16[:]))
+                act("ioa", "tgrb", T.tgr[:, P:P + K], T.io1[:, 0:K], AF.Identity, bias=float(MC))
+            relu(0)
+            relu(1)
+        if sc:
+            tt(" ".join("rkl%d rkr%d" % (s, s) for s in range(sc)), "rkc", T.rk2f[:, 0:sc], T.rk2f[:, S2:S2 + sc], T.rk2f[:, 2 * S2:2 * S2 + sc], AL.add)
         scan(" ".join("mx2a%d mx2b%d" % (s, s) for s in range(sa, S2)) + " ramp2", "cm2", T.cm2[:, sa * W2:S2 * W2], T.ramp2[:, sa * W2:S2 * W2],
              T.mx2[:, sa * W2:S2 * W2], 0.0, AL.min, AL.add)
-        if sa:
-            ts(" ".join("rk2_%d" % s for s in range(sa)), "rk2a", T.rk2[:, 0:sa], T.rk2f[:, 0:sa], -1.0, AL.add)
+        if sc:
+            ts("rkc", "rk2c", T.rk2[:, 0:sc], T.rk2f[:, 0:sc], 0.5, AL.mult, W2 / 2 - 1.0, AL.add)
+        if sa > sc:
+            ts(" ".join("rk2_%d" % s for s in range(sc, sa)), "rk2a", T.rk2[:, sc:sa], T.rk2f[:, sc:sa], -1.0, AL.add)
         ts("cm2", "rk2", T.rk2[:, sa:S2], T.cm2[:, sa * W2 + W2 - 1:S2 * W2:W2], -1.0, AL.add)
-        cp("plr rk2 rk2a", "vr", T.vr[:].indirect(T.rk2[:]), T.plr[:])
+        cp("plr rk2 rk2a rk2c", "vr", T.vr[:].indirect(T.rk2[:]), T.plr[:])
         tt("vr inv", "vr1", T.vr1[:], T.vr[:, 0:K], T.inv[:], AL.max)
         if not last:
             lane16("vr1", "sJ", "v16", T.vr1[:], K)
             cp("tgr tgrb v16", "old", T.old[:], T.tgr[:].indirect(T.v16[:, 0:3]))
             cp("vr1 a16", "at", T.at[:].indirect(T.a16[:, 0:3]), T.vr1[:])
-            lane16("old", "so", "o16", T.old[:], K)
+            scan("old c16x", "so", T.so[:], T.c16x[:, 0:K], T.old[:], 0.0, AL.mult, AL.max)
+            cp("jk v16", ek, e[:].indirect(T.v16[:, 0:3]), T.jk[:])
+            ts("so f16", "o16", T.o16[:, 0:3], T.so[:, 15:K:16], col(F16), AL.mult, -1.0, AL.add)
+            scan(ek + " c4x", "sE", T.sE[:], T.c4x[:], e[:, 0:P], 0.0, AL.mult, AL.max)
             cp("missrow o16", "at", T.at[:].indirect(T.o16[:, 0:3]), T.missrow[:])
             flags(t + 1)
-            if half < 128:
-                act("%s %s e4" % (H, X), Xn + "b", xn[:, XO + 16 * half:CO], xb[:, 0:CO].indirect(T.e4[:, half:128]))
-            lane4("vr1", "sR", "v4", T.vr1[:], K)
+            ts("sE f4 tm4", "e4", T.e4[:], T.sE[:, 3:P:4], col(F4), AL.mult, col(TM4), AL.add)
+            act("%s %s e4" % (H, X), Xn, xn[:, XO:CO], xb[:, 0:CO].indirect(T.e4[:]))
             cp("a1 v16", "tgr tgrb", T.tgr[:].indirect(T.v16[:, 0:3]), T.a1[:])
             lists(t + 1)
         else:
             lane4("vr1", "sR", "v4", T.vr1[:], K)
-            if half < 128:
-                cp("%s %s e4" % (H, X), Xn + "b", xn[:, XO + 16 * half:CO], xb[:, 0:CO].indirect(T.e4[:, half:128]))
-        cp("hv v4", "%s %sa %sb %s" % (Xn, Xn, Xn, camen), xn[:, XO:ZO].indirect(T.v4[:]), T.hv[:])
+            cp("hv v4", Xn, xn[:, XO:ZO].indirect(T.v4[:]), T.hv[:])
 
     xb, X = T["xb%d" % R], "X%d" % R
     h = P // 2
@@ -420,15 +445,15 @@ def rank_program(g, core, T, topo):
         quant(X, ("qx " if i == 0 else "") + "qx%d" % i, T.qx[:, h * i:h * i + h], T.sx[:, h * i:h * i + h], xb[:, XO + 4 * h * i:XO + 4 * h * (i + 1)])
         mm("qv qx%d" % i, 2 + i, h, T.qv[:], T.sv[:], T.qx[:, h * i:h * i + h], T.sx[:, h * i:h * i + h])
     lane16("vr1", "sJ", "v16", T.vr1[:], K)
-    cp("a0 v16", "tgo", T.tgo[:].indirect(T.v16[:, 0:3]), T.a0[:])
+    cp("old v16", "tgo", T.tgo[:].indirect(T.v16[:, 0:3]), T.old[:])
     dma("s", "qx0 qx1", "oc", T.oc[:], T.qx[:].bitcast(dt.uint8))
-    act("ps2", "ys0", T.ys[:, 0:h], T.ps[:, 1024:1024 + h])
-    dma("a", "ys0", "y0", T.y[:, 0:h], T.ys[:, 0:h])
-    cp("ps3", "ys1", T.ys[:, h:P], T.ps[:, 1536:1536 + h])
+    act("ps2", "hm ys0", T.hm[:, 0:h], T.ps[:, 1024:1024 + h])
+    dma("a", "ys0", "y0", T.y[:, 0:h], T.hm[:, 0:h])
+    cp("ps3", "k1 ys1", T.k1[:, 0:h], T.ps[:, 1536:1536 + h])
     for k in range(4):
         dma("s", "qx0 qx1", "osc%d" % k, T.osc[4 * k:4 * k + 4, :], T.sx[32 * k:32 * k + 4, :])
     dma("s", "tgo", "ot", T.ot[:], T.tgo[0:128:16, 0:P])
-    dma("a", "ys1", "y1", T.y[:, h:P], T.ys[:, h:P])
+    dma("a", "ys1", "y1", T.y[:, h:P], T.k1[:, 0:h])
     for sem in sorted(count):
         if known["g"].get(sem, 0) < count[sem]:
             g.wait_ge(T.sem[sem], count[sem])

@@ -1,3 +1,4 @@
+import numpy as np
 from concourse.mybir import dt, AluOpType, AxisListType, ActivationFunctionType
 
 MC, P, A, K, R = 1024, 512, 256, 48, 3
@@ -5,18 +6,18 @@ BIG = 1.0e29
 LIFT = 2048.0
 UP = 2.0 ** 71
 N1, N2 = P // 4, 4 * K
-W2 = N2 + 16
 S1, S2 = N1 // 16, N2 // 16
-QF = [0, -1, -1]
-QZ = [(5, 7), (5, 7), (0, 1)]
-S1A = [6, 5, 8]
-SC = [3, 3, 0]
-SA = [3, 3, 0]
-XO, CO, ZO, XW = 4 * A, 4 * (A + P), 4 * (A + P + K), 4 * (A + P + A)
+AX = A + K
+XO, HO, XW = 64, 64 + P, 64 + P + AX
+DO, TW = HO + K, HO + K + MC
 LAND = [0, K + 128, 2 * K + 128]
 LW = 3 * K + 128
+TUNE = dict(sg1=[1, 1, 1], sm1=[3, 3, 3], sg2=[4, 4, 0], sm2=[0, 0, 0], jv=[1, 1, 1], a1v=[0, 0, 0], k2v=[0, 0, 0], xv=[1, 1, 0], zv=[0, 0, 0],
+            late=[1, 1, 0], flv=[0, 0, 0], idv=[0, 0, 0], m3v=[0, 0, 0], oldv=0, tvf=[1, 1, 1], xp=4,
+            seed=0, tries=2000, noise=2000.0, slack=300.0, wake=150.0, far=1800.0, f=1.1)
 
 F32, BF, I32, U16, X4, U8 = "float32", "bfloat16", "int32", "uint16", "float8_e4m3fn_x4", "uint8"
+SHORT = "neg kh z48 a0 sgn inv ve olv old jr a1 idr sa so sV sW sR sH sC".split()
 SCRATCH = {}
 
 
@@ -31,33 +32,32 @@ for _n, _w, _d in [
     ("qw", 512, X4), ("sw", 512, U8), ("qx", 512, X4), ("sx", 512, U8), ("qz", 256, X4), ("sz", 256, U8),
     ("eb", 2048, BF), ("qe", 512, X4), ("se", 512, U8), ("zt", 512, BF),
     ("lq", LW, X4), ("ls", LW, U8), ("ft", 512, BF), ("zz", 4 * A, BF), ("hv", 4 * K, BF),
-    ("pidx", 4, I32), ("pint", 4, I32), ("io16", 16, F32), ("io1", MC, F32), ("sc", 16, F32), ("kk", 4, BF),
+    ("pint", 8, I32), ("io16", 16, F32), ("io1", MC, F32), ("sc", 16, F32), ("kk", 8, F32),
     ("pa", 32, F32), ("p16x", 16, F32), ("pcl", 16, F32), ("p4", 24, F32),
-    ("l16", 16, U16), ("l4", 32, U16), ("ul", 8, U16), ("ol", 8, U16),
-    ("c16x", A, F32), ("c4x", P, F32), ("c4m", P, F32), ("cl", N2, F32), ("cr", N2, F32),
-    ("ramp0", N1, BF), ("ramp1", 3 * N1, BF), ("ramp2", S2 * W2, BF), ("missrow", K, F32),
-    ("at", MC + K, F32), ("tgr", P + K, F32), ("tgo", P + K, F32), ("jk", K, F32),
-    ("adr", A + K, F32), ("flg", A, F32), ("cum", A, F32), ("src1", A, F32), ("sA", A, F32), ("src16", 16, U16), ("src4", 64, U16),
-    ("sE", P, F32), ("e4", 128, U16), ("sJ", K, F32), ("j16", 4, U16), ("sR", K, F32), ("hv4", 12, U16),
-    ("a1", K, F32), ("a16", 4, U16), ("iv0", K, F32), ("inv", K, F32),
+    ("l16", 16, U16), ("l4", 16, U16), ("ul", 12, U16), ("ol", 12, U16),
+    ("c16x", A, F32), ("c4x", A, F32), ("c4m", A, F32), ("cl", N2, F32), ("cr", N2, F32),
+    ("ramp0", N2, BF), ("ramp1", 3 * N1, BF), ("cap", AX, BF), ("ones", P, BF), ("stp", 144, BF),
+    ("rows", len(SHORT) * K, F32), ("at", MC + K, F32), ("tgr", DO, F32), ("tb", TW, F32),
+    ("adr", R * AX, F32), ("pre", A, F32), ("sP", A, F32), ("pre16", R * 16, U16),
+    ("flg", AX, BF), ("cum", AX, BF), ("jx", 3 * AX, BF), ("jc", 3 * AX // 2, F32), ("jf", 8, F32), ("j16", 4 * R, U16),
+    ("src1", AX, F32), ("sA", A, F32), ("src4", 64, U16), ("sE", P, F32), ("e4", 128, U16), ("hv4", 12, U16), ("a16", 4, U16),
     ("hm", P, F32), ("k0", P, F32), ("k1", P, F32),
-    ("ra1", N1, F32), ("ow1", N1, F32), ("dg", N1, BF), ("dc", N1, BF), ("mx1", S1 * N1, BF), ("cm1", S1 * N1, BF),
-    ("rk1", S1, F32), ("rk16", S1, U16),
-    ("fl", N1, BF), ("cm", N1, BF), ("mx3", 3 * N1, BF), ("cm3", 3 * N1, BF), ("id16", 4, U16), ("idr", K, F32), ("c4", 12, U16),
-    ("ra2", W2, F32), ("rb2", W2, F32), ("r2", W2, F32), ("ow2", N2, F32), ("mx2", S2 * W2, BF), ("cm2", S2 * W2, BF),
-    ("rk2f", 3 * S2, F32), ("rk2", S2, U16),
-    ("plr", N2, F32), ("vr", N2, F32), ("vr1", K, F32), ("v16", 4, U16), ("v4", 12, U16),
-    ("old", K, F32), ("so", K, F32), ("o16", 4, U16),
+    ("ra1", N1, F32), ("ow1", N1, F32), ("dg1", N1, BF), ("dc1", N1, BF), ("mx1", S1 * N1, BF), ("cm1", S1 * 64, BF),
+    ("rf1", 3 * S1, F32), ("rk1", S1, U16),
+    ("fl", N1, BF), ("cm", N1, BF), ("mx3", 3 * N1, BF), ("cm3", 3 * N1, BF), ("id16", 4, U16), ("c4", 12, U16),
+    ("k2", N2, F32), ("ra2", N2, F32), ("ow2", N2, F32), ("dg2", N2, BF), ("dc2", N2, BF), ("mx2", S2 * N2, BF), ("cm2", S2 * 96, BF),
+    ("rf2", 3 * S2, F32), ("rk2", S2, U16),
+    ("plr", N2, F32), ("vr", N2, F32), ("v16", 4, U16), ("v4", 12, U16), ("o16", 4, U16),
 ]:
     _sb(_n, _w, _d)
 for _t in range(R):
-    _sb("ee%d" % _t, P + A, F32)
+    _sb("ee%d" % _t, TW, F32)
     _sb("req%d" % _t, 12, U16)
     _sb("rql%d" % _t, 12, U16)
     _sb("qf%d" % _t, 128, X4)
     _sb("sf%d" % _t, 128, U8)
 for _t in range(R + 1):
-    _sb("xb%d" % _t, XW, BF)
+    _sb("xb%d" % _t, 4 * XW, BF)
 SCRATCH["ps"] = ("psum", [128, 4096], F32)
 
 SEMAPHORES = (["cv", "ca", "ct", "cg", "sent"] + ["d%d" % i for i in range(24)]
@@ -65,6 +65,97 @@ SEMAPHORES = (["cv", "ca", "ct", "cg", "sent"] + ["d%d" % i for i in range(24)]
 
 AL = AluOpType
 AF = ActivationFunctionType
+ORDER, SPAN = [], []
+
+
+def arrange(ops, first):
+    if ORDER:
+        return ORDER[0]
+    n = len(ops)
+    pred = [set() for _ in range(n)]
+    wrote, readers = {}, {}
+    for i, (q, rd, wr, hold, lat, fn) in enumerate(ops):
+        for k in rd:
+            pred[i].update(wrote.get(k, []))
+        for k in wr:
+            if not k.startswith("land"):
+                pred[i].update(wrote.get(k, []))
+            pred[i].update(readers.get(k, []))
+        pred[i].discard(i)
+        for k in rd:
+            readers.setdefault(k, []).append(i)
+        for k in wr:
+            wrote[k] = (wrote.get(k, []) if k.startswith("land") else []) + [i]
+            readers[k] = []
+    succ = [[] for _ in range(n)]
+    for i in range(n):
+        for j in sorted(pred[i]):
+            succ[j].append(i)
+    pred = [sorted(p) for p in pred]
+    wake = TUNE["wake"]
+    hold = [o[3] for o in ops]
+    lat = [o[4] for o in ops]
+    tail = [o[3] + o[4] + wake for o in ops]
+    queue = [o[0] for o in ops]
+
+    def lay(key, back):
+        before, after = (succ, pred) if back else (pred, succ)
+        left = [len(p) for p in before]
+        at, busy, low, seen = [0.0] * n, {q: [] for q in queue}, [0.0] * n, [False] * n
+        for i0 in sorted(range(n), key=lambda i: key[i]):
+            seen[i0] = True
+            if left[i0]:
+                continue
+            todo = [i0]
+            while todo:
+                i = todo.pop()
+                h = hold[i]
+                t = low[i] + (lat[i] if back else 0.0)
+                b = busy[queue[i]]
+                k = len(b)
+                while k and b[k - 1][1] > t:
+                    k -= 1
+                while k < len(b) and b[k][0] < t + h:
+                    if b[k][1] > t:
+                        t = b[k][1]
+                    k += 1
+                b.insert(k, (t, t + h))
+                at[i] = t
+                e = t + (h + wake if back else tail[i])
+                for j in after[i]:
+                    left[j] -= 1
+                    if low[j] < e:
+                        low[j] = e
+                    if not left[j] and seen[j]:
+                        todo.append(j)
+        return at
+
+    way = [0.0] * n
+    for i in range(n - 1, -1, -1):
+        way[i] = hold[i] + lat[i] + max([way[j] + wake for j in succ[i]], default=0.0)
+    rng = np.random.default_rng(TUNE["seed"])
+    cur, best, key = None, None, [-w for w in way]
+    for it in range(TUNE["tries"]):
+        if best:
+            key = list(cur[1])
+            for _ in range(int(rng.integers(1, 4))):
+                a = int(rng.integers(first, n))
+                d = float(rng.standard_normal()) * TUNE["noise"]
+                for i in range(a, min(n, a + int(rng.integers(1, 40)))):
+                    key[i] += d
+        for turn in range(2):
+            at = lay([-1e9 + i if i < first else key[i] for i in range(n)], False)
+            span = max(at[i] + tail[i] for i in range(n))
+            if best is None or span <= best[0]:
+                best = (span, at)
+            if cur is None or span <= cur[0] + TUNE["slack"] * (1 - it / TUNE["tries"]) * rng.random():
+                cur = (span, at)
+            if turn == 0:
+                ab = lay([-(at[i] + tail[i]) for i in range(n)], True)
+                key = [-(ab[i] + hold[i]) for i in range(n)]
+    SPAN.extend([round(best[0]), {q: round(sum(hold[i] for i in range(n) if queue[i] == q)) for q in "vag"}, round(max(way))])
+    ORDER.append(sorted(range(n), key=lambda i: (best[1][i], i)))
+    return ORDER[0]
 
 
 def rank_program(g, core, T, topo):
@@ -75,26 +166,437 @@ def rank_program(g, core, T, topo):
     nxt, prv = T.cores[(rank + 1) % n], T.cores[(rank - 1) % n]
     Q = {"v": g.vector, "a": g.scalar, "t": g.tensor, "g": g, "s": g.sync}
     OWN = {"v": "cv", "a": "ca", "t": "ct", "g": "cg"}
+    ops, alias = [], {}
+    cyc = 0.83 * TUNE["f"]
+
+    def add(q, rd, wr, hold, lat, fn):
+        ops.append((q, rd.split(), wr.split(), hold, lat, fn))
+
+    def plain(w):
+        return max(64, w) * cyc
+
+    def took(w):
+        return 60 + 1.56 * w * cyc
+
+    def put(w):
+        return 50 + 3.8 * w * cyc
+
+    def op(q, rd, wr, hold, fn):
+        add(q, rd, wr, hold, 0.0, ("op", fn))
+
+    def dma(q, rd, wr, out, in_, lat=1500.0):
+        add(q, rd, wr, 60.0, lat, ("dma", out, in_))
+
+    def send(dst, rd, wr, out, in_, sem):
+        add("g", rd, wr, 300.0, TUNE["far"], ("send", dst, out, in_, sem))
+
+    V, S = g.vector, g.scalar
+
+    def ts(c, rd, wr, out, in0, s1, op0, s2=None, op1=None):
+        if op1 is None:
+            op("v", rd, wr, c, lambda: V.tensor_scalar(out, in0, s1, None, op0))
+        else:
+            op("v", rd, wr, c, lambda: V.tensor_scalar(out, in0, s1, s2, op0, op1))
+
+    def tt(c, rd, wr, out, in0, in1, o):
+        op("v", rd, wr, c, lambda: V.tensor_tensor(out, in0, in1, o))
+
+    def cp(c, rd, wr, out, in_):
+        op("v", rd, wr, c, lambda: V.tensor_copy(out, in_))
+
+    def ms(c, wr, out, x):
+        op("v", "", wr, c, lambda: V.memset(out, x))
+
+    def scan(c, rd, wr, out, d0, d1, init, op0, op1):
+        op("v", rd, wr, c, lambda: V.tensor_tensor_scan(out, d0, d1, init, op0, op1))
+
+    def act(c, rd, wr, out, in_, func=AF.Copy, **kw):
+        op("a", rd, wr, c + (20 if "accum_out" in kw else 0), lambda: S.activation(out, in_, func, **kw))
+
+    def move(on_v, c, rd, wr, out, in_):
+        (cp if on_v else act)(c, rd, wr, out, in_)
+
+    def quant(w, rd, wr, q, s, in_):
+        op("v", rd, wr, (12 + 0.88 * w) * TUNE["f"], lambda: V.quantize_mx(q, s, in_))
+
+    def mm(rd, bank, w, lq, ls, rq, rs):
+        op("t", rd, "ps%d" % bank, 60 + 0.7 * w, lambda: g.tensor.matmul_mx(T.ps[:, 512 * bank:512 * bank + w], lq, ls, rq, rs, True, True))
+
+    def iota(w, wr, out, pattern, base):
+        op("g", "", wr, 130 + 2 * w * cyc, lambda: g.iota(out, pattern, base, 0, allow_small_or_imprecise_dtypes=True))
+
+    one = plain(1)
+
+    def col(i):
+        return T.sc[:, i:i + 1]
+    LANE, LANE1, LANE2, CLS1, T0, TM4, F16, F4 = range(8)
+
+    def short(name):
+        o = K * SHORT.index(name)
+        return T.rows[:, o:o + K]
+
+    def held(rd, tmp, key, c, row, w, o):
+        buf, o = (T.rows, K * SHORT.index(tmp)) if tmp in SHORT else (T[tmp], o)
+        scan(plain(w), rd, tmp + key, buf[:, o:o + w], c[:, 0:w], row, 0.0, AL.mult, AL.max)
+        return buf, o
+
+    def lane16(rd, tmp, wr, out, row, w):
+        buf, o = held(rd + " c16x", tmp, "", T.c16x, row, w, 0)
+        ts(one, tmp + " f16", wr, out, buf[:, o + 15:o + w:16], col(F16), AL.mult, -1.0, AL.add)
+
+    def lane4(rd, tmp, wr, out, row, w, o=0, key=""):
+        buf, o = held(rd + " c4x", tmp, key, T.c4x, row, w, o)
+        ts(plain(w // 4), tmp + key + " f4 tm4", wr, out, buf[:, o + 3:o + w:4], col(F4), AL.mult, col(TM4), AL.add)
+
+    dma("s", "", "tgi", T.tgi[:], T.tg[:])
+    dma("a", "", "adi", T.adi[:], T.ad[:])
+    dma("s", "", "uu", T.uu[:], T.u[:], 2200.0)
+    dma("s", "", "X0_0 X0_1", T.xb0[:, 4 * XO:4 * HO], T.x[:], 4000.0)
+    dma("s", "", "mm", T.mm[:, 0:4 * MC], T.m[:], 8000.0)
+    dma("s", "", "qw", T.qw[:].bitcast(dt.uint8), T.wc[:], 9000.0)
+    dma("s", "", "sw", T.sw[:], T.ws[:], 9500.0)
+    dma("s", "", "vv", T.vv[:], T.v[:], 10000.0)
+    nload = len(ops)
+
+    p4x, p4g = T.p4[:, 0:4], T.p4[:, 16:20]
+    op("g", "", "pidx", 140, lambda: g.iota(T.pint[:, 4:5], [[0, 1]], 0, 1))
+    iota(16, "io16", T.io16[:], [[1, 16]], 1)
+    iota(HO, "ioa", T.io1[:, 0:HO], [[1, HO]], 1)
+    ms(plain(256), "zt", T.zt[:], 0.0)
+    ms(plain(256), "ones", T.ones[:], 1.0)
+    act(plain(MC - HO), "ioa", "iob", T.io1[:, HO:MC], T.io1[:, 0:MC - HO], AF.Identity, bias=float(HO))
+    scan(plain(P), "ones", "at0", T.at[:, 0:P], T.ones[:], T.ones[:], float(DO), AL.add, AL.max)
+    scan(plain(P), "ones", "at1", T.at[:, P:MC], T.ones[:], T.ones[:], float(DO + P), AL.add, AL.max)
+    act(one, "ones", "at2", T.at[:, MC:MC + K], T.ones[:, 0:K])
+    act(one, "ones", "flgx", T.flg[:, A:AX], T.ones[:, 0:K])
+    act(plain(4 * K), "zt", "mmz", T.mm[:, 4 * MC:4 * (MC + K)], T.zt[:, 0:4 * K])
+    ts(plain(144), "ioa", "stp", T.stp[:], T.io1[:, 0:144], K + 1.0, AL.is_le)
+    act(plain(P), "ones", "tbn tbz0", T.tb[:, HO:HO + P], T.ones[:], AF.Identity, scale=K + 1.0)
+    act(plain(P), "ones", "tbz1", T.tb[:, HO + P:HO + MC], T.ones[:], AF.Identity, scale=K + 1.0)
+    act(one, "ones", "tbz2", T.tb[:, HO + MC:TW], T.ones[:, 0:K], AF.Identity, scale=K + 1.0)
+    act(one, "ones", "z48", short("z48"), T.ones[:, 0:K], AF.Identity, scale=K + 1.0)
+    ms(plain(AX // 2), "cap", T.cap[:], K + 1.0)
+    pidx = T.pint[:, 4:5]
+    ts(one, "pidx", "lanei", T.pint[:, 0:1], pidx, 15, AL.bitwise_and)
+    ts(one, "pidx", "ti", T.pint[:, 1:2], pidx, 3, AL.bitwise_and)
+    ts(one, "pidx", "clsi", T.pint[:, 2:3], pidx, 2, AL.arith_shift_right, 3, AL.bitwise_and)
+    cp(one, "lanei", "lane", col(LANE), T.pint[:, 0:1])
+    ts(one, "lanei", "lane1", col(LANE1), T.pint[:, 0:1], 1.0, AL.add)
+    ts(one, "lanei", "lane2", col(LANE2), T.pint[:, 0:1], 2.0, AL.add)
+    cp(one, "ti", "t0", col(T0), T.pint[:, 1:2])
+    ts(one, "clsi", "cls1", col(CLS1), T.pint[:, 2:3], 1.0, AL.add)
+    ts(one, "lanei", "f16", col(F16), T.pint[:, 0:1], 15.0, AL.is_equal, 1.0 - 1.0 / LIFT, AL.mult)
+    ts(one, "ti", "tm4", col(TM4), T.pint[:, 1:2], -4.0, AL.add)
+    ts(one, "io16 lane", "l16", T.l16[:], T.io16[:], 0.0, AL.mult, col(LANE), AL.add)
+    ts(one, "io16 lane1", "pa", T.pa[:, 0:16], T.io16[:], col(LANE1), AL.is_gt)
+    ts(one, "io16 lane2", "pb", T.pa[:, 16:32], T.io16[:], col(LANE2), AL.is_equal, LIFT, AL.mult)
+    ts(one, "io16 cls1", "p4x", p4x, T.io16[:, 0:4], col(CLS1), AL.is_gt, LIFT, AL.mult)
+    ts(one, "io16 t0", "l4", T.l4[:], T.io16[:], 0.0, AL.mult, col(T0), AL.add)
+    tt(one, "pa pb", "p16x", T.p16x[:], T.pa[:, 0:16], T.pa[:, 16:32], AL.max)
+    ts(one, "p4x", "p4g", p4g, p4x, (1.0 / LIFT - 1.0) / LIFT, AL.mult, 1.0, AL.add)
+    ts(one, "f16", "f16", col(F16), col(F16), 1.0 / LIFT, AL.add)
+    op("v", "p4g", "f4", one, lambda: V.tensor_reduce(col(F4), p4g, AxisListType.X, AL.mult))
+    ts(one, "f4", "f4", col(F4), col(F4), 4.0, AL.mult)
+    act(took(A), "p16x l16", "c16x", T.c16x[:], T.p16x[:].indirect(T.l16[:]))
+    act(took(A), "p4x l4", "c4x", T.c4x[:], p4x.indirect(T.l4[:]))
+    ts(one, "io16", "ul", T.ul[:], T.io16[:, 0:12], -1.0, AL.add, 16.0, AL.mult)
+    ts(one, "ul", "ol", T.ol[:], T.ul[:], 15.0, AL.add)
+    ts(one, "ul lane", "kk", T.kk[:, 0:3], T.ul[:, 0:3], col(LANE), AL.add)
+    ts(one, "kk", "kkh", T.kk[:, 4:7], T.kk[:, 0:3], 0.5, AL.add)
+    ts(one, "pa", "pcl", T.pcl[:], T.pa[:, 0:16], -0.5, AL.add, 2.0 * BIG, AL.mult)
+    act(plain(A), "ones", "c4m", T.c4m[:], T.ones[:, 0:A], AF.Identity, scale=-BIG)
+    act(one, "ones", "c4m", T.c4m[:, 0:A:4], T.ones[:, 0:A // 4], AF.Identity, scale=BIG)
+    act(took(N2), "pcl l16", "cl", T.cl[:], T.pcl[:].indirect(T.l16[:, 0:S2]))
+    act(plain(N2), "cl", "cr", T.cr[:], T.cl[:], AF.Identity, scale=-1.0)
+    iota(N2, "ramp0", T.ramp0[:], [[0, S2], [1, 16]], 0)
+    if max(TUNE["m3v"]):
+        iota(3 * N1, "ramp1", T.ramp1[:], [[0, 3], [1, N1]], 0)
+    iota(K, "neg", short("neg"), [[-1, K]], -HO - 1)
+    iota(K, "kh", short("kh"), [[-2, K]], -1)
+    act(plain(512 - 4 * K), "zt", "ftz", T.ft[:, 4 * K:512], T.zt[:, 4 * K:512])
+    for t in range(R):
+        act(one, "zt", "Z%d" % t, T["xb%d" % t][:, 4 * K:4 * XO], T.zt[:, 0:4 * (XO - K)])
+        act(plain(4 * K), "zt", "Y%d" % t, T["xb%d" % t][:, 4 * (HO + A):4 * XW], T.zt[:, 0:4 * K])
+        iota(P, "ee%d" % t, T["ee%d" % t][:, XO:HO], [[1, P]], XO + 1)
+        act(one, "zt", "en%d" % t, T["ee%d" % t][:, HO:DO], T.zt[:, 0:K])
+        act(one, "ioa", "adx%d" % t, T.adr[:, AX * t + A:AX * t + AX], T.io1[:, 0:K], AF.Identity, bias=float(MC))
+    for b in range(4):
+        op("g", "zt", "eb%d" % b, 170 + 1024 * cyc,
+           lambda b=b: g.affine_select(T.eb[:, 512 * b:512 * b + 512], T.zt[:], [[-1, 512]], AL.not_equal, 1.0, b, 4))
+    quant(512, "eb0 eb1 eb2 eb3", "qe", T.qe[:], T.se[:], T.eb[:])
+    quant(128, "zt", "lz", T.lq[:, K:K + 128], T.ls[:, K:K + 128], T.zt[:])
+    quant(128, "uu", "qu", T.qu[:], T.su[:], T.uu[:])
+    cp(took(128), "qu ul", "qu2", T.qu2[:].bitcast(dt.uint32), T.qu[:].bitcast(dt.uint32).indirect(T.ul[:, 0:8]))
+    act(took(128), "qu ul", "su2", T.su2[:], T.su[:].indirect(T.ul[:, 0:8]))
+    quant(128, "vv", "qv", T.qv[:], T.sv[:], T.vv[:])
+
+    cp(one, "tgi", "tg16", T.tg16[:], T.tgi[:])
+    cp(one, "adi", "ad16", T.ad16[:], T.adi[:])
+    cp(put(P), "ioa tg16", "at at0 at1 at2", T.at[:].indirect(T.tg16[:]), T.io1[:, XO:HO])
+    act(took(P), "ioa iob tg16", "tgr", T.tgr[:, XO:HO], T.io1[:].indirect(T.tg16[:]), AF.Identity, bias=-1.0)
+    act(one, "ioa", "tgra", T.tgr[:, 0:XO], T.io1[:, 0:XO])
+    act(one, "ioa", "tgrb", T.tgr[:, HO:DO], T.io1[:, 0:K], AF.Identity, bias=MC - 1.0)
+    for t in range(R):
+        act(took(A), "ioa iob ad16", "adr%d" % t, T.adr[:, AX * t:AX * t + A], T.io1[:].indirect(T.ad16[:, 16 * t:16 * t + 16]))
+    act(plain(HO), "ioa", "tbp", T.tb[:, 0:HO], T.io1[:, 0:HO])
+    tbk = "tbp tbn tbz0 tbz1 tbz2"
+
+    def ahead(t):
+        p16 = T.pre16[:, 16 * t:16 * t + 16]
+        act(took(A), "at ad16", "pre", T.pre[:], T.at[:].indirect(T.ad16[:, 16 * t:16 * t + 16]))
+        lane16("pre", "sP", "pre16_%d" % t, p16, T.pre[:], A)
+        cp(put(A), "iob pre16_%d" % t, "ee%d en%d" % (t, t), T["ee%d" % t][:].indirect(p16), T.io1[:, HO:HO + A])
+
+    def lists(t):
+        p16, j16 = T.pre16[:, 16 * t:16 * t + 16], T.j16[:, 4 * t:4 * t + 3]
+        jk, tk = "j16_%d" % t, tbk + " pre16_%d" % t
+        act(took(A), tk, "src1", T.src1[:, 0:A], T.tb[:].indirect(p16))
+        if TUNE["tvf"][t] == 1:
+            act(plain(A), "src1", "flg", T.flg[:, 0:A], T.src1[:, 0:A], AF.Relu, scale=-1.0, bias=K + 2.0)
+        elif TUNE["tvf"][t] == 2:
+            ts(took(A), tk, "flg", T.flg[:, 0:A], T.tb[:].indirect(p16), K + 2.0, AL.is_lt)
+        else:
+            act(took(A), tk, "flg", T.flg[:, 0:A], T.tb[:].indirect(p16), AF.Relu, scale=-1.0, bias=K + 2.0)
+        scan(plain(AX // 2), "flg flgx cap", "cum", T.cum[:], T.flg[:], T.cap[:], 0.0, AL.add, AL.min)
+        a, hx = 3 - TUNE["jv"][t], AX // 2
+        for s in range(3):
+            row = T.jx[:, AX * s:AX * s + AX]
+            if s < a:
+                act(plain(AX), "cum kkh", "jx%d jf%d" % (s, s), row, T.cum[:], AF.Sign, scale=-1.0, bias=T.kk[:, 4 + s:5 + s], accum_out=T.jf[:, s:s + 1])
+            else:
+                ts(plain(hx), "cum kk", "jx%d" % s, row, T.cum[:], T.kk[:, s:s + 1], AL.is_le)
+                scan(plain(hx), "jx%d" % s, "jf%d" % s, T.jc[:, hx * s:hx * s + hx], T.jx[:, AX * s:AX * s + hx], T.jx[:, AX * s + hx:AX * s + AX], 0.0, AL.add, AL.add)
+        if a:
+            ts(one, " ".join("jf%d" % s for s in range(a)), jk + "a", T.j16[:, 4 * t:4 * t + a], T.jf[:, 0:a], 0.5, AL.mult, AX / 2, AL.add)
+        if a < 3:
+            cp(one, " ".join("jf%d" % s for s in range(a, 3)), jk + "b", T.j16[:, 4 * t + a:4 * t + 3], T.jc[:, hx * a + hx - 1:3 * hx:hx])
+        jk = jk + "a " + jk + "b"
+        move(TUNE["a1v"][t], took(K), "adr%d adx%d %s" % (t, t, jk), "a1", short("a1"), T.adr[:, AX * t:AX * t + AX].indirect(j16))
+        lane4("a1", "sR", "req%d" % t, T["req%d" % t][:], short("a1"), K)
+        send(nxt, "req%d" % t, "rql%d" % t, T["rql%d" % t][:], T["req%d" % t][:], "rq%d" % t)
+        cp(put(K), "ioa " + jk, "src1", T.src1[:].indirect(j16), T.io1[:, 0:K])
+        lane4("src1", "sA", "src4", T.src4[:], T.src1[:, 0:A], A)
+        act(one, "kh cum", "sgn", short("sgn"), short("kh"), AF.Sign, scale=0.5, bias=T.cum[:, A - 1:A])
+        tt(plain(2 * K), "sgn neg", "inv", short("inv"), short("sgn"), short("neg"), AL.mult)
+        act(one, "a1", "a0", short("a0"), short("a1"), AF.Identity, bias=-1.0)
+        act(took(K), "iob " + jk, "jr", short("jr"), T.io1[:, HO:HO + AX].indirect(j16))
+        if t < R - 1:
+            lane16("a1", "sa", "a16", T.a16[:, 0:3], short("a1"), K)
+            cp(put(K), "iob a16", "at", T.at[:].indirect(T.a16[:, 0:3]), T.io1[:, HO:DO])
+            ahead(t + 1)
+
+    def ranking(i, key, kk, step, w, a, b):
+        ns, h = w // 16, w // 2
+        mx, cm, dc, rf, rk, own = T["mx%d" % i], T["cm%d" % i], T["dc%d" % i], T["rf%d" % i], T["rk%d" % i], T["ow%d" % i]
+        rd, dk = kk + " ow%d" % i, "dc%d" % i
+        less = float(i - 1)
+        for s in range(ns):
+            c, o, d = 16 * s, own[:, 16 * s + 15:16 * s + 16], dc[:, 16 * s + 15:16 * s + 16]
+            ka, kb, o0 = "mx%da%d" % (i, s), "mx%db%d" % (i, s), w * s
+            row, lrow, rrow = mx[:, o0:o0 + w], mx[:, o0:o0 + c], mx[:, o0 + c:o0 + w]
+            if s < a:
+                act(plain(w), rd, ka + " " + kb, row, key[:, step - 1:step * w:step], AF.Sign, scale=-1.0, bias=o)
+                if s:
+                    act(plain(c), "", ka + " rl%d_%d" % (i, s), lrow, lrow, AF.Sign, bias=0.5, accum_out=rf[:, ns + s:ns + s + 1])
+                act(plain(w - c), "", kb + " rr%d_%d" % (i, s), rrow, rrow, AF.Sign, bias=-0.5, accum_out=rf[:, 2 * ns + s:2 * ns + s + 1])
+                continue
+            if s:
+                ts(plain(c), rd, ka, lrow, key[:, step - 1:step * c:step], o, AL.is_le)
+            ts(plain(w - c), rd, kb, rrow, key[:, step * c + step - 1:step * w:step], o, AL.is_lt)
+            if s >= b:
+                scan(one, "%s %s %s" % (ka, kb, dk), "cm%d_%d" % (i, s), cm[:, h * s:h * s + h], mx[:, o0:o0 + h], mx[:, o0 + h:o0 + w], d, AL.add, AL.add)
+            elif w == N1:
+                act(plain(w), dk, "%s %s rs%d_%d" % (ka, kb, i, s), row, row, AF.Identity, scale=float(w), bias=d, accum_out=rf[:, s:s + 1])
+            else:
+                act(plain(w), "", "%s %s rs%d_%d" % (ka, kb, i, s), row, row, AF.Identity, accum_out=rf[:, s:s + 1])
+        done = []
+        if a:
+            if a > 1:
+                tt(one, " ".join("rl%d_%d rr%d_%d" % (i, s, i, s) for s in range(1, a)), "rt%d" % i, rf[:, 2 * ns + 1:2 * ns + a], rf[:, ns + 1:ns + a], rf[:, 2 * ns + 1:2 * ns + a], AL.add)
+            ts(one, "rt%d rr%d_0" % (i, i), "ru%d" % i, rf[:, ns:ns + a], rf[:, 2 * ns:2 * ns + a], 0.5, AL.mult, w / 2 - less, AL.add)
+            if a == 1:
+                ts(one, "ru%d %s" % (i, dk), "rk%da" % i, rk[:, 0:1], rf[:, ns:ns + 1], dc[:, 15:16], AL.add)
+            else:
+                tt(one, "ru%d %s" % (i, dk), "rv%d" % i, rf[:, 0:a], rf[:, ns:ns + a], dc[:, 15:16 * a:16], AL.add)
+                cp(one, "rv%d" % i, "rk%da" % i, rk[:, 0:a], rf[:, 0:a])
+            done.append("rk%da" % i)
+        if b > a:
+            rs = " ".join("rs%d_%d" % (i, s) for s in range(a, b))
+            if w == N1:
+                ts(one, rs, "rk%db" % i, rk[:, a:b], rf[:, a:b], 1.0 / w, AL.mult)
+            else:
+                tt(one, rs + " " + dk, "rw%d" % i, rf[:, ns + a:ns + b], rf[:, a:b], dc[:, 16 * a + 15:16 * b:16], AL.add)
+                ts(one, "rw%d" % i, "rk%db" % i, rk[:, a:b], rf[:, ns + a:ns + b], -less, AL.add)
+            done.append("rk%db" % i)
+        if b < ns:
+            ts(one, " ".join("cm%d_%d" % (i, s) for s in range(b, ns)), "rk%dc" % i, rk[:, b:ns], cm[:, h * b + h - 1:h * ns:h], -less, AL.add)
+            done.append("rk%dc" % i)
+        return " ".join(done)
+
+    h = P // 2
+
+    def lifts(t):
+        for i in range(2):
+            act(plain(h), "ee%d" % t, "hm%d" % i, T.hm[:, h * i:h * i + h], T["ee%d" % t][:, XO + h * i:XO + h * i + h], AF.Identity, scale=UP, bias=-(HO + 0.5) * UP)
+
+    ahead(0)
+    lifts(0)
+    lists(0)
+
+    banks = [[5, 6, 7, 0], [1, 2, 3, 4]]
+    for t in range(R):
+        xb, xn, e = T["xb%d" % t], T["xb%d" % (t + 1)], T["ee%d" % t]
+        ek, X, Xn = "ee%d en%d" % (t, t), "X%d_0 X%d_1" % (t, t), "X%d_0 X%d_1" % (t + 1, t + 1)
+        H = " ".join("H%d_%d" % (t, b) for b in range(8))
+        came = " ".join("C%d_%d" % (t, b) for b in range(4)) + " Z%d" % t
+        pool = "%s %s %s Y%d" % (H, X, came, t)
+        late = TUNE["late"][t]
+
+        for i in range(2):
+            c = slice(h * i, h * i + h)
+            quant(h, "X%d_%d" % (t, i), "qx%d" % i, T.qx[:, c], T.sx[:, c], xb[:, 4 * (XO + h * i):4 * (XO + h * i + h)])
+            mm("qu2 su2 qx%d" % i, 4 * i, h, T.qu2[:], T.su2[:], T.qx[:, c], T.sx[:, c])
+            tt(plain(h), "ps%d hm%d" % (4 * i, i), "k0_%d" % i, T.k0[:, c], T.ps[:, 2048 * i:2048 * i + h], T.hm[:, c], AL.max)
+            scan(plain(h), "k0_%d c4m" % i, "k1_%d" % i, T.k1[:, c], T.c4m[:], T.k0[:, c], BIG, AL.max, AL.min)
+        act(took(4 * K), "mm mmz rql%d" % t, "ft", T.ft[:, 0:4 * K], T.mm[:].indirect(T["rql%d" % t][:]))
+        qf, sf = T["qf%d" % t], T["sf%d" % t]
+        quant(128, "ft ftz", "qf%d" % t, qf[:], sf[:], T.ft[:])
+        send(prv, "qf%d" % t, "land%d" % t, T.lq[:, LAND[t]:LAND[t] + K].bitcast(dt.uint8), qf[:, 0:K].bitcast(dt.uint8), "fa%d" % t)
+        send(prv, "qf%d" % t, "land%d" % t, T.ls[:, LAND[t]:LAND[t] + K], sf[:, 0:K], "fa%d" % t)
+        tt(plain(2 * N1), "k1_0 k1_1 cl", "ra1", T.ra1[:], T.k1[:, 3:P:4], T.cl[:, 0:N1], AL.max)
+        scan(plain(N1), "ra1 cr", "ow1", T.ow1[:], T.cr[:, 0:N1], T.ra1[:], BIG, AL.max, AL.min)
+        tt(took(N1), "ow1 ol ra1", "dg1", T.dg1[:], T.ow1[:].indirect(T.ol[:, 0:S1]), T.ra1[:], AL.is_equal)
+        scan(one, "dg1 ramp0", "dc1", T.dc1[:], T.ramp0[:, 0:N1], T.dg1[:], 0.0, AL.min, AL.add)
+        rk = ranking(1, T.k1, "k1_0 k1_1", 4, N1, TUNE["sg1"][t], TUNE["sg1"][t] + TUNE["sm1"][t])
+        move(TUNE["flv"][t], took(N1), "stp " + rk, "fl", T.fl[:], T.stp[:].indirect(T.rk1[:]))
+        scan(one, "fl", "cm", T.cm[:], T.fl[:], T.fl[:], 0.0, AL.add, AL.max)
+        if TUNE["m3v"][t]:
+            for s in range(3):
+                ts(one, "cm kk", "mx3_%d" % s, T.mx3[:, N1 * s:N1 * s + N1], T.cm[:], T.kk[:, s:s + 1], AL.is_le)
+            scan(plain(192), "mx3_0 mx3_1 mx3_2 ramp1", "cm3", T.cm3[:], T.ramp1[:], T.mx3[:], 0.0, AL.min, AL.add)
+            cp(one, "cm3", "id16", T.id16[:, 0:3], T.cm3[:, N1 - 1:3 * N1:N1])
+        else:
+            for s in range(3):
+                act(plain(N1), "cm kkh", "mx3_%d idf%d" % (s, s), T.mx3[:, N1 * s:N1 * s + N1], T.cm[:], AF.Sign, scale=-1.0,
+                    bias=T.kk[:, 4 + s:5 + s], accum_out=T.jf[:, 4 + s:5 + s])
+            ts(one, "idf0 idf1 idf2", "id16", T.id16[:, 0:3], T.jf[:, 4:7], 0.5, AL.mult, N1 / 2, AL.add)
+        move(TUNE["idv"][t], took(K), "ioa id16", "idr", short("idr"), T.io1[:, 0:P].indirect(T.id16[:, 0:3]))
+        lane4("idr", "sC", "c4", T.c4[:], short("idr"), K)
+        lo = LAND[t] + K - 128 if t else 0
+        for b in range(4):
+            mm("qe lz " + " ".join("land%d" % i for i in range(t + 1)), 1 + b, 128, T.qe[:, 128 * b:128 * b + 128], T.se[:, 128 * b:128 * b + 128],
+               T.lq[:, lo:lo + 128], T.ls[:, lo:lo + 128])
+            o = 512 * (1 + b) + LAND[t] - lo
+            act(one, "ps%d" % (1 + b), "C%d_%d" % (t, b), xb[:, b:4 * K:4], T.ps[:, o:o + K])
+        for i in range(2):
+            c = slice(128 * i, 128 * i + 128)
+            move(i >= 2 - TUNE["zv"][t], took(512), "%s %s src4" % (X, came), "zz%d" % i, T.zz[:, 512 * i:512 * i + 512], xb[:, 0:4 * HO].indirect(T.src4[:, 32 * i:32 * i + 32]))
+            quant(128, "zz%d" % i, "qz%d" % i, T.qz[:, c], T.sz[:, c], T.zz[:, 512 * i:512 * i + 512])
+            for b in range(4):
+                mm("qw sw qz%d" % i, banks[i][b], 128, T.qw[:, 128 * b:128 * b + 128], T.sw[:, 128 * b:128 * b + 128], T.qz[:, c], T.sz[:, c])
+                o = 512 * banks[i][b]
+                act(plain(128), "ps%d" % banks[i][b], "H%d_%d" % (t, 4 * i + b), xb[:, 4 * HO + 512 * i + b:4 * HO + 512 * i + 512:4], T.ps[:, o:o + 128], AF.Relu, scale=0.03125)
+        k0 = "k0_0 k0_1 c4"
+        tt(took(N2), k0 + " cl", "ra2", T.ra2[:], T.k0[:].indirect(T.c4[:]), T.cl[:], AL.max)
+        move(TUNE["k2v"][t], took(N2), k0, "k2", T.k2[:], T.k0[:].indirect(T.c4[:]))
+        act(took(N2), "ioa c4", "plr", T.plr[:], T.io1[:, XO:HO].indirect(T.c4[:]))
+        scan(plain(N2), "ra2 cr", "ow2", T.ow2[:], T.cr[:], T.ra2[:], BIG, AL.max, AL.min)
+        tt(took(N2), "ow2 ol ra2", "dg2", T.dg2[:], T.ow2[:].indirect(T.ol[:]), T.ra2[:], AL.is_equal)
+        scan(plain(96), "dg2 ramp0", "dc2", T.dc2[:], T.ramp0[:], T.dg2[:], 0.0, AL.min, AL.add)
+        rk = ranking(2, T.k2, "k2", 1, N2, TUNE["sg2"][t], TUNE["sg2"][t] + TUNE["sm2"][t])
+        cp(put(N2), "plr " + rk, "vr", T.vr[:].indirect(T.rk2[:]), T.plr[:])
+
+        def gather_x():
+            xp = TUNE["xp"]
+            w = P // xp
+            for i in range(2):
+                lane4("ee%d" % t, "sE", "e4_%d" % i, T.e4[:, 64 * i:64 * i + 64], e[:, XO + h * i:XO + h * i + h], h, h * i, str(i))
+                alias["X%d_%d" % (t + 1, i)] = ["Xp%d_%d" % (t + 1, j) for j in range(xp) if j * 2 // xp == i]
+            for i in range(xp):
+                move(i >= xp - TUNE["xv"][t], took(4 * w), "%s e4_%d" % (pool, i * 2 // xp), "Xp%d_%d" % (t + 1, i),
+                     xn[:, 4 * (XO + w * i):4 * (XO + w * i + w)], xb[:].indirect(T.e4[:, w // 4 * i:w // 4 * (i + 1)]))
+
+        if not late:
+            gather_x()
+            lane4("jr", "sH", "hv4", T.hv4[:], short("jr"), K)
+            act(took(4 * K), pool + " hv4", "hv", T.hv[:], xb[:].indirect(T.hv4[:]))
+        vr1, v16 = T.tb[:, HO:DO], T.v16[:, 0:3]
+        tt(plain(2 * K), "vr inv", "tbn", vr1, T.vr[:, 0:K], short("inv"), AL.max)
+        lane16("tbn", "sV", "v16", v16, vr1, K)
+        if not late:
+            lane4("tbn", "sW", "v4", T.v4[:], vr1, K)
+            cp(put(4 * K), "hv v4", Xn, xn[:, 0:4 * DO].indirect(T.v4[:]), T.hv[:])
+        if t == 0:
+            if TUNE["oldv"]:
+                ts(took(K), "tgr tgra tgrb v16", "old", short("old"), T.tgr[:].indirect(v16), 1.0, AL.add)
+            else:
+                act(took(K), "tgr tgra tgrb v16", "old", short("old"), T.tgr[:].indirect(v16), AF.Identity, bias=1.0)
+            act(one, "old", "olv", short("olv"), short("old"), AF.Identity, bias=float(DO))
+            lane16("old", "so", "o16", T.o16[:, 0:3], short("old"), K)
+            cp(put(K), "olv o16", "at", T.at[:].indirect(T.o16[:, 0:3]), short("olv"))
+            cp(put(K), "tbn a16", "at", T.at[:].indirect(T.a16[:, 0:3]), vr1)
+        cp(put(K), "a0 v16", "tgr tgra tgrb", T.tgr[:].indirect(v16), short("a0"))
+        if t < R - 1:
+            en, nk = T["ee%d" % (t + 1)], "ee%d en%d" % (t + 1, t + 1)
+            tt(plain(2 * K), "en%d tbn" % (t + 1), "ve", short("ve"), en[:, HO:DO], vr1, AL.max)
+            if t:
+                iota(P, "tbp", T.tb[:, XO:HO], [[1, P]], XO + 1)
+            cp(put(K), "z48 v16", "tbp tbn", T.tb[:, 0:DO].indirect(v16), short("z48"))
+            cp(put(K), "ve v16", nk, en[:, 0:DO].indirect(v16), short("ve"))
+            lifts(t + 1)
+            if late:
+                cp(put(K), "jr v16", ek, e[:, 0:DO].indirect(v16), short("jr"))
+                gather_x()
+            lists(t + 1)
+
+    xb = T["xb%d" % R]
+    for i in range(2):
+        c = slice(h * i, h * i + h)
+        quant(h, "X%d_%d" % (R, i), "qx%d" % i, T.qx[:, c], T.sx[:, c], xb[:, 4 * (XO + h * i):4 * (XO + h * i + h)])
+        mm("qv qx%d" % i, 2 + i, h, T.qv[:], T.sv[:], T.qx[:, c], T.sx[:, c])
+    dma("s", "qx0 qx1", "oc", T.oc[:], T.qx[:].bitcast(dt.uint8), 2500.0)
+    act(plain(h), "ps2", "hm0", T.hm[:, 0:h], T.ps[:, 1024:1024 + h])
+    dma("a", "hm0", "y0", T.y[:, 0:h], T.hm[:, 0:h], 2000.0)
+    cp(plain(h), "ps3", "k1_0", T.k1[:, 0:h], T.ps[:, 1536:1536 + h])
+    for k in range(4):
+        dma("s", "qx0 qx1", "osc%d" % k, T.osc[4 * k:4 * k + 4, :], T.sx[32 * k:32 * k + 4, :])
+    dma("s", "tgr", "ot", T.ot[:], T.tgr[0:128:16, XO:HO])
+    dma("a", "k1_0", "y1", T.y[:, h:P], T.k1[:, 0:h], 2000.0)
+
+    ops = [(q, [x for k in rd for x in alias.get(k, [k])], [x for k in wr for x in alias.get(k, [k])], a, b, f) for q, rd, wr, a, b, f in ops]
     known = {q: {} for q in Q}
     count, wrote, readers = {}, {}, {}
-    ndma = [0]
-
-    def need(q, tok):
-        sem, val, clock = tok
-        if known[q].get(sem, 0) < val:
-            Q[q].wait_ge(T.sem[sem], val)
-            for s, x in clock.items():
-                if known[q].get(s, 0) < x:
-                    known[q][s] = x
-
-    def before(q, rd, wr):
+    for t in range(R):
+        for key, sem, src, writes in (("rql%d" % t, "rq%d" % t, prv, 1), ("land%d" % t, "fa%d" % t, nxt, 2)):
+            count[sem] = writes * len(topo.engines(src, core))
+            wrote[key] = (sem, count[sem], {sem: count[sem]})
+    ndma = 0
+    for i in arrange(ops, nload):
+        q, rd, wr, _, _, fn = ops[i]
+        if fn[0] == "send":
+            wr = []
         toks = [wrote[k] for k in rd + wr if k in wrote]
         for k in wr:
             toks += readers.get(k, [])
-        for tok in sorted(toks, key=lambda z: -z[1]):
-            need(q, tok)
-
-    def after(q, sem, inc, rd, wr):
+        for sem, val, clock in sorted(toks, key=lambda z: -z[1]):
+            if known[q].get(sem, 0) < val:
+                Q[q].wait_ge(T.sem[sem], val)
+                for s, x in clock.items():
+                    if known[q].get(s, 0) < x:
+                        known[q][s] = x
+        if fn[0] == "send":
+            dst = fn[1]
+            rid, pid, _ = topo.addr(dst)
+            g.remote_dma(fn[2], fn[3], T.sem[fn[4]], T.sem.sent, pid, rid, topo.mask(core, dst))
+            count["sent"] = count.get("sent", 0) + len(topo.engines(core, dst))
+            continue
+        if fn[0] == "dma":
+            sem, inc = "d%d" % ndma, 16
+            ndma += 1
+            Q[q].dma_start(fn[1], fn[2]).then_inc(T.sem[sem], 16)
+        else:
+            sem, inc = OWN[q], 1
+            fn[1]().then_inc(T.sem[sem], 1)
         count[sem] = count.get(sem, 0) + inc
         clock = dict(known[q])
         clock[sem] = count[sem]
@@ -104,356 +606,6 @@ def rank_program(g, core, T, topo):
         for k in wr:
             wrote[k] = tok
             readers[k] = []
-
-    def op(q, rd, wr, fn):
-        rd, wr = rd.split(), wr.split()
-        before(q, rd, wr)
-        fn().then_inc(T.sem[OWN[q]], 1)
-        after(q, OWN[q], 1, rd, wr)
-
-    def dma(q, rd, wr, out, in_):
-        rd, wr = rd.split(), wr.split()
-        before(q, rd, wr)
-        sem = "d%d" % ndma[0]
-        ndma[0] += 1
-        Q[q].dma_start(out, in_).then_inc(T.sem[sem], 16)
-        after(q, sem, 16, rd, wr)
-
-    def send(dst, rd, out, in_, sem):
-        before("g", rd.split(), [])
-        rid, pid, _ = topo.addr(dst)
-        g.remote_dma(out, in_, T.sem[sem], T.sem.sent, pid, rid, topo.mask(core, dst))
-        count["sent"] = count.get("sent", 0) + len(topo.engines(core, dst))
-
-    def lands(key, sem, src, writes):
-        count[sem] = writes * len(topo.engines(src, core))
-        wrote[key] = (sem, count[sem], {sem: count[sem]})
-
-    V, S = g.vector, g.scalar
-
-    def ts(rd, wr, out, in0, s1, op0, s2=None, op1=None):
-        if op1 is None:
-            op("v", rd, wr, lambda: V.tensor_scalar(out, in0, s1, None, op0))
-        else:
-            op("v", rd, wr, lambda: V.tensor_scalar(out, in0, s1, s2, op0, op1))
-
-    def tt(rd, wr, out, in0, in1, o):
-        op("v", rd, wr, lambda: V.tensor_tensor(out, in0, in1, o))
-
-    def cp(rd, wr, out, in_):
-        op("v", rd, wr, lambda: V.tensor_copy(out, in_))
-
-    def ms(wr, out, c):
-        op("v", "", wr, lambda: V.memset(out, c))
-
-    def scan(rd, wr, out, d0, d1, init, op0, op1):
-        op("v", rd, wr, lambda: V.tensor_tensor_scan(out, d0, d1, init, op0, op1))
-
-    def act(rd, wr, out, in_, func=AF.Copy, **kw):
-        op("a", rd, wr, lambda: S.activation(out, in_, func, **kw))
-
-    def fill(wr, out, w, c):
-        act("zt", wr, out, T.zt[:, 0:w], AF.Identity, bias=c)
-
-    def quant(rd, wr, q, s, in_):
-        op("v", rd, wr, lambda: V.quantize_mx(q, s, in_))
-
-    def mm(rd, bank, w, lq, ls, rq, rs):
-        op("t", rd, "ps%d" % bank, lambda: g.tensor.matmul_mx(T.ps[:, 512 * bank:512 * bank + w], lq, ls, rq, rs, True, True))
-
-    def iota(wr, out, pattern, base):
-        op("g", "", wr, lambda: g.iota(out, pattern, base, 0, allow_small_or_imprecise_dtypes=True))
-
-    def col(i):
-        return T.sc[:, i:i + 1]
-    LANE, LANE1, LANE2, CLS1, T0, TM4, F16, F4 = range(8)
-
-    def lane16(rd, tmp, wr, row, w):
-        scan(rd + " c16x", tmp, T[tmp][:, 0:w], T.c16x[:, 0:w], row, 0.0, AL.mult, AL.max)
-        ts(tmp + " f16", wr, T[wr][:, 0:w // 16], T[tmp][:, 15:w:16], col(F16), AL.mult, -1.0, AL.add)
-
-    def lane4(rd, tmp, wr, row, w):
-        scan(rd + " c4x", tmp, T[tmp][:, 0:w], T.c4x[:, 0:w], row, 0.0, AL.mult, AL.max)
-        ts(tmp + " f4 tm4", wr, T[wr][:, 0:w // 4], T[tmp][:, 3:w:4], col(F4), AL.mult, col(TM4), AL.add)
-
-    for t in range(R):
-        lands("rql%d" % t, "rq%d" % t, prv, 1)
-        lands("land%d" % t, "fa%d" % t, nxt, 2)
-
-    dma("s", "", "tgi", T.tgi[:], T.tg[:])
-    dma("a", "", "adi", T.adi[:], T.ad[:])
-    dma("s", "", "uu", T.uu[:], T.u[:])
-    dma("s", "", "X0", T.xb0[:, XO:CO], T.x[:])
-    dma("s", "", "mm", T.mm[:, 0:4 * MC], T.m[:])
-    dma("s", "", "qw", T.qw[:].bitcast(dt.uint8), T.wc[:])
-    dma("s", "", "sw", T.sw[:], T.ws[:])
-    dma("s", "", "vv", T.vv[:], T.v[:])
-
-    p4x, p4m, p4g = T.p4[:, 0:4], T.p4[:, 8:12], T.p4[:, 16:20]
-    op("g", "", "pidx", lambda: g.iota(T.pidx[:, 0:1], [[0, 1]], 0, 1))
-    iota("io16", T.io16[:], [[1, 16]], 1)
-    iota("ioa", T.io1[:, 0:P], [[1, P]], 1)
-    iota("iob", T.io1[:, P:MC], [[1, MC - P]], P + 1)
-    iota("ramp0", T.ramp0[:], [[0, S1], [1, 16]], 0)
-    ms("zt", T.zt[:], 0.0)
-    fill("at0", T.at[:, 0:P], P, LIFT)
-    fill("at1", T.at[:, P:MC], P, LIFT)
-    fill("at2", T.at[:, MC:MC + K], K, LIFT)
-    ts("pidx", "lanei", T.pint[:, 0:1], T.pidx[:, 0:1], 15, AL.bitwise_and)
-    ts("pidx", "ti", T.pint[:, 1:2], T.pidx[:, 0:1], 3, AL.bitwise_and)
-    ts("pidx", "clsi", T.pint[:, 2:3], T.pidx[:, 0:1], 2, AL.arith_shift_right, 3, AL.bitwise_and)
-    cp("lanei", "lane", col(LANE), T.pint[:, 0:1])
-    ts("lanei", "lane1", col(LANE1), T.pint[:, 0:1], 1.0, AL.add)
-    ts("lanei", "lane2", col(LANE2), T.pint[:, 0:1], 2.0, AL.add)
-    cp("ti", "t0", col(T0), T.pint[:, 1:2])
-    ts("clsi", "cls1", col(CLS1), T.pint[:, 2:3], 1.0, AL.add)
-    ts("lanei", "f16", col(F16), T.pint[:, 0:1], 15.0, AL.is_equal, 1.0 - 1.0 / LIFT, AL.mult)
-    ts("ti", "tm4", col(TM4), T.pint[:, 1:2], -4.0, AL.add)
-    ts("io16 lane", "l16", T.l16[:], T.io16[:], 0.0, AL.mult, col(LANE), AL.add)
-    ts("io16 lane1", "pa", T.pa[:, 0:16], T.io16[:], col(LANE1), AL.is_gt)
-    ts("io16 lane2", "pb", T.pa[:, 16:32], T.io16[:], col(LANE2), AL.is_equal, LIFT, AL.mult)
-    ts("io16 cls1", "p4x", p4x, T.io16[:, 0:4], col(CLS1), AL.is_gt, LIFT, AL.mult)
-    ts("io16 t0", "l4a", T.l4[:, 0:16], T.io16[:], 0.0, AL.mult, col(T0), AL.add)
-    ts("io16 t0", "l4b", T.l4[:, 16:32], T.io16[:], 0.0, AL.mult, col(T0), AL.add)
-    tt("pa pb", "p16x", T.p16x[:], T.pa[:, 0:16], T.pa[:, 16:32], AL.max)
-    ts("p4x", "p4g", p4g, p4x, (1.0 / LIFT - 1.0) / LIFT, AL.mult, 1.0, AL.add)
-    ts("f16", "f16", col(F16), col(F16), 1.0 / LIFT, AL.add)
-    cp("tgi", "tg16", T.tg16[:], T.tgi[:])
-    op("v", "p4g", "f4", lambda: V.tensor_reduce(col(F4), p4g, AxisListType.X, AL.mult))
-    cp("ioa tg16", "at at0 at1 at2", T.at[:].indirect(T.tg16[:]), T.io1[:, 0:P])
-    cp("adi", "ad16", T.ad16[:], T.adi[:])
-
-    def addresses(t):
-        act("ioa iob ad16", "adr", T.adr[:, 0:A], T.io1[:].indirect(T.ad16[:, 16 * t:16 * t + 16]))
-
-    def flags(t):
-        act("at ad16", "flg", T.flg[:], T.at[:].indirect(T.ad16[:, 16 * t:16 * t + 16]), AF.Relu, scale=2.0 / LIFT, bias=-1.0)
-
-    def lists(t):
-        e, ek = T["ee%d" % t], "ee%d eeb%d" % (t, t)
-        scan("flg", "cum", T.cum[:], T.flg[:], T.flg[:], float(P), AL.add, AL.max)
-        tt("at ad16 cum", "src1", T.src1[:], T.at[:].indirect(T.ad16[:, 16 * t:16 * t + 16]), T.cum[:], AL.min)
-        lane16("src1", "sA", "src16", T.src1[:], A)
-        cp("ioa src16", ek, e[:].indirect(T.src16[:]), T.io1[:, 0:A])
-        act(ek, "hm", T.hm[:], e[:, 0:P], AF.Identity, scale=-UP, bias=(A + 0.5) * UP)
-        lane16(ek, "sJ", "j16", e[:, P:P + K], K)
-        cp("adr adrb j16", "a1", T.a1[:], T.adr[:].indirect(T.j16[:, 0:3]))
-        lane4("a1", "sR", "req%d" % t, T.a1[:], K)
-        send(nxt, "req%d" % t, T["rql%d" % t][:], T["req%d" % t][:], "rq%d" % t)
-
-    def zeros(t):
-        act("zt", "Za%d" % t, T["xb%d" % t][:, ZO:ZO + 512], T.zt[:])
-        act("zt", "Zb%d" % t, T["xb%d" % t][:, ZO + 512:XW], T.zt[:, 0:XW - ZO - 512])
-
-    def unit(b):
-        op("g", "zt", "eb%d" % b, lambda: g.affine_select(T.eb[:, 512 * b:512 * b + 512], T.zt[:], [[-1, 512]], AL.not_equal, 1.0, b, 4))
-
-    act("p16x l16", "c16x", T.c16x[:], T.p16x[:].indirect(T.l16[:]))
-    act("ioa", "ee0", T.ee0[:, 0:P], T.io1[:, 0:P], AF.Identity, bias=float(A))
-    act("ioa", "eeb0", T.ee0[:, P:P + A], T.io1[:, 0:A], AF.Identity, bias=float(A))
-    act("p4x l4a l4b", "c4x", T.c4x[:], p4x.indirect(T.l4[:]))
-    flags(0)
-    act("ioa", "adrb", T.adr[:, A:A + K], T.io1[:, 0:K], AF.Identity, bias=float(MC))
-    addresses(0)
-    unit(0)
-    unit(1)
-    unit(2)
-    ts("io16", "ul", T.ul[:], T.io16[:, 0:8], -1.0, AL.add, 16.0, AL.mult)
-    quant("uu", "qu", T.qu[:], T.su[:], T.uu[:])
-    ts("io16", "p4m", p4m, T.io16[:, 0:4], 1.5, AL.is_lt, -0.5, AL.add)
-    cp("qu ul", "qu2", T.qu2[:].bitcast(dt.uint32), T.qu[:].bitcast(dt.uint32).indirect(T.ul[:]))
-    ts("pa", "pcl", T.pcl[:], T.pa[:, 0:16], -0.5, AL.add, 2.0 * BIG, AL.mult)
-    ts("f4", "f4", col(F4), col(F4), 4.0, AL.mult)
-    act("qu ul", "su2", T.su2[:], T.su[:].indirect(T.ul[:]))
-    act("p4m l4a l4b", "c4m", T.c4m[:], p4m.indirect(T.l4[:]), AF.Identity, scale=2.0 * BIG)
-    lists(0)
-    unit(3)
-    iota("ramp1", T.ramp1[:], [[0, 3], [1, N1]], 0)
-    act("pcl l16", "cl", T.cl[:], T.pcl[:].indirect(T.l16[:, 0:S2]))
-    act("cl", "cr", T.cr[:], T.cl[:], AF.Identity, scale=-1.0)
-    act("zt", "ftz", T.ft[:, 4 * K:512], T.zt[:, 4 * K:512])
-    act("zt", "mmz", T.mm[:, 4 * MC:4 * (MC + K)], T.zt[:, 0:4 * K])
-    fill("ra2p", T.ra2[:, N2:W2], 16, BIG)
-    fill("rb2p", T.rb2[:, 0:16], 16, BIG)
-    fill("missrow", T.missrow[:], K, LIFT)
-
-    banks = [[5, 6, 7, 0], [1, 2, 3, 4]]
-    for t in range(R):
-        xb, xn, e = T["xb%d" % t], T["xb%d" % (t + 1)], T["ee%d" % t]
-        ek, X, Xn = "ee%d eeb%d" % (t, t), "X%d" % t, "X%d" % (t + 1)
-        H = " ".join("H%d_%d" % (t, b) for b in range(8))
-        came = " ".join("C%d_%d" % (t, b) for b in range(4))
-        last, s1a, sc, sa = t == R - 1, S1A[t], SC[t], SC[t] + SA[t]
-
-        def serve():
-            act("mm mmz rql%d" % t, "ft", T.ft[:, 0:4 * K], T.mm[:].indirect(T["rql%d" % t][:]))
-            qf, sf = T["qf%d" % t], T["sf%d" % t]
-            quant("ft ftz", "qf%d" % t, qf[:], sf[:], T.ft[:])
-            send(prv, "qf%d" % t, T.lq[:, LAND[t]:LAND[t] + K].bitcast(dt.uint8), qf[:, 0:K].bitcast(dt.uint8), "fa%d" % t)
-            send(prv, "qf%d" % t, T.ls[:, LAND[t]:LAND[t] + K], sf[:, 0:K], "fa%d" % t)
-            if t == 0:
-                iota("ramp2", T.ramp2[:], [[0, S2], [1, W2]], 0)
-            if not last:
-                iota("ee%d" % (t + 1), T["ee%d" % (t + 1)][:, 0:P], [[1, P]], A + 1)
-                iota("eeb%d" % (t + 1), T["ee%d" % (t + 1)][:, P:P + A], [[1, A]], A + 1)
-
-        def layer(i):
-            c = slice(128 * i, 128 * i + 128)
-            quant("zz%d" % i, "qz%d" % i, T.qz[:, c], T.sz[:, c], T.zz[:, 512 * i:512 * i + 512])
-            for b in range(4):
-                mm("qw sw qz%d" % i, banks[i][b], 128, T.qw[:, 128 * b:128 * b + 128], T.sw[:, 128 * b:128 * b + 128], T.qz[:, c], T.sz[:, c])
-
-        def relu(i):
-            for b in range(4):
-                o = 512 * banks[i][b]
-                act("ps%d" % banks[i][b], "H%d_%d" % (t, 4 * i + b), xb[:, 512 * i + b:512 * i + 512:4], T.ps[:, o:o + 128], AF.Relu, scale=0.03125)
-
-        quant(X, "qx", T.qx[:], T.sx[:], xb[:, XO:CO])
-        mm("qu2 su2 qx", 0, P, T.qu2[:], T.su2[:], T.qx[:], T.sx[:])
-        ts("iob cum", "iv0", T.iv0[:], T.io1[:, P:P + K], T.cum[:, A - 1:A], AL.is_gt)
-        lane4("src1", "sA", "src4", T.src1[:], A)
-        tt("iv0 iob", "inv", T.inv[:], T.iv0[:], T.io1[:, P:P + K], AL.mult)
-        if last:
-            lane4(ek, "sR", "hv4", e[:, P:P + K], K)
-        else:
-            lane16("a1", "so", "a16", T.a1[:], K)
-            act(ek, "jk", T.jk[:], e[:, P:P + K])
-        if t == 0:
-            ts("ul", "ol", T.ol[:], T.ul[:], 15.0, AL.add)
-        if not last:
-            addresses(t + 1)
-        tt("ps0 hm", "k0", T.k0[:], T.ps[:, 0:P], T.hm[:], AL.max)
-        scan("k0 c4m", "k1", T.k1[:], T.c4m[:], T.k0[:], BIG, AL.max, AL.min)
-        tt("k1 cl", "ra1", T.ra1[:], T.k1[:, 3:P:4], T.cl[:, 0:N1], AL.max)
-        if t == 0:
-            quant("zt", "lz", T.lq[:, K:K + 128], T.ls[:, K:K + 128], T.zt[:])
-        scan("ra1 cr", "ow1", T.ow1[:], T.cr[:, 0:N1], T.ra1[:], BIG, AL.max, AL.min)
-        if t == 0:
-            quant("eb0 eb1 eb2 eb3", "qe", T.qe[:], T.se[:], T.eb[:])
-        zeros(t)
-        if QF[t] < 0:
-            serve()
-        tt("ow1 ol ra1", "dg", T.dg[:], T.ow1[:].indirect(T.ol[:]), T.ra1[:], AL.is_equal)
-        for s in range(S1):
-            c, o, row = 16 * s, T.ow1[:, 16 * s + 15:16 * s + 16], T.mx1[:, N1 * s:N1 * s + N1]
-            if s:
-                ts("k1 ow1", "mx1a%d" % s, row[:, 0:c], T.k1[:, 3:4 * c:4], o, AL.is_le)
-            ts("k1 ow1", "mx1b%d" % s, row[:, c:N1], T.k1[:, 4 * c + 3:P:4], o, AL.is_lt)
-            if s == 0:
-                scan("dg ramp0", "dc", T.dc[:], T.ramp0[:], T.dg[:], 0.0, AL.min, AL.add)
-            if QF[t] == s:
-                serve()
-            if s < s1a:
-                act("dc", "mx1a%d mx1b%d rk1_%d" % (s, s, s), row, row, AF.Identity, scale=float(N1), bias=T.dc[:, c + 15:c + 16], accum_out=T.rk1[:, s:s + 1])
-        for s in range(s1a, S1):
-            row = T.mx1[:, N1 * s:N1 * s + N1]
-            scan("dc mx1a%d mx1b%d" % (s, s), "cm1_%d" % s, T.cm1[:, N1 * s:N1 * s + N1], row, row, T.dc[:, 16 * s + 15:16 * s + 16], AL.add, AL.max)
-        if t == 0:
-            ts("ul lane", "kk", T.kk[:, 0:3], T.ul[:, 0:3], col(LANE), AL.add)
-        if last:
-            lane4(ek, "sE", "e4", e[:, 0:P], P)
-            quant("vv", "qv", T.qv[:], T.sv[:], T.vv[:])
-        ts(" ".join("rk1_%d" % s for s in range(s1a)), "rk16", T.rk16[:, 0:s1a], T.rk1[:, 0:s1a], 1.0 / N1, AL.mult)
-        if s1a < S1:
-            cp(" ".join("cm1_%d" % s for s in range(s1a, S1)), "rk16b", T.rk16[:, s1a:S1], T.cm1[:, N1 * s1a + N1 - 1:N1 * S1:N1])
-        ts("ioa rk16 rk16b", "fl", T.fl[:], T.io1[:, 0:P].indirect(T.rk16[:]), K + 1.0, AL.is_le)
-        scan("fl", "cm", T.cm[:], T.fl[:], T.fl[:], 0.0, AL.add, AL.max)
-        for s in range(3):
-            ts("cm kk", "mx3_%d" % s, T.mx3[:, N1 * s:N1 * s + N1], T.cm[:], T.kk[:, s:s + 1], AL.is_le)
-        scan("mx3_0 mx3_1 mx3_2 ramp1", "cm3", T.cm3[:], T.ramp1[:], T.mx3[:], 0.0, AL.min, AL.add)
-        cp("cm3", "id16", T.id16[:, 0:3], T.cm3[:, N1 - 1:3 * N1:N1])
-        cp("ioa id16", "idr", T.idr[:], T.io1[:, 0:P].indirect(T.id16[:, 0:3]))
-        lane4("idr", "sR", "c4", T.idr[:], K)
-        lo = LAND[t] + K - 128 if t else 0
-        for b in range(4):
-            mm("qe lz " + " ".join("land%d" % i for i in range(t + 1)), 1 + b, 128, T.qe[:, 128 * b:128 * b + 128], T.se[:, 128 * b:128 * b + 128],
-               T.lq[:, lo:lo + 128], T.ls[:, lo:lo + 128])
-            o = 512 * (1 + b) + LAND[t] - lo
-            act("ps%d" % (1 + b), "C%d_%d" % (t, b), xb[:, CO + b:ZO:4], T.ps[:, o:o + K])
-        for i in range(2):
-            act("%s %s Za%d Zb%d src4" % (X, came, t, t), "zz%d" % i, T.zz[:, 512 * i:512 * i + 512], xb[:, XO:XW].indirect(T.src4[:, 32 * i:32 * i + 32]))
-        if last:
-            act("ioa c4", "plr", T.plr[:], T.io1[:, 0:P].indirect(T.c4[:]))
-        tt("k0 c4 cl", "ra2", T.ra2[:, 0:N2], T.k0[:].indirect(T.c4[:]), T.cl[:], AL.max)
-        tt("k0 c4 cr", "rb2", T.rb2[:, 16:W2], T.k0[:].indirect(T.c4[:]), T.cr[:], AL.max)
-        scan("ra2 cr", "ow2", T.ow2[:], T.cr[:], T.ra2[:, 0:N2], BIG, AL.max, AL.min)
-        tt("ra2 rb2 ra2p rb2p", "r2", T.r2[:], T.ra2[:], T.rb2[:], AL.min)
-        for s in range(sc):
-            c, row, ks = 16 * s + 16, T.mx2[:, W2 * s:W2 * s + W2], "mx2a%d mx2b%d" % (s, s)
-            act("r2 ow2", ks, row, T.r2[:], AF.Sign, scale=-1.0, bias=T.ow2[:, c - 1:c])
-        for s in range(sc):
-            c, row = 16 * s + 16, T.mx2[:, W2 * s:W2 * s + W2]
-            act("", "mx2a%d rkl%d" % (s, s), row[:, 0:c], row[:, 0:c], AF.Sign, bias=0.5, accum_out=T.rk2f[:, S2 + s:S2 + s + 1])
-            act("", "mx2b%d rkr%d" % (s, s), row[:, c:W2], row[:, c:W2], AF.Sign, bias=-0.5, accum_out=T.rk2f[:, 2 * S2 + s:2 * S2 + s + 1])
-        for s in range(sc, S2):
-            if s == QZ[t][0]:
-                layer(0)
-                if last:
-                    relu(0)
-            if s == QZ[t][1]:
-                layer(1)
-                if last:
-                    relu(1)
-                    act("%s %s hv4" % (H, X), "hv", T.hv[:], xb[:, 0:CO].indirect(T.hv4[:]))
-                    act("%s %s e4" % (H, X), Xn, xn[:, XO:CO], xb[:, 0:CO].indirect(T.e4[:]))
-                    act("tgr tgrb", "tgo", T.tgo[:], T.tgr[:], AF.Identity, bias=-1.0)
-                    act("a1", "old", T.old[:], T.a1[:], AF.Identity, bias=-1.0)
-            c, row = 16 * s + 16, T.mx2[:, W2 * s:W2 * s + W2]
-            ts("r2 ow2", "mx2a%d" % s, row[:, 0:c], T.r2[:, 0:c], T.ow2[:, c - 1:c], AL.is_le)
-            ts("r2 ow2", "mx2b%d" % s, row[:, c:W2], T.r2[:, c:W2], T.ow2[:, c - 1:c], AL.is_lt)
-            if s < sa:
-                act("", "mx2a%d mx2b%d rk2_%d" % (s, s, s), row, row, AF.Identity, accum_out=T.rk2f[:, s:s + 1])
-        if not last:
-            act("ioa c4", "plr", T.plr[:], T.io1[:, 0:P].indirect(T.c4[:]))
-            if t == 0:
-                act("ioa iob tg16", "tgr", T.tgr[:, 0:P], T.io1[:].indirect(T.tg16[:]))
-                act("ioa", "tgrb", T.tgr[:, P:P + K], T.io1[:, 0:K], AF.Identity, bias=float(MC))
-            relu(0)
-            relu(1)
-        if sc:
-            tt(" ".join("rkl%d rkr%d" % (s, s) for s in range(sc)), "rkc", T.rk2f[:, 0:sc], T.rk2f[:, S2:S2 + sc], T.rk2f[:, 2 * S2:2 * S2 + sc], AL.add)
-        scan(" ".join("mx2a%d mx2b%d" % (s, s) for s in range(sa, S2)) + " ramp2", "cm2", T.cm2[:, sa * W2:S2 * W2], T.ramp2[:, sa * W2:S2 * W2],
-             T.mx2[:, sa * W2:S2 * W2], 0.0, AL.min, AL.add)
-        if sc:
-            ts("rkc", "rk2c", T.rk2[:, 0:sc], T.rk2f[:, 0:sc], 0.5, AL.mult, W2 / 2 - 1.0, AL.add)
-        if sa > sc:
-            ts(" ".join("rk2_%d" % s for s in range(sc, sa)), "rk2a", T.rk2[:, sc:sa], T.rk2f[:, sc:sa], -1.0, AL.add)
-        ts("cm2", "rk2", T.rk2[:, sa:S2], T.cm2[:, sa * W2 + W2 - 1:S2 * W2:W2], -1.0, AL.add)
-        cp("plr rk2 rk2a rk2c", "vr", T.vr[:].indirect(T.rk2[:]), T.plr[:])
-        tt("vr inv", "vr1", T.vr1[:], T.vr[:, 0:K], T.inv[:], AL.max)
-        if not last:
-            lane16("vr1", "sJ", "v16", T.vr1[:], K)
-            cp("tgr tgrb v16", "old", T.old[:], T.tgr[:].indirect(T.v16[:, 0:3]))
-            cp("vr1 a16", "at", T.at[:].indirect(T.a16[:, 0:3]), T.vr1[:])
-            scan("old c16x", "so", T.so[:], T.c16x[:, 0:K], T.old[:], 0.0, AL.mult, AL.max)
-            cp("jk v16", ek, e[:].indirect(T.v16[:, 0:3]), T.jk[:])
-            ts("so f16", "o16", T.o16[:, 0:3], T.so[:, 15:K:16], col(F16), AL.mult, -1.0, AL.add)
-            scan(ek + " c4x", "sE", T.sE[:], T.c4x[:], e[:, 0:P], 0.0, AL.mult, AL.max)
-            cp("missrow o16", "at", T.at[:].indirect(T.o16[:, 0:3]), T.missrow[:])
-            flags(t + 1)
-            ts("sE f4 tm4", "e4", T.e4[:], T.sE[:, 3:P:4], col(F4), AL.mult, col(TM4), AL.add)
-            act("%s %s e4" % (H, X), Xn, xn[:, XO:CO], xb[:, 0:CO].indirect(T.e4[:]))
-            cp("a1 v16", "tgr tgrb", T.tgr[:].indirect(T.v16[:, 0:3]), T.a1[:])
-            lists(t + 1)
-        else:
-            lane4("vr1", "sR", "v4", T.vr1[:], K)
-            cp("hv v4", Xn, xn[:, XO:ZO].indirect(T.v4[:]), T.hv[:])
-
-    xb, X = T["xb%d" % R], "X%d" % R
-    h = P // 2
-    for i in range(2):
-        quant(X, ("qx " if i == 0 else "") + "qx%d" % i, T.qx[:, h * i:h * i + h], T.sx[:, h * i:h * i + h], xb[:, XO + 4 * h * i:XO + 4 * h * (i + 1)])
-        mm("qv qx%d" % i, 2 + i, h, T.qv[:], T.sv[:], T.qx[:, h * i:h * i + h], T.sx[:, h * i:h * i + h])
-    lane16("vr1", "sJ", "v16", T.vr1[:], K)
-    cp("old v16", "tgo", T.tgo[:].indirect(T.v16[:, 0:3]), T.old[:])
-    dma("s", "qx0 qx1", "oc", T.oc[:], T.qx[:].bitcast(dt.uint8))
-    act("ps2", "hm ys0", T.hm[:, 0:h], T.ps[:, 1024:1024 + h])
-    dma("a", "ys0", "y0", T.y[:, 0:h], T.hm[:, 0:h])
-    cp("ps3", "k1 ys1", T.k1[:, 0:h], T.ps[:, 1536:1536 + h])
-    for k in range(4):
-        dma("s", "qx0 qx1", "osc%d" % k, T.osc[4 * k:4 * k + 4, :], T.sx[32 * k:32 * k + 4, :])
-    dma("s", "tgo", "ot", T.ot[:], T.tgo[0:128:16, 0:P])
-    dma("a", "ys1", "y1", T.y[:, h:P], T.k1[:, 0:h])
     for sem in sorted(count):
         if known["g"].get(sem, 0) < count[sem]:
             g.wait_ge(T.sem[sem], count[sem])

@@ -1,5 +1,5 @@
 import numpy as np
-from concourse.mybir import dt, AluOpType, AxisListType, ActivationFunctionType
+from concourse.mybir import dt, AluOpType, ActivationFunctionType
 
 MC, P, A, K, R = 1024, 512, 256, 48, 3
 BIG = 1.0e29
@@ -8,16 +8,16 @@ UP = 2.0 ** 71
 N1, N2 = P // 4, 4 * K
 S1, S2 = N1 // 16, N2 // 16
 AX = A + K
-XO, HO, XW = 64, 64 + P, 64 + P + AX
-DO, TW = HO + K, HO + K + MC
+XO, HO, XW = 64, 64 + P, 64 + P + A
+NO, DO, TW = HO + K, HO + K + N2, HO + K + N2 + MC
 LAND = [0, K + 128, 2 * K + 128]
 LW = 3 * K + 128
-TUNE = dict(sg1=[1, 1, 1], sm1=[3, 3, 3], sg2=[4, 4, 0], sm2=[0, 0, 0], jv=[1, 1, 1], a1v=[0, 0, 0], k2v=[0, 0, 0], xv=[1, 1, 0], zv=[0, 0, 0],
-            late=[1, 1, 0], flv=[0, 0, 0], idv=[0, 0, 0], m3v=[0, 0, 0], oldv=0, tvf=[1, 1, 1], xp=4,
-            seed=0, tries=2000, noise=2000.0, slack=300.0, wake=150.0, far=1800.0, f=1.1)
+TUNE = dict(sg1=[1, 1, 1], sm1=[3, 3, 3], sg2=[6, 6, 2], jv=[1, 1, 1], xv=[2, 2, 1], late=[1, 1, 0], xp=4, fin=4,
+            cases=[(0.92, 240.0, 0.8, 0.4), (1.0, 200.0, 1.2, 0.2), (1.15, 140.0, 1.0, 0.4)], back=40, boost=[2000.0, 10000.0, 10000.0],
+            swaps=12000, heat=60.0, seed=0, tries=1200, noise=1200.0, slack=300.0, wake=200.0, far=1800.0, f=1.1)
 
 F32, BF, I32, U16, X4, U8 = "float32", "bfloat16", "int32", "uint16", "float8_e4m3fn_x4", "uint8"
-SHORT = "neg kh z48 a0 sgn inv ve olv old jr a1 idr sa so sV sW sR sH sC".split()
+SHORT = "z48 a0 ve olv old jr a1 sa so sV sW sR sH".split()
 SCRATCH = {}
 
 
@@ -32,22 +32,22 @@ for _n, _w, _d in [
     ("qw", 512, X4), ("sw", 512, U8), ("qx", 512, X4), ("sx", 512, U8), ("qz", 256, X4), ("sz", 256, U8),
     ("eb", 2048, BF), ("qe", 512, X4), ("se", 512, U8), ("zt", 512, BF),
     ("lq", LW, X4), ("ls", LW, U8), ("ft", 512, BF), ("zz", 4 * A, BF), ("hv", 4 * K, BF),
-    ("pint", 8, I32), ("io16", 16, F32), ("io1", MC, F32), ("sc", 16, F32), ("kk", 8, F32),
-    ("pa", 32, F32), ("p16x", 16, F32), ("pcl", 16, F32), ("p4", 24, F32),
+    ("pint", 8, I32), ("io16", 16, F32), ("io1", MC, F32), ("sc", 16, F32), ("kk", 4, F32), ("q4", 4, F32),
+    ("pd", 24, F32), ("pa", 24, F32), ("pb", 24, F32), ("px", 24, F32), ("pcl", 16, F32),
     ("l16", 16, U16), ("l4", 16, U16), ("ul", 12, U16), ("ol", 12, U16),
     ("c16x", A, F32), ("c4x", A, F32), ("c4m", A, F32), ("cl", N2, F32), ("cr", N2, F32),
-    ("ramp0", N2, BF), ("ramp1", 3 * N1, BF), ("cap", AX, BF), ("ones", P, BF), ("stp", 144, BF),
-    ("rows", len(SHORT) * K, F32), ("at", MC + K, F32), ("tgr", DO, F32), ("tb", TW, F32),
+    ("ramp0", N2, BF), ("cap", A, BF), ("ones", P, BF), ("stp", 144, BF),
+    ("rows", len(SHORT) * K, F32), ("at", MC + K, F32), ("tgr", NO, F32), ("tb", TW, F32),
     ("adr", R * AX, F32), ("pre", A, F32), ("sP", A, F32), ("pre16", R * 16, U16),
-    ("flg", AX, BF), ("cum", AX, BF), ("jx", 3 * AX, BF), ("jc", 3 * AX // 2, F32), ("jf", 8, F32), ("j16", 4 * R, U16),
+    ("flg", A, BF), ("cum", AX, BF), ("jx", 3 * AX, BF), ("jc", 3 * AX // 2, F32), ("jf", 8, F32), ("j16", 4 * R, U16),
     ("src1", AX, F32), ("sA", A, F32), ("src4", 64, U16), ("sE", P, F32), ("e4", 128, U16), ("hv4", 12, U16), ("a16", 4, U16),
     ("hm", P, F32), ("k0", P, F32), ("k1", P, F32),
     ("ra1", N1, F32), ("ow1", N1, F32), ("dg1", N1, BF), ("dc1", N1, BF), ("mx1", S1 * N1, BF), ("cm1", S1 * 64, BF),
     ("rf1", 3 * S1, F32), ("rk1", S1, U16),
-    ("fl", N1, BF), ("cm", N1, BF), ("mx3", 3 * N1, BF), ("cm3", 3 * N1, BF), ("id16", 4, U16), ("c4", 12, U16),
+    ("fl", N1, BF), ("cm", N1, BF), ("mx3", 3 * N1, BF), ("c4p", 16, U16),
     ("k2", N2, F32), ("ra2", N2, F32), ("ow2", N2, F32), ("dg2", N2, BF), ("dc2", N2, BF), ("mx2", S2 * N2, BF), ("cm2", S2 * 96, BF),
     ("rf2", 3 * S2, F32), ("rk2", S2, U16),
-    ("plr", N2, F32), ("vr", N2, F32), ("v16", 4, U16), ("v4", 12, U16), ("o16", 4, U16),
+    ("plr", N2, F32), ("v16", 4, U16), ("v4", 12, U16), ("o16", 4, U16),
 ]:
     _sb(_n, _w, _d)
 for _t in range(R):
@@ -92,11 +92,12 @@ def arrange(ops, first):
         for j in sorted(pred[i]):
             succ[j].append(i)
     pred = [sorted(p) for p in pred]
-    wake = TUNE["wake"]
+    wake, cases = TUNE["wake"], TUNE["cases"]
     hold = [o[3] for o in ops]
     lat = [o[4] for o in ops]
     tail = [o[3] + o[4] + wake for o in ops]
     queue = [o[0] for o in ops]
+    costs = [([hold[i] * f for i in range(n)], [lat[i] * far + w for i in range(n)]) for f, w, far, _ in cases]
 
     def lay(key, back):
         before, after = (succ, pred) if back else (pred, succ)
@@ -130,11 +131,39 @@ def arrange(ops, first):
                         todo.append(j)
         return at
 
+    def play(seq):
+        total, ends, whys = 0.0, [], []
+        for (hf, lf), case in zip(costs, cases):
+            end, why, free, prev = [0.0] * n, [-1] * n, {q: 0.0 for q in "vatgs"}, {q: -1 for q in "vatgs"}
+            for i in seq:
+                q = queue[i]
+                t, y = free[q], -2 - prev[q]
+                for j in pred[i]:
+                    if end[j] > t:
+                        t, y = end[j], j
+                t += hf[i]
+                free[q], prev[q], why[i], end[i] = t, i, y, t + lf[i]
+            total += case[3] * max(end)
+            ends.append(end)
+            whys.append(why)
+        return total, ends, whys
+
     way = [0.0] * n
     for i in range(n - 1, -1, -1):
         way[i] = hold[i] + lat[i] + max([way[j] + wake for j in succ[i]], default=0.0)
     rng = np.random.default_rng(TUNE["seed"])
     cur, best, key = None, None, [-w for w in way]
+    for t in range(R):
+        todo = [i for i in range(n) if ops[i][2] and ops[i][2][0].startswith("H%d_" % t)]
+        stop = min(i for i in range(n) if "j16_%da" % t in ops[i][2] or "j16_%db" % t in ops[i][2]) - TUNE["back"]
+        hot = set()
+        while todo:
+            i = todo.pop()
+            if i not in hot and i >= stop:
+                hot.add(i)
+                todo.extend(pred[i])
+        for i in hot:
+            key[i] -= TUNE["boost"][t]
     for it in range(TUNE["tries"]):
         if best:
             key = list(cur[1])
@@ -145,16 +174,60 @@ def arrange(ops, first):
                     key[i] += d
         for turn in range(2):
             at = lay([-1e9 + i if i < first else key[i] for i in range(n)], False)
-            span = max(at[i] + tail[i] for i in range(n))
-            if best is None or span <= best[0]:
-                best = (span, at)
-            if cur is None or span <= cur[0] + TUNE["slack"] * (1 - it / TUNE["tries"]) * rng.random():
-                cur = (span, at)
+            if turn or not it:
+                span = play(sorted(range(n), key=lambda i: (at[i], i)))[0]
+                if best is None or span <= best[0]:
+                    best = (span, at)
+                if cur is None or span <= cur[0] + TUNE["slack"] * (1 - it / TUNE["tries"]) * rng.random():
+                    cur = (span, at)
             if turn == 0:
                 ab = lay([-(at[i] + tail[i]) for i in range(n)], True)
                 key = [-(ab[i] + hold[i]) for i in range(n)]
-    SPAN.extend([round(best[0]), {q: round(sum(hold[i] for i in range(n) if queue[i] == q)) for q in "vag"}, round(max(way))])
-    ORDER.append(sorted(range(n), key=lambda i: (best[1][i], i)))
+    seq = sorted(range(n), key=lambda i: (best[1][i], i))
+    now = play(seq)
+    top = (now[0], seq)
+    for it in range(TUNE["swaps"]):
+        c = int(rng.integers(len(cases)))
+        end, why = now[1][c], now[2][c]
+        i, arcs = max(range(n), key=lambda i: end[i]), []
+        while i >= 0:
+            if why[i] <= -2:
+                arcs.append((-2 - why[i], i))
+                i = -2 - why[i]
+            else:
+                i = why[i]
+        if not arcs:
+            break
+        p, i = arcs[int(rng.integers(len(arcs)))]
+        if p < first:
+            continue
+        a, b = seq.index(p), seq.index(i)
+        ahead = rng.random() < 0.5
+        for _ in range(int(rng.integers(0, 4)) ** 2 // 2):
+            k = a - 1 if ahead else b + 1
+            while 0 <= k < n and queue[seq[k]] != queue[i]:
+                k += -1 if ahead else 1
+            if 0 <= k < n and seq[k] >= first:
+                a, b = (k, b) if ahead else (a, k)
+        link = pred if ahead else succ
+        moved, rest, qs = [i if ahead else p], [], set()
+        need = set(link[moved[0]])
+        for k in (range(b - 1, a - 1, -1) if ahead else range(a + 1, b + 1)):
+            j = seq[k]
+            if j in need or queue[j] in qs:
+                moved.append(j)
+                need.update(link[j])
+                qs.add(queue[j])
+            else:
+                rest.append(j)
+        new = seq[:a] + (moved[::-1] + rest[::-1] if ahead else rest + moved) + seq[b + 1:]
+        trial = play(new)
+        if trial[0] <= now[0] + TUNE["heat"] * (1 - it / TUNE["swaps"]) * rng.random() ** 2:
+            seq, now = new, trial
+            if now[0] < top[0]:
+                top = (now[0], seq)
+    SPAN.extend([round(best[0]), round(top[0]), {q: round(sum(hold[i] for i in range(n) if queue[i] == q)) for q in "vag"}, round(max(way))])
+    ORDER.append(top[1])
     return ORDER[0]
 
 
@@ -166,7 +239,7 @@ def rank_program(g, core, T, topo):
     nxt, prv = T.cores[(rank + 1) % n], T.cores[(rank - 1) % n]
     Q = {"v": g.vector, "a": g.scalar, "t": g.tensor, "g": g, "s": g.sync}
     OWN = {"v": "cv", "a": "ca", "t": "ct", "g": "cg"}
-    ops, alias = [], {}
+    ops, alias = [], {k: ["%s_%d" % (k, b) for b in range(4)] for k in ("ra2", "k2", "plr")}
     cyc = 0.83 * TUNE["f"]
 
     def add(q, rd, wr, hold, lat, fn):
@@ -229,7 +302,7 @@ def rank_program(g, core, T, topo):
 
     def col(i):
         return T.sc[:, i:i + 1]
-    LANE, LANE1, LANE2, CLS1, T0, TM4, F16, F4 = range(8)
+    LANE, CLS, T0, TM4, S0, F16, F4 = range(7)
 
     def short(name):
         o = K * SHORT.index(name)
@@ -258,8 +331,8 @@ def rank_program(g, core, T, topo):
     dma("s", "", "vv", T.vv[:], T.v[:], 10000.0)
     nload = len(ops)
 
-    p4x, p4g = T.p4[:, 0:4], T.p4[:, 16:20]
-    op("g", "", "pidx", 140, lambda: g.iota(T.pint[:, 4:5], [[0, 1]], 0, 1))
+    pidx = T.pint[:, 4:5]
+    op("g", "", "pidx", 140, lambda: g.iota(pidx, [[0, 1]], 0, 1))
     iota(16, "io16", T.io16[:], [[1, 16]], 1)
     iota(HO, "ioa", T.io1[:, 0:HO], [[1, HO]], 1)
     ms(plain(256), "zt", T.zt[:], 0.0)
@@ -268,58 +341,48 @@ def rank_program(g, core, T, topo):
     scan(plain(P), "ones", "at0", T.at[:, 0:P], T.ones[:], T.ones[:], float(DO), AL.add, AL.max)
     scan(plain(P), "ones", "at1", T.at[:, P:MC], T.ones[:], T.ones[:], float(DO + P), AL.add, AL.max)
     act(one, "ones", "at2", T.at[:, MC:MC + K], T.ones[:, 0:K])
-    act(one, "ones", "flgx", T.flg[:, A:AX], T.ones[:, 0:K])
     act(plain(4 * K), "zt", "mmz", T.mm[:, 4 * MC:4 * (MC + K)], T.zt[:, 0:4 * K])
-    ts(plain(144), "ioa", "stp", T.stp[:], T.io1[:, 0:144], K + 1.0, AL.is_le)
-    act(plain(P), "ones", "tbn tbz0", T.tb[:, HO:HO + P], T.ones[:], AF.Identity, scale=K + 1.0)
-    act(plain(P), "ones", "tbz1", T.tb[:, HO + P:HO + MC], T.ones[:], AF.Identity, scale=K + 1.0)
-    act(one, "ones", "tbz2", T.tb[:, HO + MC:TW], T.ones[:, 0:K], AF.Identity, scale=K + 1.0)
+    act(one, "ones", "stp", T.stp[:, 0:K + 1], T.ones[:, 0:K + 1])
+    act(plain(96), "zt", "stq", T.stp[:, K + 1:144], T.zt[:, K + 1:144])
+    act(plain(K + N2), "ones", "tbn", T.tb[:, HO:DO], T.ones[:, 0:K + N2])
+    act(plain(P), "ones", "tbz0", T.tb[:, DO:DO + P], T.ones[:], AF.Identity, scale=K + 1.0)
+    act(plain(P), "ones", "tbz1", T.tb[:, DO + P:TW], T.ones[:], AF.Identity, scale=K + 1.0)
     act(one, "ones", "z48", short("z48"), T.ones[:, 0:K], AF.Identity, scale=K + 1.0)
-    ms(plain(AX // 2), "cap", T.cap[:], K + 1.0)
-    pidx = T.pint[:, 4:5]
+    act(plain(A), "ones", "cap", T.cap[:], T.ones[:, 0:A], AF.Identity, scale=K + 1.0)
+    ts(one, "io16", "q4", T.q4[:], T.io16[:, 0:4], 0.5, AL.mult, N1 - 0.5, AL.add)
     ts(one, "pidx", "lanei", T.pint[:, 0:1], pidx, 15, AL.bitwise_and)
     ts(one, "pidx", "ti", T.pint[:, 1:2], pidx, 3, AL.bitwise_and)
-    ts(one, "pidx", "clsi", T.pint[:, 2:3], pidx, 2, AL.arith_shift_right, 3, AL.bitwise_and)
+    ts(one, "pidx", "clsi", T.pint[:, 2:3], pidx, 12, AL.bitwise_and)
     cp(one, "lanei", "lane", col(LANE), T.pint[:, 0:1])
-    ts(one, "lanei", "lane1", col(LANE1), T.pint[:, 0:1], 1.0, AL.add)
-    ts(one, "lanei", "lane2", col(LANE2), T.pint[:, 0:1], 2.0, AL.add)
     cp(one, "ti", "t0", col(T0), T.pint[:, 1:2])
-    ts(one, "clsi", "cls1", col(CLS1), T.pint[:, 2:3], 1.0, AL.add)
-    ts(one, "lanei", "f16", col(F16), T.pint[:, 0:1], 15.0, AL.is_equal, 1.0 - 1.0 / LIFT, AL.mult)
+    ts(one, "clsi", "cls", col(CLS), T.pint[:, 2:3], 0.25, AL.mult)
+    ts(one, "lanei", "f16", col(F16), T.pint[:, 0:1], -14.0, AL.add, 1.0 / LIFT, AL.max)
+    ts(one, "clsi", "f4", col(F4), T.pint[:, 2:3], -8.0, AL.add, 4.0 / LIFT, AL.max)
     ts(one, "ti", "tm4", col(TM4), T.pint[:, 1:2], -4.0, AL.add)
     ts(one, "io16 lane", "l16", T.l16[:], T.io16[:], 0.0, AL.mult, col(LANE), AL.add)
-    ts(one, "io16 lane1", "pa", T.pa[:, 0:16], T.io16[:], col(LANE1), AL.is_gt)
-    ts(one, "io16 lane2", "pb", T.pa[:, 16:32], T.io16[:], col(LANE2), AL.is_equal, LIFT, AL.mult)
-    ts(one, "io16 cls1", "p4x", p4x, T.io16[:, 0:4], col(CLS1), AL.is_gt, LIFT, AL.mult)
     ts(one, "io16 t0", "l4", T.l4[:], T.io16[:], 0.0, AL.mult, col(T0), AL.add)
-    tt(one, "pa pb", "p16x", T.p16x[:], T.pa[:, 0:16], T.pa[:, 16:32], AL.max)
-    ts(one, "p4x", "p4g", p4g, p4x, (1.0 / LIFT - 1.0) / LIFT, AL.mult, 1.0, AL.add)
-    ts(one, "f16", "f16", col(F16), col(F16), 1.0 / LIFT, AL.add)
-    op("v", "p4g", "f4", one, lambda: V.tensor_reduce(col(F4), p4g, AxisListType.X, AL.mult))
-    ts(one, "f4", "f4", col(F4), col(F4), 4.0, AL.mult)
-    act(took(A), "p16x l16", "c16x", T.c16x[:], T.p16x[:].indirect(T.l16[:]))
-    act(took(A), "p4x l4", "c4x", T.c4x[:], p4x.indirect(T.l4[:]))
+    ts(one, "io16 lane", "pd0", T.pd[:, 0:16], T.io16[:], col(LANE), AL.subtract)
+    ts(one, "io16 cls", "pd1", T.pd[:, 16:20], T.io16[:, 0:4], col(CLS), AL.subtract)
+    ts(one, "pd0 pd1", "pa", T.pa[:, 0:20], T.pd[:, 0:20], 1.0, AL.is_gt)
+    ts(one, "pd0 pd1", "pb", T.pb[:, 0:20], T.pd[:, 0:20], 2.0, AL.is_equal, LIFT, AL.mult)
+    tt(one, "pa pb", "px", T.px[:, 0:20], T.pa[:, 0:20], T.pb[:, 0:20], AL.max)
+    act(took(A), "px l16", "c16x", T.c16x[:], T.px[:, 0:16].indirect(T.l16[:]))
+    act(took(A), "px l4", "c4x", T.c4x[:], T.px[:, 16:20].indirect(T.l4[:]))
     ts(one, "io16", "ul", T.ul[:], T.io16[:, 0:12], -1.0, AL.add, 16.0, AL.mult)
     ts(one, "ul", "ol", T.ol[:], T.ul[:], 15.0, AL.add)
-    ts(one, "ul lane", "kk", T.kk[:, 0:3], T.ul[:, 0:3], col(LANE), AL.add)
-    ts(one, "kk", "kkh", T.kk[:, 4:7], T.kk[:, 0:3], 0.5, AL.add)
+    ts(one, "ul lane", "kk", T.kk[:, 0:3], T.ul[:, 0:3], col(LANE), AL.add, 0.5, AL.add)
     ts(one, "pa", "pcl", T.pcl[:], T.pa[:, 0:16], -0.5, AL.add, 2.0 * BIG, AL.mult)
     act(plain(A), "ones", "c4m", T.c4m[:], T.ones[:, 0:A], AF.Identity, scale=-BIG)
     act(one, "ones", "c4m", T.c4m[:, 0:A:4], T.ones[:, 0:A // 4], AF.Identity, scale=BIG)
     act(took(N2), "pcl l16", "cl", T.cl[:], T.pcl[:].indirect(T.l16[:, 0:S2]))
     act(plain(N2), "cl", "cr", T.cr[:], T.cl[:], AF.Identity, scale=-1.0)
     iota(N2, "ramp0", T.ramp0[:], [[0, S2], [1, 16]], 0)
-    if max(TUNE["m3v"]):
-        iota(3 * N1, "ramp1", T.ramp1[:], [[0, 3], [1, N1]], 0)
-    iota(K, "neg", short("neg"), [[-1, K]], -HO - 1)
-    iota(K, "kh", short("kh"), [[-2, K]], -1)
     act(plain(512 - 4 * K), "zt", "ftz", T.ft[:, 4 * K:512], T.zt[:, 4 * K:512])
     for t in range(R):
         act(one, "zt", "Z%d" % t, T["xb%d" % t][:, 4 * K:4 * XO], T.zt[:, 0:4 * (XO - K)])
-        act(plain(4 * K), "zt", "Y%d" % t, T["xb%d" % t][:, 4 * (HO + A):4 * XW], T.zt[:, 0:4 * K])
         iota(P, "ee%d" % t, T["ee%d" % t][:, XO:HO], [[1, P]], XO + 1)
-        act(one, "zt", "en%d" % t, T["ee%d" % t][:, HO:DO], T.zt[:, 0:K])
-        act(one, "ioa", "adx%d" % t, T.adr[:, AX * t + A:AX * t + AX], T.io1[:, 0:K], AF.Identity, bias=float(MC))
+        act(one, "zt", "en%d" % t, T["ee%d" % t][:, HO:NO], T.zt[:, 0:K])
+        act(one, "ioa", "adx%d" % t, T.adr[:, AX * t:AX * t + K], T.io1[:, 0:K], AF.Identity, bias=float(MC))
     for b in range(4):
         op("g", "zt", "eb%d" % b, 170 + 1024 * cyc,
            lambda b=b: g.affine_select(T.eb[:, 512 * b:512 * b + 512], T.zt[:], [[-1, 512]], AL.not_equal, 1.0, b, 4))
@@ -335,11 +398,11 @@ def rank_program(g, core, T, topo):
     cp(put(P), "ioa tg16", "at at0 at1 at2", T.at[:].indirect(T.tg16[:]), T.io1[:, XO:HO])
     act(took(P), "ioa iob tg16", "tgr", T.tgr[:, XO:HO], T.io1[:].indirect(T.tg16[:]), AF.Identity, bias=-1.0)
     act(one, "ioa", "tgra", T.tgr[:, 0:XO], T.io1[:, 0:XO])
-    act(one, "ioa", "tgrb", T.tgr[:, HO:DO], T.io1[:, 0:K], AF.Identity, bias=MC - 1.0)
+    act(one, "ioa", "tgrb", T.tgr[:, HO:NO], T.io1[:, 0:K], AF.Identity, bias=MC - 1.0)
     for t in range(R):
-        act(took(A), "ioa iob ad16", "adr%d" % t, T.adr[:, AX * t:AX * t + A], T.io1[:].indirect(T.ad16[:, 16 * t:16 * t + 16]))
+        act(took(A), "ioa iob ad16", "adr%d" % t, T.adr[:, AX * t + K:AX * t + AX], T.io1[:].indirect(T.ad16[:, 16 * t:16 * t + 16]))
     act(plain(HO), "ioa", "tbp", T.tb[:, 0:HO], T.io1[:, 0:HO])
-    tbk = "tbp tbn tbz0 tbz1 tbz2"
+    tbk = "tbp tbn tbz0 tbz1"
 
     def ahead(t):
         p16 = T.pre16[:, 16 * t:16 * t + 16]
@@ -350,46 +413,47 @@ def rank_program(g, core, T, topo):
     def lists(t):
         p16, j16 = T.pre16[:, 16 * t:16 * t + 16], T.j16[:, 4 * t:4 * t + 3]
         jk, tk = "j16_%d" % t, tbk + " pre16_%d" % t
-        act(took(A), tk, "src1", T.src1[:, 0:A], T.tb[:].indirect(p16))
-        if TUNE["tvf"][t] == 1:
-            act(plain(A), "src1", "flg", T.flg[:, 0:A], T.src1[:, 0:A], AF.Relu, scale=-1.0, bias=K + 2.0)
-        elif TUNE["tvf"][t] == 2:
-            ts(took(A), tk, "flg", T.flg[:, 0:A], T.tb[:].indirect(p16), K + 2.0, AL.is_lt)
+        act(took(A), tk, "src1", T.src1[:, K:AX], T.tb[:].indirect(p16))
+        nm, s0 = T.jf[:, 3:4], col(S0)
+        if t == 0:
+            act(plain(A), "pre", "sg0", T.jx[:, 0:A], T.pre[:], AF.Sign, bias=-DO - 0.5)
+            act(plain(A), "sg0", "flg nm", T.flg[:], T.jx[:, 0:A], AF.Relu, accum_out=nm)
         else:
-            act(took(A), tk, "flg", T.flg[:, 0:A], T.tb[:].indirect(p16), AF.Relu, scale=-1.0, bias=K + 2.0)
-        scan(plain(AX // 2), "flg flgx cap", "cum", T.cum[:], T.flg[:], T.cap[:], 0.0, AL.add, AL.min)
+            act(took(A), tk, "flg nm", T.flg[:], T.tb[:].indirect(p16), AF.Relu, scale=-1.0, bias=K + 2.0, accum_out=nm)
+        act(one, "nm", "s0", s0, nm, AF.Relu, scale=-1.0, bias=float(K))
+        scan(plain(A // 2), "flg s0 cap", "cum", T.cum[:, K:AX], T.flg[:], T.cap[:], s0, AL.add, AL.min)
+        ts(one, "ioa s0", "cumx", T.cum[:, 0:K], T.io1[:, 0:K], s0, AL.min)
         a, hx = 3 - TUNE["jv"][t], AX // 2
         for s in range(3):
-            row = T.jx[:, AX * s:AX * s + AX]
+            row, rd = T.jx[:, AX * s:AX * s + AX], "cum cumx sg0 kk"
             if s < a:
-                act(plain(AX), "cum kkh", "jx%d jf%d" % (s, s), row, T.cum[:], AF.Sign, scale=-1.0, bias=T.kk[:, 4 + s:5 + s], accum_out=T.jf[:, s:s + 1])
+                act(plain(AX), rd, "jx%d jf%d" % (s, s), row, T.cum[:], AF.Sign, scale=-1.0, bias=T.kk[:, s:s + 1], accum_out=T.jf[:, s:s + 1])
             else:
-                ts(plain(hx), "cum kk", "jx%d" % s, row, T.cum[:], T.kk[:, s:s + 1], AL.is_le)
+                ts(plain(hx), rd, "jx%d" % s, row, T.cum[:], T.kk[:, s:s + 1], AL.is_lt)
                 scan(plain(hx), "jx%d" % s, "jf%d" % s, T.jc[:, hx * s:hx * s + hx], T.jx[:, AX * s:AX * s + hx], T.jx[:, AX * s + hx:AX * s + AX], 0.0, AL.add, AL.add)
         if a:
             ts(one, " ".join("jf%d" % s for s in range(a)), jk + "a", T.j16[:, 4 * t:4 * t + a], T.jf[:, 0:a], 0.5, AL.mult, AX / 2, AL.add)
         if a < 3:
             cp(one, " ".join("jf%d" % s for s in range(a, 3)), jk + "b", T.j16[:, 4 * t + a:4 * t + 3], T.jc[:, hx * a + hx - 1:3 * hx:hx])
         jk = jk + "a " + jk + "b"
-        move(TUNE["a1v"][t], took(K), "adr%d adx%d %s" % (t, t, jk), "a1", short("a1"), T.adr[:, AX * t:AX * t + AX].indirect(j16))
+        act(took(K), "adr%d adx%d %s" % (t, t, jk), "a1", short("a1"), T.adr[:, AX * t:AX * t + AX].indirect(j16))
         lane4("a1", "sR", "req%d" % t, T["req%d" % t][:], short("a1"), K)
         send(nxt, "req%d" % t, "rql%d" % t, T["rql%d" % t][:], T["req%d" % t][:], "rq%d" % t)
         cp(put(K), "ioa " + jk, "src1", T.src1[:].indirect(j16), T.io1[:, 0:K])
-        lane4("src1", "sA", "src4", T.src4[:], T.src1[:, 0:A], A)
-        act(one, "kh cum", "sgn", short("sgn"), short("kh"), AF.Sign, scale=0.5, bias=T.cum[:, A - 1:A])
-        tt(plain(2 * K), "sgn neg", "inv", short("inv"), short("sgn"), short("neg"), AL.mult)
+        lane4("src1", "sA", "src4", T.src4[:], T.src1[:, K:AX], A)
+        act(one, "iob", "tbn", T.tb[:, HO:NO], T.io1[:, HO:NO])
         act(one, "a1", "a0", short("a0"), short("a1"), AF.Identity, bias=-1.0)
-        act(took(K), "iob " + jk, "jr", short("jr"), T.io1[:, HO:HO + AX].indirect(j16))
+        act(took(K), "ioa iob " + jk, "jr", short("jr"), T.io1[:, HO - K:HO + A].indirect(j16))
         if t < R - 1:
             lane16("a1", "sa", "a16", T.a16[:, 0:3], short("a1"), K)
-            cp(put(K), "iob a16", "at", T.at[:].indirect(T.a16[:, 0:3]), T.io1[:, HO:DO])
+            cp(put(K), "iob a16", "at", T.at[:].indirect(T.a16[:, 0:3]), T.io1[:, HO:NO])
             ahead(t + 1)
 
     def ranking(i, key, kk, step, w, a, b):
         ns, h = w // 16, w // 2
         mx, cm, dc, rf, rk, own = T["mx%d" % i], T["cm%d" % i], T["dc%d" % i], T["rf%d" % i], T["rk%d" % i], T["ow%d" % i]
         rd, dk = kk + " ow%d" % i, "dc%d" % i
-        less = float(i - 1)
+        more, mk, less = (0.0, "", 0.0) if i == 1 else (col(S0), " s0", 1.0)
         for s in range(ns):
             c, o, d = 16 * s, own[:, 16 * s + 15:16 * s + 16], dc[:, 16 * s + 15:16 * s + 16]
             ka, kb, o0 = "mx%da%d" % (i, s), "mx%db%d" % (i, s), w * s
@@ -405,31 +469,24 @@ def rank_program(g, core, T, topo):
             ts(plain(w - c), rd, kb, rrow, key[:, step * c + step - 1:step * w:step], o, AL.is_lt)
             if s >= b:
                 scan(one, "%s %s %s" % (ka, kb, dk), "cm%d_%d" % (i, s), cm[:, h * s:h * s + h], mx[:, o0:o0 + h], mx[:, o0 + h:o0 + w], d, AL.add, AL.add)
-            elif w == N1:
-                act(plain(w), dk, "%s %s rs%d_%d" % (ka, kb, i, s), row, row, AF.Identity, scale=float(w), bias=d, accum_out=rf[:, s:s + 1])
             else:
-                act(plain(w), "", "%s %s rs%d_%d" % (ka, kb, i, s), row, row, AF.Identity, accum_out=rf[:, s:s + 1])
+                act(plain(w), dk, "%s %s rs%d_%d" % (ka, kb, i, s), row, row, AF.Identity, scale=float(w), bias=d, accum_out=rf[:, s:s + 1])
         done = []
         if a:
             if a > 1:
                 tt(one, " ".join("rl%d_%d rr%d_%d" % (i, s, i, s) for s in range(1, a)), "rt%d" % i, rf[:, 2 * ns + 1:2 * ns + a], rf[:, ns + 1:ns + a], rf[:, 2 * ns + 1:2 * ns + a], AL.add)
             ts(one, "rt%d rr%d_0" % (i, i), "ru%d" % i, rf[:, ns:ns + a], rf[:, 2 * ns:2 * ns + a], 0.5, AL.mult, w / 2 - less, AL.add)
             if a == 1:
-                ts(one, "ru%d %s" % (i, dk), "rk%da" % i, rk[:, 0:1], rf[:, ns:ns + 1], dc[:, 15:16], AL.add)
+                ts(one, "ru%d %s" % (i, dk) + mk, "rk%da" % i, rk[:, 0:1], rf[:, ns:ns + 1], dc[:, 15:16], AL.add, more, AL.add)
             else:
                 tt(one, "ru%d %s" % (i, dk), "rv%d" % i, rf[:, 0:a], rf[:, ns:ns + a], dc[:, 15:16 * a:16], AL.add)
-                cp(one, "rv%d" % i, "rk%da" % i, rk[:, 0:a], rf[:, 0:a])
+                ts(one, "rv%d" % i + mk, "rk%da" % i, rk[:, 0:a], rf[:, 0:a], more, AL.add)
             done.append("rk%da" % i)
         if b > a:
-            rs = " ".join("rs%d_%d" % (i, s) for s in range(a, b))
-            if w == N1:
-                ts(one, rs, "rk%db" % i, rk[:, a:b], rf[:, a:b], 1.0 / w, AL.mult)
-            else:
-                tt(one, rs + " " + dk, "rw%d" % i, rf[:, ns + a:ns + b], rf[:, a:b], dc[:, 16 * a + 15:16 * b:16], AL.add)
-                ts(one, "rw%d" % i, "rk%db" % i, rk[:, a:b], rf[:, ns + a:ns + b], -less, AL.add)
+            ts(one, " ".join("rs%d_%d" % (i, s) for s in range(a, b)), "rk%db" % i, rk[:, a:b], rf[:, a:b], 1.0 / w, AL.mult)
             done.append("rk%db" % i)
         if b < ns:
-            ts(one, " ".join("cm%d_%d" % (i, s) for s in range(b, ns)), "rk%dc" % i, rk[:, b:ns], cm[:, h * b + h - 1:h * ns:h], -less, AL.add)
+            ts(one, " ".join("cm%d_%d" % (i, s) for s in range(b, ns)) + mk, "rk%dc" % i, rk[:, b:ns], cm[:, h * b + h - 1:h * ns:h], more, AL.add, -less, AL.add)
             done.append("rk%dc" % i)
         return " ".join(done)
 
@@ -449,7 +506,7 @@ def rank_program(g, core, T, topo):
         ek, X, Xn = "ee%d en%d" % (t, t), "X%d_0 X%d_1" % (t, t), "X%d_0 X%d_1" % (t + 1, t + 1)
         H = " ".join("H%d_%d" % (t, b) for b in range(8))
         came = " ".join("C%d_%d" % (t, b) for b in range(4)) + " Z%d" % t
-        pool = "%s %s %s Y%d" % (H, X, came, t)
+        pool = "%s %s %s" % (H, X, came)
         late = TUNE["late"][t]
 
         for i in range(2):
@@ -468,20 +525,12 @@ def rank_program(g, core, T, topo):
         tt(took(N1), "ow1 ol ra1", "dg1", T.dg1[:], T.ow1[:].indirect(T.ol[:, 0:S1]), T.ra1[:], AL.is_equal)
         scan(one, "dg1 ramp0", "dc1", T.dc1[:], T.ramp0[:, 0:N1], T.dg1[:], 0.0, AL.min, AL.add)
         rk = ranking(1, T.k1, "k1_0 k1_1", 4, N1, TUNE["sg1"][t], TUNE["sg1"][t] + TUNE["sm1"][t])
-        move(TUNE["flv"][t], took(N1), "stp " + rk, "fl", T.fl[:], T.stp[:].indirect(T.rk1[:]))
+        act(took(N1), "stp stq " + rk, "fl", T.fl[:], T.stp[:].indirect(T.rk1[:]))
         scan(one, "fl", "cm", T.cm[:], T.fl[:], T.fl[:], 0.0, AL.add, AL.max)
-        if TUNE["m3v"][t]:
-            for s in range(3):
-                ts(one, "cm kk", "mx3_%d" % s, T.mx3[:, N1 * s:N1 * s + N1], T.cm[:], T.kk[:, s:s + 1], AL.is_le)
-            scan(plain(192), "mx3_0 mx3_1 mx3_2 ramp1", "cm3", T.cm3[:], T.ramp1[:], T.mx3[:], 0.0, AL.min, AL.add)
-            cp(one, "cm3", "id16", T.id16[:, 0:3], T.cm3[:, N1 - 1:3 * N1:N1])
-        else:
-            for s in range(3):
-                act(plain(N1), "cm kkh", "mx3_%d idf%d" % (s, s), T.mx3[:, N1 * s:N1 * s + N1], T.cm[:], AF.Sign, scale=-1.0,
-                    bias=T.kk[:, 4 + s:5 + s], accum_out=T.jf[:, 4 + s:5 + s])
-            ts(one, "idf0 idf1 idf2", "id16", T.id16[:, 0:3], T.jf[:, 4:7], 0.5, AL.mult, N1 / 2, AL.add)
-        move(TUNE["idv"][t], took(K), "ioa id16", "idr", short("idr"), T.io1[:, 0:P].indirect(T.id16[:, 0:3]))
-        lane4("idr", "sC", "c4", T.c4[:], short("idr"), K)
+        for s in range(3):
+            act(plain(N1), "cm kk", "mx3_%d idf%d" % (s, s), T.mx3[:, N1 * s:N1 * s + N1], T.cm[:], AF.Sign, scale=-1.0,
+                bias=T.kk[:, s:s + 1], accum_out=T.jf[:, 4 + s:5 + s])
+            ts(one, "idf%d q4" % s, "c4p%d" % s, T.c4p[:, s:16:4], T.q4[:], T.jf[:, 4 + s:5 + s], AL.add, 2.0, AL.mult)
         lo = LAND[t] + K - 128 if t else 0
         for b in range(4):
             mm("qe lz " + " ".join("land%d" % i for i in range(t + 1)), 1 + b, 128, T.qe[:, 128 * b:128 * b + 128], T.se[:, 128 * b:128 * b + 128],
@@ -490,21 +539,22 @@ def rank_program(g, core, T, topo):
             act(one, "ps%d" % (1 + b), "C%d_%d" % (t, b), xb[:, b:4 * K:4], T.ps[:, o:o + K])
         for i in range(2):
             c = slice(128 * i, 128 * i + 128)
-            move(i >= 2 - TUNE["zv"][t], took(512), "%s %s src4" % (X, came), "zz%d" % i, T.zz[:, 512 * i:512 * i + 512], xb[:, 0:4 * HO].indirect(T.src4[:, 32 * i:32 * i + 32]))
+            act(took(512), "%s %s src4" % (X, came), "zz%d" % i, T.zz[:, 512 * i:512 * i + 512], xb[:, 0:4 * HO].indirect(T.src4[:, 32 * i:32 * i + 32]))
             quant(128, "zz%d" % i, "qz%d" % i, T.qz[:, c], T.sz[:, c], T.zz[:, 512 * i:512 * i + 512])
             for b in range(4):
                 mm("qw sw qz%d" % i, banks[i][b], 128, T.qw[:, 128 * b:128 * b + 128], T.sw[:, 128 * b:128 * b + 128], T.qz[:, c], T.sz[:, c])
                 o = 512 * banks[i][b]
                 act(plain(128), "ps%d" % banks[i][b], "H%d_%d" % (t, 4 * i + b), xb[:, 4 * HO + 512 * i + b:4 * HO + 512 * i + 512:4], T.ps[:, o:o + 128], AF.Relu, scale=0.03125)
-        k0 = "k0_0 k0_1 c4"
-        tt(took(N2), k0 + " cl", "ra2", T.ra2[:], T.k0[:].indirect(T.c4[:]), T.cl[:], AL.max)
-        move(TUNE["k2v"][t], took(N2), k0, "k2", T.k2[:], T.k0[:].indirect(T.c4[:]))
-        act(took(N2), "ioa c4", "plr", T.plr[:], T.io1[:, XO:HO].indirect(T.c4[:]))
+        for b in range(4):
+            lk, lb = "c4p0 c4p1 c4p2", T.c4p[:, 4 * b:4 * b + 3]
+            tt(took(K), "k0_0 k0_1 cl " + lk, "ra2_%d" % b, T.ra2[:, b:N2:4], T.k0[:].indirect(lb), T.cl[:, b:N2:4], AL.max)
+            act(took(K), "k0_0 k0_1 " + lk, "k2_%d" % b, T.k2[:, b:N2:4], T.k0[:].indirect(lb))
+            act(took(K), "ioa " + lk, "plr_%d" % b, T.plr[:, b:N2:4], T.io1[:, XO:HO].indirect(lb))
         scan(plain(N2), "ra2 cr", "ow2", T.ow2[:], T.cr[:], T.ra2[:], BIG, AL.max, AL.min)
         tt(took(N2), "ow2 ol ra2", "dg2", T.dg2[:], T.ow2[:].indirect(T.ol[:]), T.ra2[:], AL.is_equal)
         scan(plain(96), "dg2 ramp0", "dc2", T.dc2[:], T.ramp0[:], T.dg2[:], 0.0, AL.min, AL.add)
-        rk = ranking(2, T.k2, "k2", 1, N2, TUNE["sg2"][t], TUNE["sg2"][t] + TUNE["sm2"][t])
-        cp(put(N2), "plr " + rk, "vr", T.vr[:].indirect(T.rk2[:]), T.plr[:])
+        rk = ranking(2, T.k2, "k2", 1, N2, TUNE["sg2"][t], TUNE["sg2"][t])
+        cp(put(N2), "plr " + rk, "tbn", T.tb[:, HO:DO].indirect(T.rk2[:]), T.plr[:])
 
         def gather_x():
             xp = TUNE["xp"]
@@ -520,17 +570,13 @@ def rank_program(g, core, T, topo):
             gather_x()
             lane4("jr", "sH", "hv4", T.hv4[:], short("jr"), K)
             act(took(4 * K), pool + " hv4", "hv", T.hv[:], xb[:].indirect(T.hv4[:]))
-        vr1, v16 = T.tb[:, HO:DO], T.v16[:, 0:3]
-        tt(plain(2 * K), "vr inv", "tbn", vr1, T.vr[:, 0:K], short("inv"), AL.max)
+        vr1, v16 = T.tb[:, HO:NO], T.v16[:, 0:3]
         lane16("tbn", "sV", "v16", v16, vr1, K)
         if not late:
             lane4("tbn", "sW", "v4", T.v4[:], vr1, K)
-            cp(put(4 * K), "hv v4", Xn, xn[:, 0:4 * DO].indirect(T.v4[:]), T.hv[:])
+            cp(put(4 * K), "hv v4", Xn, xn[:, 0:4 * NO].indirect(T.v4[:]), T.hv[:])
         if t == 0:
-            if TUNE["oldv"]:
-                ts(took(K), "tgr tgra tgrb v16", "old", short("old"), T.tgr[:].indirect(v16), 1.0, AL.add)
-            else:
-                act(took(K), "tgr tgra tgrb v16", "old", short("old"), T.tgr[:].indirect(v16), AF.Identity, bias=1.0)
+            act(took(K), "tgr tgra tgrb v16", "old", short("old"), T.tgr[:].indirect(v16), AF.Identity, bias=1.0)
             act(one, "old", "olv", short("olv"), short("old"), AF.Identity, bias=float(DO))
             lane16("old", "so", "o16", T.o16[:, 0:3], short("old"), K)
             cp(put(K), "olv o16", "at", T.at[:].indirect(T.o16[:, 0:3]), short("olv"))
@@ -538,30 +584,31 @@ def rank_program(g, core, T, topo):
         cp(put(K), "a0 v16", "tgr tgra tgrb", T.tgr[:].indirect(v16), short("a0"))
         if t < R - 1:
             en, nk = T["ee%d" % (t + 1)], "ee%d en%d" % (t + 1, t + 1)
-            tt(plain(2 * K), "en%d tbn" % (t + 1), "ve", short("ve"), en[:, HO:DO], vr1, AL.max)
+            tt(plain(2 * K), "en%d tbn" % (t + 1), "ve", short("ve"), en[:, HO:NO], vr1, AL.max)
             if t:
                 iota(P, "tbp", T.tb[:, XO:HO], [[1, P]], XO + 1)
-            cp(put(K), "z48 v16", "tbp tbn", T.tb[:, 0:DO].indirect(v16), short("z48"))
-            cp(put(K), "ve v16", nk, en[:, 0:DO].indirect(v16), short("ve"))
+            cp(put(K), "z48 v16", "tbp tbn", T.tb[:, 0:NO].indirect(v16), short("z48"))
+            cp(put(K), "ve v16", nk, en[:, 0:NO].indirect(v16), short("ve"))
             lifts(t + 1)
             if late:
-                cp(put(K), "jr v16", ek, e[:, 0:DO].indirect(v16), short("jr"))
+                cp(put(K), "jr v16", ek, e[:, 0:NO].indirect(v16), short("jr"))
                 gather_x()
             lists(t + 1)
 
-    xb = T["xb%d" % R]
+    xb, fin = T["xb%d" % R], TUNE["fin"]
+    w = P // fin
+    for i in range(fin):
+        c, half = slice(w * i, w * i + w), i * 2 // fin
+        quant(w, "X%d_%d" % (R, half), "qx%d qy%d" % (half, i) if i * 2 % fin == 0 else "qy%d" % i, T.qx[:, c], T.sx[:, c], xb[:, 4 * (XO + w * i):4 * (XO + w * i + w)])
+        mm("qv qy%d" % i, 1 + i, w, T.qv[:], T.sv[:], T.qx[:, c], T.sx[:, c])
+        move(i % 2, plain(w), "ps%d" % (1 + i), "hm%d ys%d" % (half, i) if i * 2 % fin == 0 else "ys%d" % i, T.hm[:, c], T.ps[:, 512 * (1 + i):512 * (1 + i) + w])
+        dma("a" if i % 2 == 0 else "s", "ys%d" % i, "y%d" % i, T.y[:, c], T.hm[:, c], 1800.0)
     for i in range(2):
-        c = slice(h * i, h * i + h)
-        quant(h, "X%d_%d" % (R, i), "qx%d" % i, T.qx[:, c], T.sx[:, c], xb[:, 4 * (XO + h * i):4 * (XO + h * i + h)])
-        mm("qv qx%d" % i, 2 + i, h, T.qv[:], T.sv[:], T.qx[:, c], T.sx[:, c])
-    dma("s", "qx0 qx1", "oc", T.oc[:], T.qx[:].bitcast(dt.uint8), 2500.0)
-    act(plain(h), "ps2", "hm0", T.hm[:, 0:h], T.ps[:, 1024:1024 + h])
-    dma("a", "hm0", "y0", T.y[:, 0:h], T.hm[:, 0:h], 2000.0)
-    cp(plain(h), "ps3", "k1_0", T.k1[:, 0:h], T.ps[:, 1536:1536 + h])
+        dma("s", " ".join("qy%d" % j for j in range(fin) if j * 2 // fin == i), "oc%d" % i, T.oc[:, 4 * h * i:4 * h * i + 4 * h],
+            T.qx[:, h * i:h * i + h].bitcast(dt.uint8), 2000.0)
     for k in range(4):
-        dma("s", "qx0 qx1", "osc%d" % k, T.osc[4 * k:4 * k + 4, :], T.sx[32 * k:32 * k + 4, :])
+        dma("s", " ".join("qy%d" % j for j in range(fin)), "osc%d" % k, T.osc[4 * k:4 * k + 4, :], T.sx[32 * k:32 * k + 4, :])
     dma("s", "tgr", "ot", T.ot[:], T.tgr[0:128:16, XO:HO])
-    dma("a", "k1_0", "y1", T.y[:, h:P], T.k1[:, 0:h], 2000.0)
 
     ops = [(q, [x for k in rd for x in alias.get(k, [k])], [x for k in wr for x in alias.get(k, [k])], a, b, f) for q, rd, wr, a, b, f in ops]
     known = {q: {} for q in Q}

@@ -2,22 +2,24 @@ import numpy as np
 from concourse.mybir import dt, AluOpType, ActivationFunctionType
 
 MC, P, A, K, R = 1024, 512, 256, 48, 3
+L = R - 1
 BIG = 1.0e29
-LIFT = 2048.0
+LIFT = 8192.0
 UP = 2.0 ** 71
+FAR = 2.0 ** 84
 N1, N2 = P // 4, 4 * K
 S1, S2 = N1 // 16, N2 // 16
 AX = A + K
-XO, HO, XW = 64, 64 + P, 64 + P + A
-NO, DO, TW = HO + K, HO + K + N2, HO + K + N2 + MC
-LAND = [0, K + 128, 2 * K + 128]
-LW = 3 * K + 128
-TUNE = dict(sg1=[1, 1, 1], sm1=[3, 3, 3], sg2=[6, 6, 2], jv=[1, 1, 1], xv=[2, 2, 1], late=[1, 1, 0], xp=4, fin=4,
-            cases=[(0.92, 240.0, 0.8, 0.4), (1.0, 200.0, 1.2, 0.2), (1.15, 140.0, 1.0, 0.4)], back=40, boost=[2000.0, 10000.0, 10000.0],
-            swaps=12000, heat=60.0, seed=0, tries=1200, noise=1200.0, slack=300.0, wake=200.0, far=1800.0, f=1.1)
+CO, XO, HO, XW = 16, 64, 64 + P, 64 + P + A
+OFF = MC + K
+SO, NO, TW = OFF + HO, OFF + HO + K, OFF + HO + K + N2
+TUNE = dict(sg1=[3, 3, 3], sg2=[5, 5, 5], xv=[1, 1, 1], late=[1, 1, 0], xp=4, fin=4, adr=[0, 0, 0],
+            cases=[(1.0, 1.56, 3.8, 220.0, 1.0, 0.4), (1.15, 1.5, 3.0, 150.0, 1.2, 0.3), (1.35, 2.3, 5.5, 200.0, 0.8, 0.3)], plan=(1.1, 1.7, 4.1, 200.0),
+            back=40, boost=[6000.0, 3000.0, 0.0], swaps=8000, heat=60.0, seed=1, tries=600, noise=2000.0, slack=300.0,
+            far=1800.0, first=2000.0, long=4000.0, xl=4800.0)
 
 F32, BF, I32, U16, X4, U8 = "float32", "bfloat16", "int32", "uint16", "float8_e4m3fn_x4", "uint8"
-SHORT = "z48 a0 ve olv old jr a1 sa so sV sW sR sH".split()
+SHORT = "cam caj slo z48 ve old jr a1 sa so sV sW sR sH".split()
 SCRATCH = {}
 
 
@@ -27,21 +29,20 @@ def _sb(name, n, dtype):
 
 for _n, _w, _d in [
     ("tgi", 32, I32), ("adi", 48, I32), ("tg16", 32, U16), ("ad16", 48, U16),
-    ("mm", 4 * (MC + K), BF), ("uu", 512, BF), ("vv", 512, BF),
+    ("mm", 4 * OFF, BF), ("uu", 512, BF), ("vv", 512, BF),
     ("qu", 128, X4), ("su", 128, U8), ("qu2", 128, X4), ("su2", 128, U8), ("qv", 128, X4), ("sv", 128, U8),
     ("qw", 512, X4), ("sw", 512, U8), ("qx", 512, X4), ("sx", 512, U8), ("qz", 256, X4), ("sz", 256, U8),
-    ("eb", 2048, BF), ("qe", 512, X4), ("se", 512, U8), ("zt", 512, BF),
-    ("lq", LW, X4), ("ls", LW, U8), ("ft", 512, BF), ("zz", 4 * A, BF), ("hv", 4 * K, BF),
-    ("pint", 8, I32), ("io16", 16, F32), ("io1", MC, F32), ("sc", 16, F32), ("kk", 4, F32), ("q4", 4, F32),
-    ("pd", 24, F32), ("pa", 24, F32), ("pb", 24, F32), ("px", 24, F32), ("pcl", 16, F32),
-    ("l16", 16, U16), ("l4", 16, U16), ("ul", 12, U16), ("ol", 12, U16),
-    ("c16x", A, F32), ("c4x", A, F32), ("c4m", A, F32), ("cl", N2, F32), ("cr", N2, F32),
-    ("ramp0", N2, BF), ("cap", A, BF), ("ones", P, BF), ("stp", 144, BF),
-    ("rows", len(SHORT) * K, F32), ("at", MC + K, F32), ("tgr", NO, F32), ("tb", TW, F32),
-    ("adr", R * AX, F32), ("pre", A, F32), ("sP", A, F32), ("pre16", R * 16, U16),
-    ("flg", A, BF), ("cum", AX, BF), ("jx", 3 * AX, BF), ("jc", 3 * AX // 2, F32), ("jf", 8, F32), ("j16", 4 * R, U16),
-    ("src1", AX, F32), ("sA", A, F32), ("src4", 64, U16), ("sE", P, F32), ("e4", 128, U16), ("hv4", 12, U16), ("a16", 4, U16),
-    ("hm", P, F32), ("k0", P, F32), ("k1", P, F32),
+    ("eb", 528, BF), ("qe", 512, X4), ("se", 512, U8),
+    ("ft", 512, BF), ("zz", 4 * A, BF), ("hv", 4 * K, BF),
+    ("rqa", 16, U16), ("rq4", 64, U16), ("fa", 4 * A, BF), ("qa", A, X4), ("sa", A, U8), ("la", A, X4), ("lb", A, U8),
+    ("pint", 8, I32), ("sc", 24, F32), ("sb", 16, BF), ("q4", 4, F32), ("ul", 12, U16), ("ol", 12, U16),
+    ("c16", A, F32), ("c4", A, F32), ("c4u", A, F32), ("c4m", A, F32), ("cl", N2, F32), ("cr", N2, F32),
+    ("r16", A, BF), ("r4", A, BF), ("ones", HO, BF),
+    ("rows", len(SHORT) * K, F32), ("at", OFF, F32), ("tgr", HO, F32), ("tb", TW, F32), ("idu", HO + K, F32), ("ju", AX, F32), ("jv", AX, F32),
+    ("adr", R * AX, F32), ("src", R * AX, F32), ("pre", A, F32), ("sP", A, F32), ("pre16", R * 16, U16),
+    ("flg", A, BF), ("cum", A, BF), ("jx", 3 * A, BF), ("jc", 3 * A // 2, BF), ("jf", 8, F32), ("j16", 4 * R, U16),
+    ("sA", A, F32), ("src4", 64, U16), ("sE", P, F32), ("e4", 128, U16), ("hv4", 12, U16), ("a16", 4, U16),
+    ("ys", P, F32), ("k0", P, F32), ("k1", P, F32),
     ("ra1", N1, F32), ("ow1", N1, F32), ("dg1", N1, BF), ("dc1", N1, BF), ("mx1", S1 * N1, BF), ("cm1", S1 * 64, BF),
     ("rf1", 3 * S1, F32), ("rk1", S1, U16),
     ("fl", N1, BF), ("cm", N1, BF), ("mx3", 3 * N1, BF), ("c4p", 16, U16),
@@ -51,13 +52,14 @@ for _n, _w, _d in [
 ]:
     _sb(_n, _w, _d)
 for _t in range(R):
-    _sb("ee%d" % _t, TW, F32)
+    _sb("ee%d" % _t, NO, F32)
+for _t in range(L):
     _sb("req%d" % _t, 12, U16)
     _sb("rql%d" % _t, 12, U16)
-    _sb("qf%d" % _t, 128, X4)
-    _sb("sf%d" % _t, 128, U8)
+    _sb("qf%d" % _t, K + 128, X4)
+    _sb("sf%d" % _t, K + 128, U8)
 for _t in range(R + 1):
-    _sb("xb%d" % _t, 4 * XW, BF)
+    _sb("xb%d" % _t, 4 * (XW + A * (_t == L)), BF)
 SCRATCH["ps"] = ("psum", [128, 4096], F32)
 
 SEMAPHORES = (["cv", "ca", "ct", "cg", "sent"] + ["d%d" % i for i in range(24)]
@@ -92,17 +94,21 @@ def arrange(ops, first):
         for j in sorted(pred[i]):
             succ[j].append(i)
     pred = [sorted(p) for p in pred]
-    wake, cases = TUNE["wake"], TUNE["cases"]
-    hold = [o[3] for o in ops]
+    cases, wake = TUNE["cases"], TUNE["plan"][3]
+
+    def held(c):
+        return [float(o[3][0] + 0.83 * (o[3][1] * c[0] + o[3][2] * c[1] + o[3][3] * c[2])) for o in ops]
+    hold = held(TUNE["plan"])
     lat = [o[4] for o in ops]
-    tail = [o[3] + o[4] + wake for o in ops]
+    tail = [hold[i] + lat[i] + wake for i in range(n)]
     queue = [o[0] for o in ops]
-    costs = [([hold[i] * f for i in range(n)], [lat[i] * far + w for i in range(n)]) for f, w, far, _ in cases]
+    qn = ["vatgs".index(q) for q in queue]
+    costs = [(held(c), [lat[i] * c[4] + c[3] for i in range(n)]) for c in cases]
 
     def lay(key, back):
         before, after = (succ, pred) if back else (pred, succ)
         left = [len(p) for p in before]
-        at, busy, low, seen = [0.0] * n, {q: [] for q in queue}, [0.0] * n, [False] * n
+        at, busy, low, seen = [0.0] * n, [[] for _ in range(5)], [0.0] * n, [False] * n
         for i0 in sorted(range(n), key=lambda i: key[i]):
             seen[i0] = True
             if left[i0]:
@@ -112,7 +118,7 @@ def arrange(ops, first):
                 i = todo.pop()
                 h = hold[i]
                 t = low[i] + (lat[i] if back else 0.0)
-                b = busy[queue[i]]
+                b = busy[qn[i]]
                 k = len(b)
                 while k and b[k - 1][1] > t:
                     k -= 1
@@ -131,23 +137,36 @@ def arrange(ops, first):
                         todo.append(j)
         return at
 
-    def play(seq):
+    def play(seq, a, old):
         total, ends, whys = 0.0, [], []
-        for (hf, lf), case in zip(costs, cases):
-            end, why, free, prev = [0.0] * n, [-1] * n, {q: 0.0 for q in "vatgs"}, {q: -1 for q in "vatgs"}
-            for i in seq:
-                q = queue[i]
+        last = [-1] * 5
+        k, found = a - 1, 0
+        while k >= 0 and found < 5:
+            if last[qn[seq[k]]] < 0:
+                last[qn[seq[k]]] = seq[k]
+                found += 1
+            k -= 1
+        rest = seq[a:]
+        for c, (hf, lf) in enumerate(costs):
+            end, why, prev = old[1][c][:], old[2][c][:], last[:]
+            free = [end[j] - lf[j] if j >= 0 else 0.0 for j in last]
+            for i in rest:
+                q = qn[i]
                 t, y = free[q], -2 - prev[q]
                 for j in pred[i]:
                     if end[j] > t:
                         t, y = end[j], j
                 t += hf[i]
-                free[q], prev[q], why[i], end[i] = t, i, y, t + lf[i]
-            total += case[3] * max(end)
+                free[q] = t
+                prev[q] = i
+                why[i] = y
+                end[i] = t + lf[i]
+            total += cases[c][5] * max(end)
             ends.append(end)
             whys.append(why)
         return total, ends, whys
 
+    blank = (0.0, [[0.0] * n for _ in cases], [[-1] * n for _ in cases])
     way = [0.0] * n
     for i in range(n - 1, -1, -1):
         way[i] = hold[i] + lat[i] + max([way[j] + wake for j in succ[i]], default=0.0)
@@ -155,7 +174,7 @@ def arrange(ops, first):
     cur, best, key = None, None, [-w for w in way]
     for t in range(R):
         todo = [i for i in range(n) if ops[i][2] and ops[i][2][0].startswith("H%d_" % t)]
-        stop = min(i for i in range(n) if "j16_%da" % t in ops[i][2] or "j16_%db" % t in ops[i][2]) - TUNE["back"]
+        stop = min(i for i in range(n) if "j16_%d" % t in ops[i][2]) - TUNE["back"]
         hot = set()
         while todo:
             i = todo.pop()
@@ -175,7 +194,7 @@ def arrange(ops, first):
         for turn in range(2):
             at = lay([-1e9 + i if i < first else key[i] for i in range(n)], False)
             if turn or not it:
-                span = play(sorted(range(n), key=lambda i: (at[i], i)))[0]
+                span = play(sorted(range(n), key=lambda i: (at[i], i)), 0, blank)[0]
                 if best is None or span <= best[0]:
                     best = (span, at)
                 if cur is None or span <= cur[0] + TUNE["slack"] * (1 - it / TUNE["tries"]) * rng.random():
@@ -184,12 +203,12 @@ def arrange(ops, first):
                 ab = lay([-(at[i] + tail[i]) for i in range(n)], True)
                 key = [-(ab[i] + hold[i]) for i in range(n)]
     seq = sorted(range(n), key=lambda i: (best[1][i], i))
-    now = play(seq)
+    now = play(seq, 0, blank)
     top = (now[0], seq)
     for it in range(TUNE["swaps"]):
         c = int(rng.integers(len(cases)))
         end, why = now[1][c], now[2][c]
-        i, arcs = max(range(n), key=lambda i: end[i]), []
+        i, arcs = end.index(max(end)), []
         while i >= 0:
             if why[i] <= -2:
                 arcs.append((-2 - why[i], i))
@@ -221,7 +240,7 @@ def arrange(ops, first):
             else:
                 rest.append(j)
         new = seq[:a] + (moved[::-1] + rest[::-1] if ahead else rest + moved) + seq[b + 1:]
-        trial = play(new)
+        trial = play(new, a, now)
         if trial[0] <= now[0] + TUNE["heat"] * (1 - it / TUNE["swaps"]) * rng.random() ** 2:
             seq, now = new, trial
             if now[0] < top[0]:
@@ -240,28 +259,28 @@ def rank_program(g, core, T, topo):
     Q = {"v": g.vector, "a": g.scalar, "t": g.tensor, "g": g, "s": g.sync}
     OWN = {"v": "cv", "a": "ca", "t": "ct", "g": "cg"}
     ops, alias = [], {k: ["%s_%d" % (k, b) for b in range(4)] for k in ("ra2", "k2", "plr")}
-    cyc = 0.83 * TUNE["f"]
+    alias.update(ra1=["ra1_0", "ra1_1"], ow1=["ow1_0", "ow1_1"])
 
     def add(q, rd, wr, hold, lat, fn):
         ops.append((q, rd.split(), wr.split(), hold, lat, fn))
 
-    def plain(w):
-        return max(64, w) * cyc
+    def plain(w, fixed=0):
+        return (fixed, max(64, w), 0, 0)
 
     def took(w):
-        return 60 + 1.56 * w * cyc
+        return (60, 0, w, 0)
 
     def put(w):
-        return 50 + 3.8 * w * cyc
+        return (50, 0, 0, w)
 
     def op(q, rd, wr, hold, fn):
         add(q, rd, wr, hold, 0.0, ("op", fn))
 
     def dma(q, rd, wr, out, in_, lat=1500.0):
-        add(q, rd, wr, 60.0, lat, ("dma", out, in_))
+        add(q, rd, wr, (60, 0, 0, 0), lat, ("dma", out, in_))
 
-    def send(dst, rd, wr, out, in_, sem):
-        add("g", rd, wr, 300.0, TUNE["far"], ("send", dst, out, in_, sem))
+    def send(dst, rd, wr, out, in_, sem, more=0.0, lat=TUNE["far"]):
+        add("g", rd, wr, (300 + more, 0, 0, 0), lat, ("send", dst, out, in_, sem))
 
     V, S = g.vector, g.scalar
 
@@ -277,32 +296,37 @@ def rank_program(g, core, T, topo):
     def cp(c, rd, wr, out, in_):
         op("v", rd, wr, c, lambda: V.tensor_copy(out, in_))
 
-    def ms(c, wr, out, x):
-        op("v", "", wr, c, lambda: V.memset(out, x))
-
     def scan(c, rd, wr, out, d0, d1, init, op0, op1):
         op("v", rd, wr, c, lambda: V.tensor_tensor_scan(out, d0, d1, init, op0, op1))
 
-    def act(c, rd, wr, out, in_, func=AF.Copy, **kw):
-        op("a", rd, wr, c + (20 if "accum_out" in kw else 0), lambda: S.activation(out, in_, func, **kw))
+    def act(c, rd, wr, out, in_, func=AF.Identity, **kw):
+        op("a", rd, wr, (c[0] + (20 if "accum_out" in kw else 0),) + c[1:], lambda: S.activation(out, in_, func, **kw))
 
     def move(on_v, c, rd, wr, out, in_):
-        (cp if on_v else act)(c, rd, wr, out, in_)
+        if on_v:
+            cp(c, rd, wr, out, in_)
+        else:
+            act(c, rd, wr, out, in_, AF.Copy)
 
     def quant(w, rd, wr, q, s, in_):
-        op("v", rd, wr, (12 + 0.88 * w) * TUNE["f"], lambda: V.quantize_mx(q, s, in_))
+        op("v", rd, wr, (0, 14 + 1.06 * w, 0, 0), lambda: V.quantize_mx(q, s, in_))
 
     def mm(rd, bank, w, lq, ls, rq, rs):
-        op("t", rd, "ps%d" % bank, 60 + 0.7 * w, lambda: g.tensor.matmul_mx(T.ps[:, 512 * bank:512 * bank + w], lq, ls, rq, rs, True, True))
+        op("t", rd, "ps%d" % bank, (60 + 0.7 * w, 0, 0, 0), lambda: g.tensor.matmul_mx(T.ps[:, 512 * bank:512 * bank + w], lq, ls, rq, rs, True, True))
 
     def iota(w, wr, out, pattern, base):
-        op("g", "", wr, 130 + 2 * w * cyc, lambda: g.iota(out, pattern, base, 0, allow_small_or_imprecise_dtypes=True))
+        op("g", "", wr, (130, 2 * w, 0, 0), lambda: g.iota(out, pattern, base, 0, allow_small_or_imprecise_dtypes=True))
+
+    def count(wr, out, w, base):
+        iota(w, wr, out, [[1, w]], base)
 
     one = plain(1)
 
     def col(i):
         return T.sc[:, i:i + 1]
-    LANE, CLS, T0, TM4, S0, F16, F4 = range(7)
+    LANE, T0, CLS4, B16, BF1, BF2, B4, L16, L4, CA, CB, CE, L21, S0, KM = range(15)
+    S2X, K21, BASE = T.sb[:, 0:1], 2, 6
+    MID = A / 2 - K
 
     def short(name):
         o = K * SHORT.index(name)
@@ -310,152 +334,161 @@ def rank_program(g, core, T, topo):
 
     def held(rd, tmp, key, c, row, w, o):
         buf, o = (T.rows, K * SHORT.index(tmp)) if tmp in SHORT else (T[tmp], o)
-        scan(plain(w), rd, tmp + key, buf[:, o:o + w], c[:, 0:w], row, 0.0, AL.mult, AL.max)
+        scan(plain(w), rd, tmp + key, buf[:, o:o + w], c[:, 0:w], row, 0.0, AL.add, AL.max)
         return buf, o
 
-    def lane16(rd, tmp, wr, out, row, w):
-        buf, o = held(rd + " c16x", tmp, "", T.c16x, row, w, 0)
-        ts(one, tmp + " f16", wr, out, buf[:, o + 15:o + w:16], col(F16), AL.mult, -1.0, AL.add)
+    def lane16(rd, tmp, wr, out, row, w, less=0.0):
+        buf, o = held(rd + " c16", tmp, "", T.c16, row, w, 0)
+        ts(one, tmp + " l16", wr, out, buf[:, o + 15:o + w:16], col(L16), AL.subtract, -less, AL.add)
 
-    def lane4(rd, tmp, wr, out, row, w, o=0, key=""):
-        buf, o = held(rd + " c4x", tmp, key, T.c4x, row, w, o)
-        ts(plain(w // 4), tmp + key + " f4 tm4", wr, out, buf[:, o + 3:o + w:4], col(F4), AL.mult, col(TM4), AL.add)
+    def lane4(rd, tmp, wr, out, row, w, kind, o=0, key=""):
+        c, f = ("c4u", 4.0 / UP) if kind == CE else ("c4", 4.0)
+        buf, o = held(rd + " " + c, tmp, key, T[c], row, w, o)
+        ts(plain(w // 4), tmp + key + " cc%d" % kind, wr, out, buf[:, o + 3:o + w:4], f, AL.mult, col(kind), AL.subtract)
 
     dma("s", "", "tgi", T.tgi[:], T.tg[:])
     dma("a", "", "adi", T.adi[:], T.ad[:])
     dma("s", "", "uu", T.uu[:], T.u[:], 2200.0)
-    dma("s", "", "X0_0 X0_1", T.xb0[:, 4 * XO:4 * HO], T.x[:], 4000.0)
+    dma("s", "", "X0_0 X0_1", T.xb0[:, 4 * XO:4 * HO], T.x[:], TUNE["xl"])
     dma("s", "", "mm", T.mm[:, 0:4 * MC], T.m[:], 8000.0)
     dma("s", "", "qw", T.qw[:].bitcast(dt.uint8), T.wc[:], 9000.0)
     dma("s", "", "sw", T.sw[:], T.ws[:], 9500.0)
     dma("s", "", "vv", T.vv[:], T.v[:], 10000.0)
     nload = len(ops)
 
-    pidx = T.pint[:, 4:5]
-    op("g", "", "pidx", 140, lambda: g.iota(pidx, [[0, 1]], 0, 1))
-    iota(16, "io16", T.io16[:], [[1, 16]], 1)
-    iota(HO, "ioa", T.io1[:, 0:HO], [[1, HO]], 1)
-    ms(plain(256), "zt", T.zt[:], 0.0)
-    ms(plain(256), "ones", T.ones[:], 1.0)
-    act(plain(MC - HO), "ioa", "iob", T.io1[:, HO:MC], T.io1[:, 0:MC - HO], AF.Identity, bias=float(HO))
-    scan(plain(P), "ones", "at0", T.at[:, 0:P], T.ones[:], T.ones[:], float(DO), AL.add, AL.max)
-    scan(plain(P), "ones", "at1", T.at[:, P:MC], T.ones[:], T.ones[:], float(DO + P), AL.add, AL.max)
-    act(one, "ones", "at2", T.at[:, MC:MC + K], T.ones[:, 0:K])
-    act(plain(4 * K), "zt", "mmz", T.mm[:, 4 * MC:4 * (MC + K)], T.zt[:, 0:4 * K])
-    act(one, "ones", "stp", T.stp[:, 0:K + 1], T.ones[:, 0:K + 1])
-    act(plain(96), "zt", "stq", T.stp[:, K + 1:144], T.zt[:, K + 1:144])
-    act(plain(K + N2), "ones", "tbn", T.tb[:, HO:DO], T.ones[:, 0:K + N2])
-    act(plain(P), "ones", "tbz0", T.tb[:, DO:DO + P], T.ones[:], AF.Identity, scale=K + 1.0)
-    act(plain(P), "ones", "tbz1", T.tb[:, DO + P:TW], T.ones[:], AF.Identity, scale=K + 1.0)
-    act(one, "ones", "z48", short("z48"), T.ones[:, 0:K], AF.Identity, scale=K + 1.0)
-    act(plain(A), "ones", "cap", T.cap[:], T.ones[:, 0:A], AF.Identity, scale=K + 1.0)
-    ts(one, "io16", "q4", T.q4[:], T.io16[:, 0:4], 0.5, AL.mult, N1 - 0.5, AL.add)
+    pidx, ones, io = T.pint[:, 4:5], T.ones, T.tb
+    op("g", "", "pidx", (140, 0, 0, 0), lambda: g.iota(pidx, [[0, 1]], 0, 1))
+    op("v", "", "ones", plain(HO // 2), lambda: V.memset(ones[:], 1.0))
+    hf = OFF // 2
+    for i in range(2):
+        scan(plain(hf), "ones", "at%d" % i, T.at[:, hf * i:hf * i + hf], ones[:, 0:hf], ones[:, 0:hf], hf * i - 1.0, AL.add, AL.mult)
+    scan(plain(HO), "ones", "tbp", T.tb[:, OFF:SO], ones[:], ones[:], OFF - 1.0, AL.add, AL.mult)
+    iota(A, "r16", T.r16[:], [[0, A // 16], [1, 16]], 0)
+    iota(A, "r4", T.r4[:], [[0, A // 4], [1, 4]], 0)
+    count("ioa", io[:, 0:AX], AX, 0)
+    count("iob", io[:, AX:OFF], OFF - AX, AX)
+    count("tbn", T.tb[:, SO:NO], K, OFF + CO)
+    count("cam", short("cam"), K, OFF + CO)
+    count("slo", short("slo"), K, SO)
+    count("tgra", T.tgr[:, 0:XO], XO, MC - CO)
     ts(one, "pidx", "lanei", T.pint[:, 0:1], pidx, 15, AL.bitwise_and)
     ts(one, "pidx", "ti", T.pint[:, 1:2], pidx, 3, AL.bitwise_and)
-    ts(one, "pidx", "clsi", T.pint[:, 2:3], pidx, 12, AL.bitwise_and)
-    cp(one, "lanei", "lane", col(LANE), T.pint[:, 0:1])
-    cp(one, "ti", "t0", col(T0), T.pint[:, 1:2])
-    ts(one, "clsi", "cls", col(CLS), T.pint[:, 2:3], 0.25, AL.mult)
-    ts(one, "lanei", "f16", col(F16), T.pint[:, 0:1], -14.0, AL.add, 1.0 / LIFT, AL.max)
-    ts(one, "clsi", "f4", col(F4), T.pint[:, 2:3], -8.0, AL.add, 4.0 / LIFT, AL.max)
-    ts(one, "ti", "tm4", col(TM4), T.pint[:, 1:2], -4.0, AL.add)
-    ts(one, "io16 lane", "l16", T.l16[:], T.io16[:], 0.0, AL.mult, col(LANE), AL.add)
-    ts(one, "io16 t0", "l4", T.l4[:], T.io16[:], 0.0, AL.mult, col(T0), AL.add)
-    ts(one, "io16 lane", "pd0", T.pd[:, 0:16], T.io16[:], col(LANE), AL.subtract)
-    ts(one, "io16 cls", "pd1", T.pd[:, 16:20], T.io16[:, 0:4], col(CLS), AL.subtract)
-    ts(one, "pd0 pd1", "pa", T.pa[:, 0:20], T.pd[:, 0:20], 1.0, AL.is_gt)
-    ts(one, "pd0 pd1", "pb", T.pb[:, 0:20], T.pd[:, 0:20], 2.0, AL.is_equal, LIFT, AL.mult)
-    tt(one, "pa pb", "px", T.px[:, 0:20], T.pa[:, 0:20], T.pb[:, 0:20], AL.max)
-    act(took(A), "px l16", "c16x", T.c16x[:], T.px[:, 0:16].indirect(T.l16[:]))
-    act(took(A), "px l4", "c4x", T.c4x[:], T.px[:, 16:20].indirect(T.l4[:]))
-    ts(one, "io16", "ul", T.ul[:], T.io16[:, 0:12], -1.0, AL.add, 16.0, AL.mult)
-    ts(one, "ul", "ol", T.ol[:], T.ul[:], 15.0, AL.add)
-    ts(one, "ul lane", "kk", T.kk[:, 0:3], T.ul[:, 0:3], col(LANE), AL.add, 0.5, AL.add)
-    ts(one, "pa", "pcl", T.pcl[:], T.pa[:, 0:16], -0.5, AL.add, 2.0 * BIG, AL.mult)
-    act(plain(A), "ones", "c4m", T.c4m[:], T.ones[:, 0:A], AF.Identity, scale=-BIG)
-    act(one, "ones", "c4m", T.c4m[:, 0:A:4], T.ones[:, 0:A // 4], AF.Identity, scale=BIG)
-    act(took(N2), "pcl l16", "cl", T.cl[:], T.pcl[:].indirect(T.l16[:, 0:S2]))
-    act(plain(N2), "cl", "cr", T.cr[:], T.cl[:], AF.Identity, scale=-1.0)
-    iota(N2, "ramp0", T.ramp0[:], [[0, S2], [1, 16]], 0)
-    act(plain(512 - 4 * K), "zt", "ftz", T.ft[:, 4 * K:512], T.zt[:, 4 * K:512])
+    cp(one, "lanei ti", "lane", T.sc[:, 0:2], T.pint[:, 0:2])
+    act(one, "lane", "cls4", col(CLS4), col(T0), scale=-1.0, bias=col(LANE))
+    act(one, "lane", "b16", col(B16), col(LANE), scale=-LIFT, bias=-0.5 * LIFT)
+    act(one, "lane", "bf1", col(BF1), col(LANE), scale=-FAR, bias=-0.5 * FAR)
+    act(one, "lane", "bf2", col(BF2), col(LANE), scale=FAR, bias=0.5 * FAR)
+    act(one, "cls4", "b4", col(B4), col(CLS4), scale=-LIFT / 4, bias=-0.5 * LIFT)
+    root = (LIFT / 2) ** 0.5
+    act(one, "lane", "l16", col(L16), col(LANE), AF.Square, scale=-root, bias=15 * root)
+    act(one, "cls4", "l4", col(L4), col(CLS4), AF.Square, scale=-root / 2, bias=6 * root)
+    act(one, "l4 lane", "cc%d" % CA, col(CA), col(T0), scale=-1.0, bias=col(L4))
+    act(one, "cc%d" % CA, "cc%d" % CB, col(CB), col(CA), bias=4.0 * OFF)
+    act(one, "cc%d" % CA, "cc%d" % CE, col(CE), col(CA), bias=2.0 - 4 * HO)
+    act(one, "lane", "l21", col(L21), col(LANE), scale=2.0, bias=1.0)
+    act(one, "ioa l21", "k21", T.sb[:, K21:K21 + 3], io[:, 0:K:16], scale=2.0, bias=col(L21))
+    act(one, "k21", "km", T.sc[:, KM:KM + 3], T.sb[:, K21:K21 + 3], scale=0.5, bias=-MID - 0.5)
+    act(plain(A), "r16 b16", "c16", T.c16[:], T.r16[:], scale=LIFT, bias=col(B16))
+    act(one, "ones", "c16", T.c16[:, 0:A:16], ones[:, 0:A // 16], scale=-512 * LIFT)
+    act(plain(A), "r4 b4", "c4", T.c4[:], T.r4[:], scale=LIFT, bias=col(B4))
+    act(one, "ones", "c4", T.c4[:, 0:A:4], ones[:, 0:A // 4], scale=-512 * LIFT)
+    act(plain(A), "c4", "c4u", T.c4u[:], T.c4[:], scale=UP)
+    act(plain(A), "r4", "c4m", T.c4m[:], T.r4[:], scale=-FAR, bias=0.5 * FAR)
+    act(plain(N2), "r16 bf1", "cl", T.cl[:], T.r16[:, 0:N2], scale=FAR, bias=col(BF1))
+    act(plain(N2), "r16 bf2", "cr", T.cr[:], T.r16[:, 0:N2], scale=-FAR, bias=col(BF2))
+    act(one, "r4", "q4", T.q4[:], T.r4[:, 0:4], scale=0.5, bias=float(N1))
+    act(plain(AX), "ioa", "ju", T.ju[:], io[:, 0:AX], scale=UP, bias=(0.5 - K) * UP)
+    act(plain(AX), "ioa", "jv", T.jv[:], io[:, 0:AX], scale=UP, bias=(0.5 - K + A) * UP)
+    act(plain(HO), "tbp", "idu", T.idu[:, 0:HO], T.tb[:, OFF:SO], scale=UP, bias=(0.5 - SO) * UP)
+    act(one, "ones", "idn", T.idu[:, HO:HO + K], ones[:, 0:K], scale=-1024 * UP)
+    act(plain(P), "tbp", "ee0", T.ee0[:, OFF + XO:SO], T.tb[:, OFF + XO:SO], scale=UP, bias=(0.5 - SO) * UP)
+    act(plain(512 - 4 * K), "ones", "ftz", T.ft[:, 4 * K:512], ones[:, 4 * K:512], scale=0.0)
+    act(plain(4 * K), "ones", "mmz", T.mm[:, 4 * MC:4 * OFF], ones[:, 0:4 * K], scale=0.0)
+    ts(one, "ioa", "ul", T.ul[:], io[:, 0:12], 16.0, AL.mult)
+    ts(one, "ioa", "ol", T.ol[:], io[:, 0:12], 16.0, AL.mult, 15.0, AL.add)
     for t in range(R):
-        act(one, "zt", "Z%d" % t, T["xb%d" % t][:, 4 * K:4 * XO], T.zt[:, 0:4 * (XO - K)])
-        iota(P, "ee%d" % t, T["ee%d" % t][:, XO:HO], [[1, P]], XO + 1)
-        act(one, "zt", "en%d" % t, T["ee%d" % t][:, HO:NO], T.zt[:, 0:K])
-        act(one, "ioa", "adx%d" % t, T.adr[:, AX * t:AX * t + K], T.io1[:, 0:K], AF.Identity, bias=float(MC))
+        zw = 4 * (XO if t == L else CO)
+        iota(zw, "Z%d" % t, T["xb%d" % t][:, 0:zw], [[0, zw]], 0)
+        if t:
+            op("g", "idu idn", "ee%d en%d" % (t, t), (170, 2 * (P + K), 0, 0),
+               lambda t=t: g.affine_select(T["ee%d" % t][:, OFF + XO:NO], T.idu[:, XO:HO + K], [[0, P + K]], AL.is_ge, 0.0, 0, 0))
+        count("srx%d" % t, T.src[:, AX * t:AX * t + K], K, MC)
+        if TUNE["adr"][t]:
+            count("adx%d" % t, T.adr[:, AX * t:AX * t + K], K, MC)
+    if max(TUNE["adr"]):
+        iota(K, "z48", short("z48"), [[0, K]], 0)
+    op("g", "ones", "eb", (170, 2 * 528, 0, 0), lambda: g.affine_select(T.eb[:], ones[:, 0:528], [[-1, 528]], AL.is_equal, 0.0, 3, 4))
     for b in range(4):
-        op("g", "zt", "eb%d" % b, 170 + 1024 * cyc,
-           lambda b=b: g.affine_select(T.eb[:, 512 * b:512 * b + 512], T.zt[:], [[-1, 512]], AL.not_equal, 1.0, b, 4))
-    quant(512, "eb0 eb1 eb2 eb3", "qe", T.qe[:], T.se[:], T.eb[:])
-    quant(128, "zt", "lz", T.lq[:, K:K + 128], T.ls[:, K:K + 128], T.zt[:])
+        quant(128, "eb", "qe%d" % b, T.qe[:, 128 * b:128 * b + 128], T.se[:, 128 * b:128 * b + 128], T.eb[:, 3 - b:515 - b])
     quant(128, "uu", "qu", T.qu[:], T.su[:], T.uu[:])
     cp(took(128), "qu ul", "qu2", T.qu2[:].bitcast(dt.uint32), T.qu[:].bitcast(dt.uint32).indirect(T.ul[:, 0:8]))
-    act(took(128), "qu ul", "su2", T.su2[:], T.su[:].indirect(T.ul[:, 0:8]))
+    act(took(128), "qu ul", "su2", T.su2[:], T.su[:].indirect(T.ul[:, 0:8]), AF.Copy)
     quant(128, "vv", "qv", T.qv[:], T.sv[:], T.vv[:])
 
     cp(one, "tgi", "tg16", T.tg16[:], T.tgi[:])
     cp(one, "adi", "ad16", T.ad16[:], T.adi[:])
-    cp(put(P), "ioa tg16", "at at0 at1 at2", T.at[:].indirect(T.tg16[:]), T.io1[:, XO:HO])
-    act(took(P), "ioa iob tg16", "tgr", T.tgr[:, XO:HO], T.io1[:].indirect(T.tg16[:]), AF.Identity, bias=-1.0)
-    act(one, "ioa", "tgra", T.tgr[:, 0:XO], T.io1[:, 0:XO])
-    act(one, "ioa", "tgrb", T.tgr[:, HO:NO], T.io1[:, 0:K], AF.Identity, bias=MC - 1.0)
+    send(nxt, "ad16", "first rql%d" % L, T.rqa[:], T.ad16[:, 16 * L:16 * L + 16], "rq%d" % L, TUNE["first"])
+    cp(put(P), "tbp tg16", "at at0 at1", T.at[:].indirect(T.tg16[:]), T.tb[:, OFF + XO:SO])
+    act(took(P), "ioa iob tg16", "tgr", T.tgr[:, XO:HO], io[:, 0:MC].indirect(T.tg16[:]))
     for t in range(R):
-        act(took(A), "ioa iob ad16", "adr%d" % t, T.adr[:, AX * t + K:AX * t + AX], T.io1[:].indirect(T.ad16[:, 16 * t:16 * t + 16]))
-    act(plain(HO), "ioa", "tbp", T.tb[:, 0:HO], T.io1[:, 0:HO])
-    tbk = "tbp tbn tbz0 tbz1"
+        if TUNE["adr"][t]:
+            act(took(A), "ioa iob ad16", "adr%d" % t, T.adr[:, AX * t + K:AX * t + AX], io[:, 0:MC].indirect(T.ad16[:, 16 * t:16 * t + 16]))
 
     def ahead(t):
         p16 = T.pre16[:, 16 * t:16 * t + 16]
-        act(took(A), "at ad16", "pre", T.pre[:], T.at[:].indirect(T.ad16[:, 16 * t:16 * t + 16]))
-        lane16("pre", "sP", "pre16_%d" % t, p16, T.pre[:], A)
-        cp(put(A), "iob pre16_%d" % t, "ee%d en%d" % (t, t), T["ee%d" % t][:].indirect(p16), T.io1[:, HO:HO + A])
+        pre, pk = (T.pre[:], "pre") if t else (T.src[:, K:AX], "src0")
+        act(took(A), "at ad16", pk, pre, T.at[:].indirect(T.ad16[:, 16 * t:16 * t + 16]))
+        lane16(pk, "sP", "pre16_%d" % t, p16, pre, A)
+        jn = "jv" if t == L else "ju"
+        cp(put(A), jn + " pre16_%d" % t, "ee%d en%d" % (t, t), T["ee%d" % t][:].indirect(p16), T[jn][:, K:AX])
 
     def lists(t):
-        p16, j16 = T.pre16[:, 16 * t:16 * t + 16], T.j16[:, 4 * t:4 * t + 3]
-        jk, tk = "j16_%d" % t, tbk + " pre16_%d" % t
-        act(took(A), tk, "src1", T.src1[:, K:AX], T.tb[:].indirect(p16))
-        nm, s0 = T.jf[:, 3:4], col(S0)
-        if t == 0:
-            act(plain(A), "pre", "sg0", T.jx[:, 0:A], T.pre[:], AF.Sign, bias=-DO - 0.5)
-            act(plain(A), "sg0", "flg nm", T.flg[:], T.jx[:, 0:A], AF.Relu, accum_out=nm)
-        else:
-            act(took(A), tk, "flg nm", T.flg[:], T.tb[:].indirect(p16), AF.Relu, scale=-1.0, bias=K + 2.0, accum_out=nm)
-        act(one, "nm", "s0", s0, nm, AF.Relu, scale=-1.0, bias=float(K))
-        scan(plain(A // 2), "flg s0 cap", "cum", T.cum[:, K:AX], T.flg[:], T.cap[:], s0, AL.add, AL.min)
-        ts(one, "ioa s0", "cumx", T.cum[:, 0:K], T.io1[:, 0:K], s0, AL.min)
-        a, hx = 3 - TUNE["jv"][t], AX // 2
+        j16, jk = T.j16[:, 4 * t:4 * t + 3], "j16_%d" % t
+        src, sk, acc = T.src[:, AX * t:AX * t + AX], "src%d srx%d" % (t, t), T.jf[:, 3:4]
+        real = T.src[:, AX * t + K:AX * t + AX]
+        tk, win = ("ioa iob tbp tbn pre16_%d" % t, T.tb[:, 0:NO].indirect(T.pre16[:, 16 * t:16 * t + 16])) if t else ("at ad16", T.at[:].indirect(T.ad16[:, 0:16]))
+        act(took(A), tk, "flg acc", T.flg[:], win, AF.Sign, scale=-1.0, bias=OFF - 0.5, accum_out=acc)
+        if t:
+            act(took(A), tk, "src%d" % t, real, win)
+            count("tbn", T.tb[:, SO:NO], K, OFF + CO)
+            if t < L:
+                count("tbp", T.tb[:, OFF:SO], HO, OFF)
+        act(one, "acc", "s2", S2X, acc, AF.Relu, scale=-1.0, bias=-2 * MID)
+        act(one, "acc", "s0", col(S0), acc, AF.Relu, scale=-0.5, bias=-MID)
+        scan(plain(A // 2), "flg ones", "cum", T.cum[:], T.flg[:], ones[:, 0:A], 0.0, AL.add, AL.add)
+        ts(one, "km s0", "base", T.sb[:, BASE:BASE + 3], T.sc[:, KM:KM + 3], col(S0), AL.subtract, -MID, AL.min)
+        hx = A // 2
         for s in range(3):
-            row, rd = T.jx[:, AX * s:AX * s + AX], "cum cumx sg0 kk"
-            if s < a:
-                act(plain(AX), rd, "jx%d jf%d" % (s, s), row, T.cum[:], AF.Sign, scale=-1.0, bias=T.kk[:, s:s + 1], accum_out=T.jf[:, s:s + 1])
-            else:
-                ts(plain(hx), rd, "jx%d" % s, row, T.cum[:], T.kk[:, s:s + 1], AL.is_lt)
-                scan(plain(hx), "jx%d" % s, "jf%d" % s, T.jc[:, hx * s:hx * s + hx], T.jx[:, AX * s:AX * s + hx], T.jx[:, AX * s + hx:AX * s + AX], 0.0, AL.add, AL.add)
-        if a:
-            ts(one, " ".join("jf%d" % s for s in range(a)), jk + "a", T.j16[:, 4 * t:4 * t + a], T.jf[:, 0:a], 0.5, AL.mult, AX / 2, AL.add)
-        if a < 3:
-            cp(one, " ".join("jf%d" % s for s in range(a, 3)), jk + "b", T.j16[:, 4 * t + a:4 * t + 3], T.jc[:, hx * a + hx - 1:3 * hx:hx])
-        jk = jk + "a " + jk + "b"
-        act(took(K), "adr%d adx%d %s" % (t, t, jk), "a1", short("a1"), T.adr[:, AX * t:AX * t + AX].indirect(j16))
-        lane4("a1", "sR", "req%d" % t, T["req%d" % t][:], short("a1"), K)
-        send(nxt, "req%d" % t, "rql%d" % t, T["rql%d" % t][:], T["req%d" % t][:], "rq%d" % t)
-        cp(put(K), "ioa " + jk, "src1", T.src1[:].indirect(j16), T.io1[:, 0:K])
-        lane4("src1", "sA", "src4", T.src4[:], T.src1[:, K:AX], A)
-        act(one, "iob", "tbn", T.tb[:, HO:NO], T.io1[:, HO:NO])
-        act(one, "a1", "a0", short("a0"), short("a1"), AF.Identity, bias=-1.0)
-        act(took(K), "ioa iob " + jk, "jr", short("jr"), T.io1[:, HO - K:HO + A].indirect(j16))
-        if t < R - 1:
+            ts(plain(hx), "cum s2 k21", "jx%d" % s, T.jx[:, A * s:A * s + A], T.cum[:], S2X, AL.add, T.sb[:, K21 + s:K21 + s + 1], AL.is_lt)
+            scan(one, "jx%d base" % s, "jc%d" % s, T.jc[:, hx * s:hx * s + hx], T.jx[:, A * s:A * s + hx], T.jx[:, A * s + hx:A * s + A],
+                 T.sb[:, BASE + s:BASE + s + 1], AL.add, AL.add)
+        ts(one, "jc0 jc1 jc2", jk, j16, T.jc[:, hx - 1:3 * hx:hx], A / 2, AL.add)
+        if TUNE["adr"][t]:
+            act(took(K), "adr%d adx%d %s" % (t, t, jk), "a1", short("a1"), T.adr[:, AX * t:AX * t + AX].indirect(j16))
+        else:
+            act(took(K), sk + " " + jk, "a1", short("a1"), src.indirect(j16))
+        ck, jn = ("caj", "jv") if t == L else ("cam", "ju")
+        if t == L:
+            act(took(K), "ioa " + jk, "caj", short("caj"), io[:, 0:AX].indirect(j16), bias=float(SO - K))
+        else:
+            lane4("a1", "sR", "req%d" % t, T["req%d" % t][:], short("a1"), K, CA)
+            send(nxt, "first req%d" % t, "rql%d" % t, T["rql%d" % t][:], T["req%d" % t][:], "rq%d" % t)
+        cp(put(K), ck + " " + jk, sk, src.indirect(j16), short(ck))
+        lane4(sk, "sA", "src4", T.src4[:], real, A, CB)
+        act(took(K), jn + " " + jk, "jr", short("jr"), T[jn][:].indirect(j16))
+        if t < L:
             lane16("a1", "sa", "a16", T.a16[:, 0:3], short("a1"), K)
-            cp(put(K), "iob a16", "at", T.at[:].indirect(T.a16[:, 0:3]), T.io1[:, HO:NO])
+            cp(put(K), "slo a16", "at", T.at[:].indirect(T.a16[:, 0:3]), short("slo"))
             ahead(t + 1)
 
-    def ranking(i, key, kk, step, w, a, b):
+    def ranking(i, key, kk, step, w, a):
         ns, h = w // 16, w // 2
         mx, cm, dc, rf, rk, own = T["mx%d" % i], T["cm%d" % i], T["dc%d" % i], T["rf%d" % i], T["rk%d" % i], T["ow%d" % i]
-        rd, dk = kk + " ow%d" % i, "dc%d" % i
+        dk = "dc%d" % i
         more, mk, less = (0.0, "", 0.0) if i == 1 else (col(S0), " s0", 1.0)
         for s in range(ns):
             c, o, d = 16 * s, own[:, 16 * s + 15:16 * s + 16], dc[:, 16 * s + 15:16 * s + 16]
+            rd = kk + (" ow2" if i == 2 else " ow1_%d" % (s // 4))
             ka, kb, o0 = "mx%da%d" % (i, s), "mx%db%d" % (i, s), w * s
             row, lrow, rrow = mx[:, o0:o0 + w], mx[:, o0:o0 + c], mx[:, o0 + c:o0 + w]
             if s < a:
@@ -467,100 +500,105 @@ def rank_program(g, core, T, topo):
             if s:
                 ts(plain(c), rd, ka, lrow, key[:, step - 1:step * c:step], o, AL.is_le)
             ts(plain(w - c), rd, kb, rrow, key[:, step * c + step - 1:step * w:step], o, AL.is_lt)
-            if s >= b:
-                scan(one, "%s %s %s" % (ka, kb, dk), "cm%d_%d" % (i, s), cm[:, h * s:h * s + h], mx[:, o0:o0 + h], mx[:, o0 + h:o0 + w], d, AL.add, AL.add)
-            else:
-                act(plain(w), dk, "%s %s rs%d_%d" % (ka, kb, i, s), row, row, AF.Identity, scale=float(w), bias=d, accum_out=rf[:, s:s + 1])
+            scan(one, "%s %s %s" % (ka, kb, dk), "cm%d_%d" % (i, s), cm[:, h * s:h * s + h], mx[:, o0:o0 + h], mx[:, o0 + h:o0 + w], d, AL.add, AL.add)
         done = []
         if a:
+            if i == 2:
+                act(one, "s0", "s1", T.jf[:, 7:8], col(S0), scale=2.0, bias=w - 2.0)
+            act(one, dk + " s1", "ru%d" % i, rf[:, 0:a], dc[:, 15:16 * a:16], scale=2.0, bias=T.jf[:, 7:8] if i == 2 else float(w))
             if a > 1:
-                tt(one, " ".join("rl%d_%d rr%d_%d" % (i, s, i, s) for s in range(1, a)), "rt%d" % i, rf[:, 2 * ns + 1:2 * ns + a], rf[:, ns + 1:ns + a], rf[:, 2 * ns + 1:2 * ns + a], AL.add)
-            ts(one, "rt%d rr%d_0" % (i, i), "ru%d" % i, rf[:, ns:ns + a], rf[:, 2 * ns:2 * ns + a], 0.5, AL.mult, w / 2 - less, AL.add)
-            if a == 1:
-                ts(one, "ru%d %s" % (i, dk) + mk, "rk%da" % i, rk[:, 0:1], rf[:, ns:ns + 1], dc[:, 15:16], AL.add, more, AL.add)
-            else:
-                tt(one, "ru%d %s" % (i, dk), "rv%d" % i, rf[:, 0:a], rf[:, ns:ns + a], dc[:, 15:16 * a:16], AL.add)
-                ts(one, "rv%d" % i + mk, "rk%da" % i, rk[:, 0:a], rf[:, 0:a], more, AL.add)
-            done.append("rk%da" % i)
-        if b > a:
-            ts(one, " ".join("rs%d_%d" % (i, s) for s in range(a, b)), "rk%db" % i, rk[:, a:b], rf[:, a:b], 1.0 / w, AL.mult)
-            done.append("rk%db" % i)
-        if b < ns:
-            ts(one, " ".join("cm%d_%d" % (i, s) for s in range(b, ns)) + mk, "rk%dc" % i, rk[:, b:ns], cm[:, h * b + h - 1:h * ns:h], more, AL.add, -less, AL.add)
+                tt(one, "ru%d " % i + " ".join("rl%d_%d" % (i, s) for s in range(1, a)), "ru%d" % i, rf[:, 1:a], rf[:, 1:a], rf[:, ns + 1:ns + a], AL.add)
+            for s in range(a):
+                ts(one, "ru%d rr%d_%d" % (i, i, s), "rk%da%d" % (i, s), rk[:, s:s + 1], rf[:, 2 * ns + s:2 * ns + s + 1], rf[:, s:s + 1], AL.add, 0.5, AL.mult)
+                done.append("rk%da%d" % (i, s))
+        if a < ns:
+            ts(one, " ".join("cm%d_%d" % (i, s) for s in range(a, ns)) + mk, "rk%dc" % i, rk[:, a:ns], cm[:, h * a + h - 1:h * ns:h], more, AL.add, -less, AL.add)
             done.append("rk%dc" % i)
         return " ".join(done)
 
     h = P // 2
-
-    def lifts(t):
-        for i in range(2):
-            act(plain(h), "ee%d" % t, "hm%d" % i, T.hm[:, h * i:h * i + h], T["ee%d" % t][:, XO + h * i:XO + h * i + h], AF.Identity, scale=UP, bias=-(HO + 0.5) * UP)
-
     ahead(0)
-    lifts(0)
     lists(0)
 
     banks = [[5, 6, 7, 0], [1, 2, 3, 4]]
     for t in range(R):
         xb, xn, e = T["xb%d" % t], T["xb%d" % (t + 1)], T["ee%d" % t]
-        ek, X, Xn = "ee%d en%d" % (t, t), "X%d_0 X%d_1" % (t, t), "X%d_0 X%d_1" % (t + 1, t + 1)
+        ek, X, Xn = "ee%d" % t, "X%d_0 X%d_1" % (t, t), "X%d_0 X%d_1" % (t + 1, t + 1)
         H = " ".join("H%d_%d" % (t, b) for b in range(8))
         came = " ".join("C%d_%d" % (t, b) for b in range(4)) + " Z%d" % t
         pool = "%s %s %s" % (H, X, came)
         late = TUNE["late"][t]
+        e0 = OFF + XO
 
         for i in range(2):
             c = slice(h * i, h * i + h)
             quant(h, "X%d_%d" % (t, i), "qx%d" % i, T.qx[:, c], T.sx[:, c], xb[:, 4 * (XO + h * i):4 * (XO + h * i + h)])
             mm("qu2 su2 qx%d" % i, 4 * i, h, T.qu2[:], T.su2[:], T.qx[:, c], T.sx[:, c])
-            tt(plain(h), "ps%d hm%d" % (4 * i, i), "k0_%d" % i, T.k0[:, c], T.ps[:, 2048 * i:2048 * i + h], T.hm[:, c], AL.max)
+            tt(plain(h), "ps%d %s" % (4 * i, ek), "k0_%d" % i, T.k0[:, c], T.ps[:, 2048 * i:2048 * i + h], e[:, e0 + h * i:e0 + h * i + h], AL.max)
             scan(plain(h), "k0_%d c4m" % i, "k1_%d" % i, T.k1[:, c], T.c4m[:], T.k0[:, c], BIG, AL.max, AL.min)
-        act(took(4 * K), "mm mmz rql%d" % t, "ft", T.ft[:, 0:4 * K], T.mm[:].indirect(T["rql%d" % t][:]))
-        qf, sf = T["qf%d" % t], T["sf%d" % t]
-        quant(128, "ft ftz", "qf%d" % t, qf[:], sf[:], T.ft[:])
-        send(prv, "qf%d" % t, "land%d" % t, T.lq[:, LAND[t]:LAND[t] + K].bitcast(dt.uint8), qf[:, 0:K].bitcast(dt.uint8), "fa%d" % t)
-        send(prv, "qf%d" % t, "land%d" % t, T.ls[:, LAND[t]:LAND[t] + K], sf[:, 0:K], "fa%d" % t)
-        tt(plain(2 * N1), "k1_0 k1_1 cl", "ra1", T.ra1[:], T.k1[:, 3:P:4], T.cl[:, 0:N1], AL.max)
-        scan(plain(N1), "ra1 cr", "ow1", T.ow1[:], T.cr[:, 0:N1], T.ra1[:], BIG, AL.max, AL.min)
+        if t < L:
+            act(took(4 * K), "mm mmz rql%d" % t, "ft", T.ft[:, 0:4 * K], T.mm[:].indirect(T["rql%d" % t][:]), AF.Copy)
+            qf, sf = T["qf%d" % t], T["sf%d" % t]
+            quant(128, "ft ftz", "qf%d" % t, qf[:, K:K + 128], sf[:, K:K + 128], T.ft[:])
+            send(prv, "qf%d" % t, "land%d" % t, qf[:, 0:K].bitcast(dt.uint8), qf[:, K:2 * K].bitcast(dt.uint8), "fa%d" % t)
+            send(prv, "qf%d" % t, "land%d" % t, sf[:, 0:K], sf[:, K:2 * K], "fa%d" % t)
+        if t == 0:
+            for b in range(4):
+                ts(one, "rql%d" % L, "rq4_%d" % b, T.rq4[:, 16 * b:16 * b + 16], T.rqa[:], 4.0, AL.mult, float(b), AL.add)
+                act(took(A), "mm mmz rq4_%d" % b, "fa%d" % b, T.fa[:, b:4 * A:4], T.mm[:].indirect(T.rq4[:, 16 * b:16 * b + 16]), AF.Copy)
+            quant(A, "fa0 fa1 fa2 fa3", "qa", T.qa[:], T.sa[:], T.fa[:])
+            send(prv, "qa land0", "land%d" % L, T.la[:].bitcast(dt.uint8), T.qa[:].bitcast(dt.uint8), "fa%d" % L, lat=TUNE["long"])
+            send(prv, "qa land0", "land%d" % L, T.lb[:], T.sa[:], "fa%d" % L, lat=TUNE["long"])
+        for i in range(2):
+            c = slice(64 * i, 64 * i + 64)
+            tt(plain(N1), "k1_%d cl" % i, "ra1_%d" % i, T.ra1[:, c], T.k1[:, h * i + 3:h * i + h:4], T.cl[:, 0:64], AL.max)
+            scan(one, "ra1_%d cr" % i, "ow1_%d" % i, T.ow1[:, c], T.cr[:, 0:64], T.ra1[:, c], BIG, AL.max, AL.min)
         tt(took(N1), "ow1 ol ra1", "dg1", T.dg1[:], T.ow1[:].indirect(T.ol[:, 0:S1]), T.ra1[:], AL.is_equal)
-        scan(one, "dg1 ramp0", "dc1", T.dc1[:], T.ramp0[:, 0:N1], T.dg1[:], 0.0, AL.min, AL.add)
-        rk = ranking(1, T.k1, "k1_0 k1_1", 4, N1, TUNE["sg1"][t], TUNE["sg1"][t] + TUNE["sm1"][t])
-        act(took(N1), "stp stq " + rk, "fl", T.fl[:], T.stp[:].indirect(T.rk1[:]))
-        scan(one, "fl", "cm", T.cm[:], T.fl[:], T.fl[:], 0.0, AL.add, AL.max)
+        scan(one, "dg1 r16", "dc1", T.dc1[:], T.r16[:, 0:N1], T.dg1[:], 0.0, AL.min, AL.add)
+        rk = ranking(1, T.k1, "k1_0 k1_1", 4, N1, TUNE["sg1"][t])
+        act(took(N1), "ioa " + rk, "fl", T.fl[:], io[:, 0:AX].indirect(T.rk1[:]), AF.Sign, scale=-1.0, bias=K + 0.5)
+        scan(one, "fl ones", "cm", T.cm[:], T.fl[:], ones[:, 0:N1], 0.0, AL.add, AL.add)
         for s in range(3):
-            act(plain(N1), "cm kk", "mx3_%d idf%d" % (s, s), T.mx3[:, N1 * s:N1 * s + N1], T.cm[:], AF.Sign, scale=-1.0,
-                bias=T.kk[:, s:s + 1], accum_out=T.jf[:, 4 + s:5 + s])
+            act(plain(N1), "cm k21", "mx3_%d idf%d" % (s, s), T.mx3[:, N1 * s:N1 * s + N1], T.cm[:], AF.Sign, scale=-1.0,
+                bias=T.sb[:, K21 + s:K21 + s + 1], accum_out=T.jf[:, 4 + s:5 + s])
             ts(one, "idf%d q4" % s, "c4p%d" % s, T.c4p[:, s:16:4], T.q4[:], T.jf[:, 4 + s:5 + s], AL.add, 2.0, AL.mult)
-        lo = LAND[t] + K - 128 if t else 0
+        ho = HO + A * (t == L)
         for b in range(4):
-            mm("qe lz " + " ".join("land%d" % i for i in range(t + 1)), 1 + b, 128, T.qe[:, 128 * b:128 * b + 128], T.se[:, 128 * b:128 * b + 128],
-               T.lq[:, lo:lo + 128], T.ls[:, lo:lo + 128])
-            o = 512 * (1 + b) + LAND[t] - lo
-            act(one, "ps%d" % (1 + b), "C%d_%d" % (t, b), xb[:, b:4 * K:4], T.ps[:, o:o + K])
+            eq, es, o = T.qe[:, 128 * b:128 * b + 128], T.se[:, 128 * b:128 * b + 128], 512 * (1 + b)
+            if t == L:
+                mm("qe%d land%d" % (b, t), 1 + b, A, eq, es, T.la[:], T.lb[:])
+                act(plain(A), "ps%d" % (1 + b), "C%d_%d" % (t, b), xb[:, 4 * HO + b:4 * ho:4], T.ps[:, o:o + A], AF.Copy)
+            else:
+                mm("qe%d qf%d land%d" % (b, t, t), 1 + b, 128, eq, es, qf[:, 0:128], sf[:, 0:128])
+                act(one, "ps%d" % (1 + b), "C%d_%d" % (t, b), xb[:, 4 * CO + b:4 * XO:4], T.ps[:, o:o + K], AF.Copy)
         for i in range(2):
             c = slice(128 * i, 128 * i + 128)
-            act(took(512), "%s %s src4" % (X, came), "zz%d" % i, T.zz[:, 512 * i:512 * i + 512], xb[:, 0:4 * HO].indirect(T.src4[:, 32 * i:32 * i + 32]))
+            act(took(512), "%s %s src4" % (X, came), "zz%d" % i, T.zz[:, 512 * i:512 * i + 512], xb[:, 0:4 * ho].indirect(T.src4[:, 32 * i:32 * i + 32]), AF.Copy)
             quant(128, "zz%d" % i, "qz%d" % i, T.qz[:, c], T.sz[:, c], T.zz[:, 512 * i:512 * i + 512])
             for b in range(4):
                 mm("qw sw qz%d" % i, banks[i][b], 128, T.qw[:, 128 * b:128 * b + 128], T.sw[:, 128 * b:128 * b + 128], T.qz[:, c], T.sz[:, c])
                 o = 512 * banks[i][b]
-                act(plain(128), "ps%d" % banks[i][b], "H%d_%d" % (t, 4 * i + b), xb[:, 4 * HO + 512 * i + b:4 * HO + 512 * i + 512:4], T.ps[:, o:o + 128], AF.Relu, scale=0.03125)
+                act(plain(128), "ps%d" % banks[i][b], "H%d_%d" % (t, 4 * i + b), xb[:, 4 * ho + 512 * i + b:4 * ho + 512 * i + 512:4], T.ps[:, o:o + 128], AF.Relu, scale=0.03125)
+        lk = "c4p0 c4p1 c4p2"
         for b in range(4):
-            lk, lb = "c4p0 c4p1 c4p2", T.c4p[:, 4 * b:4 * b + 3]
+            lb = T.c4p[:, 4 * b:4 * b + 3]
             tt(took(K), "k0_0 k0_1 cl " + lk, "ra2_%d" % b, T.ra2[:, b:N2:4], T.k0[:].indirect(lb), T.cl[:, b:N2:4], AL.max)
             act(took(K), "k0_0 k0_1 " + lk, "k2_%d" % b, T.k2[:, b:N2:4], T.k0[:].indirect(lb))
-            act(took(K), "ioa " + lk, "plr_%d" % b, T.plr[:, b:N2:4], T.io1[:, XO:HO].indirect(lb))
+            if b:
+                act(one, "plr_0", "plr_%d" % b, T.plr[:, b:N2:4], T.plr[:, 0:N2:4], bias=float(b))
+            else:
+                act(took(K), "ioa iob " + lk, "plr_0", T.plr[:, 0:N2:4], io[:, 0:P].indirect(lb), bias=float(e0))
         scan(plain(N2), "ra2 cr", "ow2", T.ow2[:], T.cr[:], T.ra2[:], BIG, AL.max, AL.min)
         tt(took(N2), "ow2 ol ra2", "dg2", T.dg2[:], T.ow2[:].indirect(T.ol[:]), T.ra2[:], AL.is_equal)
-        scan(plain(96), "dg2 ramp0", "dc2", T.dc2[:], T.ramp0[:], T.dg2[:], 0.0, AL.min, AL.add)
-        rk = ranking(2, T.k2, "k2", 1, N2, TUNE["sg2"][t], TUNE["sg2"][t])
-        cp(put(N2), "plr " + rk, "tbn", T.tb[:, HO:DO].indirect(T.rk2[:]), T.plr[:])
+        scan(plain(96), "dg2 r16", "dc2", T.dc2[:], T.r16[:, 0:N2], T.dg2[:], 0.0, AL.min, AL.add)
+        rk = ranking(2, T.k2, "k2", 1, N2, TUNE["sg2"][t])
+        cp(put(N2), "plr " + rk, "tbn", T.tb[:, SO:TW].indirect(T.rk2[:]), T.plr[:])
 
         def gather_x():
             xp = TUNE["xp"]
             w = P // xp
             for i in range(2):
-                lane4("ee%d" % t, "sE", "e4_%d" % i, T.e4[:, 64 * i:64 * i + 64], e[:, XO + h * i:XO + h * i + h], h, h * i, str(i))
+                lane4(ek, "sE", "e4_%d" % i, T.e4[:, 64 * i:64 * i + 64], e[:, e0 + h * i:e0 + h * i + h], h, CE, h * i, str(i))
                 alias["X%d_%d" % (t + 1, i)] = ["Xp%d_%d" % (t + 1, j) for j in range(xp) if j * 2 // xp == i]
             for i in range(xp):
                 move(i >= xp - TUNE["xv"][t], took(4 * w), "%s e4_%d" % (pool, i * 2 // xp), "Xp%d_%d" % (t + 1, i),
@@ -568,30 +606,29 @@ def rank_program(g, core, T, topo):
 
         if not late:
             gather_x()
-            lane4("jr", "sH", "hv4", T.hv4[:], short("jr"), K)
-            act(took(4 * K), pool + " hv4", "hv", T.hv[:], xb[:].indirect(T.hv4[:]))
-        vr1, v16 = T.tb[:, HO:NO], T.v16[:, 0:3]
-        lane16("tbn", "sV", "v16", v16, vr1, K)
+            lane4("jr", "sH", "hv4", T.hv4[:], short("jr"), K, CE)
+            act(took(4 * K), pool + " hv4", "hv", T.hv[:], xb[:].indirect(T.hv4[:]), AF.Copy)
+        vr, v16 = T.tb[:, SO:NO], T.v16[:, 0:3]
+        lane16("tbn", "sV", "v16", v16, vr, K, float(OFF))
         if not late:
-            lane4("tbn", "sW", "v4", T.v4[:], vr1, K)
-            cp(put(4 * K), "hv v4", Xn, xn[:, 0:4 * NO].indirect(T.v4[:]), T.hv[:])
+            lane4("tbn", "sW", "v4", T.v4[:], vr, K, CB)
+            cp(put(4 * K), "hv v4", Xn + (" Z%d " % (t + 1) + " ".join("C%d_%d" % (t + 1, b) for b in range(4)) if t < L else ""), xn[:, 0:4 * HO].indirect(T.v4[:]), T.hv[:])
+        byold = t < L and not TUNE["adr"][t + 1]
+        if t == 0 or byold:
+            act(took(K), "tgr tgra v16", "old", short("old"), T.tgr[:].indirect(v16))
         if t == 0:
-            act(took(K), "tgr tgra tgrb v16", "old", short("old"), T.tgr[:].indirect(v16), AF.Identity, bias=1.0)
-            act(one, "old", "olv", short("olv"), short("old"), AF.Identity, bias=float(DO))
             lane16("old", "so", "o16", T.o16[:, 0:3], short("old"), K)
-            cp(put(K), "olv o16", "at", T.at[:].indirect(T.o16[:, 0:3]), short("olv"))
-            cp(put(K), "tbn a16", "at", T.at[:].indirect(T.a16[:, 0:3]), vr1)
-        cp(put(K), "a0 v16", "tgr tgra tgrb", T.tgr[:].indirect(v16), short("a0"))
-        if t < R - 1:
-            en, nk = T["ee%d" % (t + 1)], "ee%d en%d" % (t + 1, t + 1)
-            tt(plain(2 * K), "en%d tbn" % (t + 1), "ve", short("ve"), en[:, HO:NO], vr1, AL.max)
-            if t:
-                iota(P, "tbp", T.tb[:, XO:HO], [[1, P]], XO + 1)
-            cp(put(K), "z48 v16", "tbp tbn", T.tb[:, 0:NO].indirect(v16), short("z48"))
-            cp(put(K), "ve v16", nk, en[:, 0:NO].indirect(v16), short("ve"))
-            lifts(t + 1)
+            cp(put(K), "old o16", "at", T.at[:].indirect(T.o16[:, 0:3]), short("old"))
+            cp(put(K), "tbn a16", "at", T.at[:].indirect(T.a16[:, 0:3]), vr)
+        cp(put(K), "a1 v16", "tgr tgra", T.tgr[:].indirect(v16), short("a1"))
+        if t < L:
+            en = T["ee%d" % (t + 1)]
+            tt(took(K), "en%d idu v16" % (t + 1), "ve", short("ve"), T.idu[:, 0:HO].indirect(v16), en[:, SO:NO], AL.max)
+            zk = "old" if byold else "z48"
+            cp(put(K), zk + " v16", "tbp", T.tb[:, OFF:SO].indirect(v16), short(zk))
+            cp(put(K), "ve v16", "ee%d" % (t + 1), en[:, OFF:SO].indirect(v16), short("ve"))
             if late:
-                cp(put(K), "jr v16", ek, e[:, 0:NO].indirect(v16), short("jr"))
+                cp(put(K), "jr v16", ek, e[:, OFF:SO].indirect(v16), short("jr"))
                 gather_x()
             lists(t + 1)
 
@@ -601,8 +638,8 @@ def rank_program(g, core, T, topo):
         c, half = slice(w * i, w * i + w), i * 2 // fin
         quant(w, "X%d_%d" % (R, half), "qx%d qy%d" % (half, i) if i * 2 % fin == 0 else "qy%d" % i, T.qx[:, c], T.sx[:, c], xb[:, 4 * (XO + w * i):4 * (XO + w * i + w)])
         mm("qv qy%d" % i, 1 + i, w, T.qv[:], T.sv[:], T.qx[:, c], T.sx[:, c])
-        move(i % 2, plain(w), "ps%d" % (1 + i), "hm%d ys%d" % (half, i) if i * 2 % fin == 0 else "ys%d" % i, T.hm[:, c], T.ps[:, 512 * (1 + i):512 * (1 + i) + w])
-        dma("a" if i % 2 == 0 else "s", "ys%d" % i, "y%d" % i, T.y[:, c], T.hm[:, c], 1800.0)
+        move(i % 2, plain(w), "ps%d" % (1 + i), "ys%d" % i, T.ys[:, c], T.ps[:, 512 * (1 + i):512 * (1 + i) + w])
+        dma("a" if i % 2 == 0 else "s", "ys%d" % i, "y%d" % i, T.y[:, c], T.ys[:, c], 1800.0)
     for i in range(2):
         dma("s", " ".join("qy%d" % j for j in range(fin) if j * 2 // fin == i), "oc%d" % i, T.oc[:, 4 * h * i:4 * h * i + 4 * h],
             T.qx[:, h * i:h * i + h].bitcast(dt.uint8), 2000.0)
@@ -612,11 +649,11 @@ def rank_program(g, core, T, topo):
 
     ops = [(q, [x for k in rd for x in alias.get(k, [k])], [x for k in wr for x in alias.get(k, [k])], a, b, f) for q, rd, wr, a, b, f in ops]
     known = {q: {} for q in Q}
-    count, wrote, readers = {}, {}, {}
+    total, wrote, readers = {}, {}, {}
     for t in range(R):
         for key, sem, src, writes in (("rql%d" % t, "rq%d" % t, prv, 1), ("land%d" % t, "fa%d" % t, nxt, 2)):
-            count[sem] = writes * len(topo.engines(src, core))
-            wrote[key] = (sem, count[sem], {sem: count[sem]})
+            total[sem] = writes * len(topo.engines(src, core))
+            wrote[key] = (sem, total[sem], {sem: total[sem]})
     ndma = 0
     for i in arrange(ops, nload):
         q, rd, wr, _, _, fn = ops[i]
@@ -635,7 +672,7 @@ def rank_program(g, core, T, topo):
             dst = fn[1]
             rid, pid, _ = topo.addr(dst)
             g.remote_dma(fn[2], fn[3], T.sem[fn[4]], T.sem.sent, pid, rid, topo.mask(core, dst))
-            count["sent"] = count.get("sent", 0) + len(topo.engines(core, dst))
+            total["sent"] = total.get("sent", 0) + len(topo.engines(core, dst))
             continue
         if fn[0] == "dma":
             sem, inc = "d%d" % ndma, 16
@@ -644,15 +681,15 @@ def rank_program(g, core, T, topo):
         else:
             sem, inc = OWN[q], 1
             fn[1]().then_inc(T.sem[sem], 1)
-        count[sem] = count.get(sem, 0) + inc
+        total[sem] = total.get(sem, 0) + inc
         clock = dict(known[q])
-        clock[sem] = count[sem]
-        tok = (sem, count[sem], clock)
+        clock[sem] = total[sem]
+        tok = (sem, total[sem], clock)
         for k in rd:
             readers.setdefault(k, []).append(tok)
         for k in wr:
             wrote[k] = tok
             readers[k] = []
-    for sem in sorted(count):
-        if known["g"].get(sem, 0) < count[sem]:
-            g.wait_ge(T.sem[sem], count[sem])
+    for sem in sorted(total):
+        if known["g"].get(sem, 0) < total[sem]:
+            g.wait_ge(T.sem[sem], total[sem])

import numpy as np
from concourse.mybir import dt, AluOpType, ActivationFunctionType

MC, P, A, K, R = 1024, 512, 256, 48, 3
L = R - 1
BIG = 1.0e29
LIFT = 8192.0
UP = 2.0 ** 71
FAR = 2.0 ** 84
N1, N2 = P // 4, 4 * K
S1, S2 = N1 // 16, N2 // 16
AX = A + K
CO, XO, HO, XW = 16, 64, 64 + P, 64 + P + A
OFF = MC + K
SO, NO, TW = OFF + HO, OFF + HO + K, OFF + HO + K + N2
TUNE = dict(sg1=[3, 3, 3], sg2=[5, 5, 5], xv=[1, 1, 1], late=[1, 1, 0], xp=4, fin=4, adr=[0, 0, 0],
            cases=[(1.0, 1.56, 3.8, 220.0, 1.0, 0.4), (1.15, 1.5, 3.0, 150.0, 1.2, 0.3), (1.35, 2.3, 5.5, 200.0, 0.8, 0.3)], plan=(1.1, 1.7, 4.1, 200.0),
            back=40, boost=[6000.0, 3000.0, 0.0], swaps=8000, heat=60.0, seed=1, tries=600, noise=2000.0, slack=300.0,
            far=1800.0, first=2000.0, long=4000.0, xl=4800.0)

F32, BF, I32, U16, X4, U8 = "float32", "bfloat16", "int32", "uint16", "float8_e4m3fn_x4", "uint8"
SHORT = "cam caj slo z48 ve old jr a1 sa so sV sW sR sH".split()
SCRATCH = {}


def _sb(name, n, dtype):
    SCRATCH[name] = ("sbuf", [128, n], dtype)


for _n, _w, _d in [
    ("tgi", 32, I32), ("adi", 48, I32), ("tg16", 32, U16), ("ad16", 48, U16),
    ("mm", 4 * OFF, BF), ("uu", 512, BF), ("vv", 512, BF),
    ("qu", 128, X4), ("su", 128, U8), ("qu2", 128, X4), ("su2", 128, U8), ("qv", 128, X4), ("sv", 128, U8),
    ("qw", 512, X4), ("sw", 512, U8), ("qx", 512, X4), ("sx", 512, U8), ("qz", 256, X4), ("sz", 256, U8),
    ("eb", 528, BF), ("qe", 512, X4), ("se", 512, U8),
    ("ft", 512, BF), ("zz", 4 * A, BF), ("hv", 4 * K, BF),
    ("rqa", 16, U16), ("rq4", 64, U16), ("fa", 4 * A, BF), ("qa", A, X4), ("sa", A, U8), ("la", A, X4), ("lb", A, U8),
    ("pint", 8, I32), ("sc", 24, F32), ("sb", 16, BF), ("q4", 4, F32), ("ul", 12, U16), ("ol", 12, U16),
    ("c16", A, F32), ("c4", A, F32), ("c4u", A, F32), ("c4m", A, F32), ("cl", N2, F32), ("cr", N2, F32),
    ("r16", A, BF), ("r4", A, BF), ("ones", HO, BF),
    ("rows", len(SHORT) * K, F32), ("at", OFF, F32), ("tgr", HO, F32), ("tb", TW, F32), ("idu", HO + K, F32), ("ju", AX, F32), ("jv", AX, F32),
    ("adr", R * AX, F32), ("src", R * AX, F32), ("pre", A, F32), ("sP", A, F32), ("pre16", R * 16, U16),
    ("flg", A, BF), ("cum", A, BF), ("jx", 3 * A, BF), ("jc", 3 * A // 2, BF), ("jf", 8, F32), ("j16", 4 * R, U16),
    ("sA", A, F32), ("src4", 64, U16), ("sE", P, F32), ("e4", 128, U16), ("hv4", 12, U16), ("a16", 4, U16),
    ("ys", P, F32), ("k0", P, F32), ("k1", P, F32),
    ("ra1", N1, F32), ("ow1", N1, F32), ("dg1", N1, BF), ("dc1", N1, BF), ("mx1", S1 * N1, BF), ("cm1", S1 * 64, BF),
    ("rf1", 3 * S1, F32), ("rk1", S1, U16),
    ("fl", N1, BF), ("cm", N1, BF), ("mx3", 3 * N1, BF), ("c4p", 16, U16),
    ("k2", N2, F32), ("ra2", N2, F32), ("ow2", N2, F32), ("dg2", N2, BF), ("dc2", N2, BF), ("mx2", S2 * N2, BF), ("cm2", S2 * 96, BF),
    ("rf2", 3 * S2, F32), ("rk2", S2, U16),
    ("plr", N2, F32), ("v16", 4, U16), ("v4", 12, U16), ("o16", 4, U16),
]:
    _sb(_n, _w, _d)
for _t in range(R):
    _sb("ee%d" % _t, NO, F32)
for _t in range(L):
    _sb("req%d" % _t, 12, U16)
    _sb("rql%d" % _t, 12, U16)
    _sb("qf%d" % _t, K + 128, X4)
    _sb("sf%d" % _t, K + 128, U8)
for _t in range(R + 1):
    _sb("xb%d" % _t, 4 * (XW + A * (_t == L)), BF)
SCRATCH["ps"] = ("psum", [128, 4096], F32)

SEMAPHORES = (["cv", "ca", "ct", "cg", "sent"] + ["d%d" % i for i in range(24)]
              + ["rq%d" % t for t in range(R)] + ["fa%d" % t for t in range(R)])

AL = AluOpType
AF = ActivationFunctionType
ORDER, SPAN = [], []


def arrange(ops, first):
    if ORDER:
        return ORDER[0]
    n = len(ops)
    pred = [set() for _ in range(n)]
    wrote, readers = {}, {}
    for i, (q, rd, wr, hold, lat, fn) in enumerate(ops):
        for k in rd:
            pred[i].update(wrote.get(k, []))
        for k in wr:
            if not k.startswith("land"):
                pred[i].update(wrote.get(k, []))
            pred[i].update(readers.get(k, []))
        pred[i].discard(i)
        for k in rd:
            readers.setdefault(k, []).append(i)
        for k in wr:
            wrote[k] = (wrote.get(k, []) if k.startswith("land") else []) + [i]
            readers[k] = []
    succ = [[] for _ in range(n)]
    for i in range(n):
        for j in sorted(pred[i]):
            succ[j].append(i)
    pred = [sorted(p) for p in pred]
    cases, wake = TUNE["cases"], TUNE["plan"][3]

    def held(c):
        return [float(o[3][0] + 0.83 * (o[3][1] * c[0] + o[3][2] * c[1] + o[3][3] * c[2])) for o in ops]
    hold = held(TUNE["plan"])
    lat = [o[4] for o in ops]
    tail = [hold[i] + lat[i] + wake for i in range(n)]
    queue = [o[0] for o in ops]
    qn = ["vatgs".index(q) for q in queue]
    costs = [(held(c), [lat[i] * c[4] + c[3] for i in range(n)]) for c in cases]

    def lay(key, back):
        before, after = (succ, pred) if back else (pred, succ)
        left = [len(p) for p in before]
        at, busy, low, seen = [0.0] * n, [[] for _ in range(5)], [0.0] * n, [False] * n
        for i0 in sorted(range(n), key=lambda i: key[i]):
            seen[i0] = True
            if left[i0]:
                continue
            todo = [i0]
            while todo:
                i = todo.pop()
                h = hold[i]
                t = low[i] + (lat[i] if back else 0.0)
                b = busy[qn[i]]
                k = len(b)
                while k and b[k - 1][1] > t:
                    k -= 1
                while k < len(b) and b[k][0] < t + h:
                    if b[k][1] > t:
                        t = b[k][1]
                    k += 1
                b.insert(k, (t, t + h))
                at[i] = t
                e = t + (h + wake if back else tail[i])
                for j in after[i]:
                    left[j] -= 1
                    if low[j] < e:
                        low[j] = e
                    if not left[j] and seen[j]:
                        todo.append(j)
        return at

    def play(seq, a, old):
        total, ends, whys = 0.0, [], []
        last = [-1] * 5
        k, found = a - 1, 0
        while k >= 0 and found < 5:
            if last[qn[seq[k]]] < 0:
                last[qn[seq[k]]] = seq[k]
                found += 1
            k -= 1
        rest = seq[a:]
        for c, (hf, lf) in enumerate(costs):
            end, why, prev = old[1][c][:], old[2][c][:], last[:]
            free = [end[j] - lf[j] if j >= 0 else 0.0 for j in last]
            for i in rest:
                q = qn[i]
                t, y = free[q], -2 - prev[q]
                for j in pred[i]:
                    if end[j] > t:
                        t, y = end[j], j
                t += hf[i]
                free[q] = t
                prev[q] = i
                why[i] = y
                end[i] = t + lf[i]
            total += cases[c][5] * max(end)
            ends.append(end)
            whys.append(why)
        return total, ends, whys

    blank = (0.0, [[0.0] * n for _ in cases], [[-1] * n for _ in cases])
    way = [0.0] * n
    for i in range(n - 1, -1, -1):
        way[i] = hold[i] + lat[i] + max([way[j] + wake for j in succ[i]], default=0.0)
    rng = np.random.default_rng(TUNE["seed"])
    cur, best, key = None, None, [-w for w in way]
    for t in range(R):
        todo = [i for i in range(n) if ops[i][2] and ops[i][2][0].startswith("H%d_" % t)]
        stop = min(i for i in range(n) if "j16_%d" % t in ops[i][2]) - TUNE["back"]
        hot = set()
        while todo:
            i = todo.pop()
            if i not in hot and i >= stop:
                hot.add(i)
                todo.extend(pred[i])
        for i in hot:
            key[i] -= TUNE["boost"][t]
    for it in range(TUNE["tries"]):
        if best:
            key = list(cur[1])
            for _ in range(int(rng.integers(1, 4))):
                a = int(rng.integers(first, n))
                d = float(rng.standard_normal()) * TUNE["noise"]
                for i in range(a, min(n, a + int(rng.integers(1, 40)))):
                    key[i] += d
        for turn in range(2):
            at = lay([-1e9 + i if i < first else key[i] for i in range(n)], False)
            if turn or not it:
                span = play(sorted(range(n), key=lambda i: (at[i], i)), 0, blank)[0]
                if best is None or span <= best[0]:
                    best = (span, at)
                if cur is None or span <= cur[0] + TUNE["slack"] * (1 - it / TUNE["tries"]) * rng.random():
                    cur = (span, at)
            if turn == 0:
                ab = lay([-(at[i] + tail[i]) for i in range(n)], True)
                key = [-(ab[i] + hold[i]) for i in range(n)]
    seq = sorted(range(n), key=lambda i: (best[1][i], i))
    now = play(seq, 0, blank)
    top = (now[0], seq)
    for it in range(TUNE["swaps"]):
        c = int(rng.integers(len(cases)))
        end, why = now[1][c], now[2][c]
        i, arcs = end.index(max(end)), []
        while i >= 0:
            if why[i] <= -2:
                arcs.append((-2 - why[i], i))
                i = -2 - why[i]
            else:
                i = why[i]
        if not arcs:
            break
        p, i = arcs[int(rng.integers(len(arcs)))]
        if p < first:
            continue
        a, b = seq.index(p), seq.index(i)
        ahead = rng.random() < 0.5
        for _ in range(int(rng.integers(0, 4)) ** 2 // 2):
            k = a - 1 if ahead else b + 1
            while 0 <= k < n and queue[seq[k]] != queue[i]:
                k += -1 if ahead else 1
            if 0 <= k < n and seq[k] >= first:
                a, b = (k, b) if ahead else (a, k)
        link = pred if ahead else succ
        moved, rest, qs = [i if ahead else p], [], set()
        need = set(link[moved[0]])
        for k in (range(b - 1, a - 1, -1) if ahead else range(a + 1, b + 1)):
            j = seq[k]
            if j in need or queue[j] in qs:
                moved.append(j)
                need.update(link[j])
                qs.add(queue[j])
            else:
                rest.append(j)
        new = seq[:a] + (moved[::-1] + rest[::-1] if ahead else rest + moved) + seq[b + 1:]
        trial = play(new, a, now)
        if trial[0] <= now[0] + TUNE["heat"] * (1 - it / TUNE["swaps"]) * rng.random() ** 2:
            seq, now = new, trial
            if now[0] < top[0]:
                top = (now[0], seq)
    SPAN.extend([round(best[0]), round(top[0]), {q: round(sum(hold[i] for i in range(n) if queue[i] == q)) for q in "vag"}, round(max(way))])
    ORDER.append(top[1])
    return ORDER[0]


def rank_program(g, core, T, topo):
    rank = T.rank_of(core)
    if rank is None:
        return
    n = len(T.cores)
    nxt, prv = T.cores[(rank + 1) % n], T.cores[(rank - 1) % n]
    Q = {"v": g.vector, "a": g.scalar, "t": g.tensor, "g": g, "s": g.sync}
    OWN = {"v": "cv", "a": "ca", "t": "ct", "g": "cg"}
    ops, alias = [], {k: ["%s_%d" % (k, b) for b in range(4)] for k in ("ra2", "k2", "plr")}
    alias.update(ra1=["ra1_0", "ra1_1"], ow1=["ow1_0", "ow1_1"])

    def add(q, rd, wr, hold, lat, fn):
        ops.append((q, rd.split(), wr.split(), hold, lat, fn))

    def plain(w, fixed=0):
        return (fixed, max(64, w), 0, 0)

    def took(w):
        return (60, 0, w, 0)

    def put(w):
        return (50, 0, 0, w)

    def op(q, rd, wr, hold, fn):
        add(q, rd, wr, hold, 0.0, ("op", fn))

    def dma(q, rd, wr, out, in_, lat=1500.0):
        add(q, rd, wr, (60, 0, 0, 0), lat, ("dma", out, in_))

    def send(dst, rd, wr, out, in_, sem, more=0.0, lat=TUNE["far"]):
        add("g", rd, wr, (300 + more, 0, 0, 0), lat, ("send", dst, out, in_, sem))

    V, S = g.vector, g.scalar

    def ts(c, rd, wr, out, in0, s1, op0, s2=None, op1=None):
        if op1 is None:
            op("v", rd, wr, c, lambda: V.tensor_scalar(out, in0, s1, None, op0))
        else:
            op("v", rd, wr, c, lambda: V.tensor_scalar(out, in0, s1, s2, op0, op1))

    def tt(c, rd, wr, out, in0, in1, o):
        op("v", rd, wr, c, lambda: V.tensor_tensor(out, in0, in1, o))

    def cp(c, rd, wr, out, in_):
        op("v", rd, wr, c, lambda: V.tensor_copy(out, in_))

    def scan(c, rd, wr, out, d0, d1, init, op0, op1):
        op("v", rd, wr, c, lambda: V.tensor_tensor_scan(out, d0, d1, init, op0, op1))

    def act(c, rd, wr, out, in_, func=AF.Identity, **kw):
        op("a", rd, wr, (c[0] + (20 if "accum_out" in kw else 0),) + c[1:], lambda: S.activation(out, in_, func, **kw))

    def move(on_v, c, rd, wr, out, in_):
        if on_v:
            cp(c, rd, wr, out, in_)
        else:
            act(c, rd, wr, out, in_, AF.Copy)

    def quant(w, rd, wr, q, s, in_):
        op("v", rd, wr, (0, 14 + 1.06 * w, 0, 0), lambda: V.quantize_mx(q, s, in_))

    def mm(rd, bank, w, lq, ls, rq, rs):
        op("t", rd, "ps%d" % bank, (60 + 0.7 * w, 0, 0, 0), lambda: g.tensor.matmul_mx(T.ps[:, 512 * bank:512 * bank + w], lq, ls, rq, rs, True, True))

    def iota(w, wr, out, pattern, base):
        op("g", "", wr, (130, 2 * w, 0, 0), lambda: g.iota(out, pattern, base, 0, allow_small_or_imprecise_dtypes=True))

    def count(wr, out, w, base):
        iota(w, wr, out, [[1, w]], base)

    one = plain(1)

    def col(i):
        return T.sc[:, i:i + 1]
    LANE, T0, CLS4, B16, BF1, BF2, B4, L16, L4, CA, CB, CE, L21, S0, KM = range(15)
    S2X, K21, BASE = T.sb[:, 0:1], 2, 6
    MID = A / 2 - K

    def short(name):
        o = K * SHORT.index(name)
        return T.rows[:, o:o + K]

    def held(rd, tmp, key, c, row, w, o):
        buf, o = (T.rows, K * SHORT.index(tmp)) if tmp in SHORT else (T[tmp], o)
        scan(plain(w), rd, tmp + key, buf[:, o:o + w], c[:, 0:w], row, 0.0, AL.add, AL.max)
        return buf, o

    def lane16(rd, tmp, wr, out, row, w, less=0.0):
        buf, o = held(rd + " c16", tmp, "", T.c16, row, w, 0)
        ts(one, tmp + " l16", wr, out, buf[:, o + 15:o + w:16], col(L16), AL.subtract, -less, AL.add)

    def lane4(rd, tmp, wr, out, row, w, kind, o=0, key=""):
        c, f = ("c4u", 4.0 / UP) if kind == CE else ("c4", 4.0)
        buf, o = held(rd + " " + c, tmp, key, T[c], row, w, o)
        ts(plain(w // 4), tmp + key + " cc%d" % kind, wr, out, buf[:, o + 3:o + w:4], f, AL.mult, col(kind), AL.subtract)

    dma("s", "", "tgi", T.tgi[:], T.tg[:])
    dma("a", "", "adi", T.adi[:], T.ad[:])
    dma("s", "", "uu", T.uu[:], T.u[:], 2200.0)
    dma("s", "", "X0_0 X0_1", T.xb0[:, 4 * XO:4 * HO], T.x[:], TUNE["xl"])
    dma("s", "", "mm", T.mm[:, 0:4 * MC], T.m[:], 8000.0)
    dma("s", "", "qw", T.qw[:].bitcast(dt.uint8), T.wc[:], 9000.0)
    dma("s", "", "sw", T.sw[:], T.ws[:], 9500.0)
    dma("s", "", "vv", T.vv[:], T.v[:], 10000.0)
    nload = len(ops)

    pidx, ones, io = T.pint[:, 4:5], T.ones, T.tb
    op("g", "", "pidx", (140, 0, 0, 0), lambda: g.iota(pidx, [[0, 1]], 0, 1))
    op("v", "", "ones", plain(HO // 2), lambda: V.memset(ones[:], 1.0))
    hf = OFF // 2
    for i in range(2):
        scan(plain(hf), "ones", "at%d" % i, T.at[:, hf * i:hf * i + hf], ones[:, 0:hf], ones[:, 0:hf], hf * i - 1.0, AL.add, AL.mult)
    scan(plain(HO), "ones", "tbp", T.tb[:, OFF:SO], ones[:], ones[:], OFF - 1.0, AL.add, AL.mult)
    iota(A, "r16", T.r16[:], [[0, A // 16], [1, 16]], 0)
    iota(A, "r4", T.r4[:], [[0, A // 4], [1, 4]], 0)
    count("ioa", io[:, 0:AX], AX, 0)
    count("iob", io[:, AX:OFF], OFF - AX, AX)
    count("tbn", T.tb[:, SO:NO], K, OFF + CO)
    count("cam", short("cam"), K, OFF + CO)
    count("slo", short("slo"), K, SO)
    count("tgra", T.tgr[:, 0:XO], XO, MC - CO)
    ts(one, "pidx", "lanei", T.pint[:, 0:1], pidx, 15, AL.bitwise_and)
    ts(one, "pidx", "ti", T.pint[:, 1:2], pidx, 3, AL.bitwise_and)
    cp(one, "lanei ti", "lane", T.sc[:, 0:2], T.pint[:, 0:2])
    act(one, "lane", "cls4", col(CLS4), col(T0), scale=-1.0, bias=col(LANE))
    act(one, "lane", "b16", col(B16), col(LANE), scale=-LIFT, bias=-0.5 * LIFT)
    act(one, "lane", "bf1", col(BF1), col(LANE), scale=-FAR, bias=-0.5 * FAR)
    act(one, "lane", "bf2", col(BF2), col(LANE), scale=FAR, bias=0.5 * FAR)
    act(one, "cls4", "b4", col(B4), col(CLS4), scale=-LIFT / 4, bias=-0.5 * LIFT)
    root = (LIFT / 2) ** 0.5
    act(one, "lane", "l16", col(L16), col(LANE), AF.Square, scale=-root, bias=15 * root)
    act(one, "cls4", "l4", col(L4), col(CLS4), AF.Square, scale=-root / 2, bias=6 * root)
    act(one, "l4 lane", "cc%d" % CA, col(CA), col(T0), scale=-1.0, bias=col(L4))
    act(one, "cc%d" % CA, "cc%d" % CB, col(CB), col(CA), bias=4.0 * OFF)
    act(one, "cc%d" % CA, "cc%d" % CE, col(CE), col(CA), bias=2.0 - 4 * HO)
    act(one, "lane", "l21", col(L21), col(LANE), scale=2.0, bias=1.0)
    act(one, "ioa l21", "k21", T.sb[:, K21:K21 + 3], io[:, 0:K:16], scale=2.0, bias=col(L21))
    act(one, "k21", "km", T.sc[:, KM:KM + 3], T.sb[:, K21:K21 + 3], scale=0.5, bias=-MID - 0.5)
    act(plain(A), "r16 b16", "c16", T.c16[:], T.r16[:], scale=LIFT, bias=col(B16))
    act(one, "ones", "c16", T.c16[:, 0:A:16], ones[:, 0:A // 16], scale=-512 * LIFT)
    act(plain(A), "r4 b4", "c4", T.c4[:], T.r4[:], scale=LIFT, bias=col(B4))
    act(one, "ones", "c4", T.c4[:, 0:A:4], ones[:, 0:A // 4], scale=-512 * LIFT)
    act(plain(A), "c4", "c4u", T.c4u[:], T.c4[:], scale=UP)
    act(plain(A), "r4", "c4m", T.c4m[:], T.r4[:], scale=-FAR, bias=0.5 * FAR)
    act(plain(N2), "r16 bf1", "cl", T.cl[:], T.r16[:, 0:N2], scale=FAR, bias=col(BF1))
    act(plain(N2), "r16 bf2", "cr", T.cr[:], T.r16[:, 0:N2], scale=-FAR, bias=col(BF2))
    act(one, "r4", "q4", T.q4[:], T.r4[:, 0:4], scale=0.5, bias=float(N1))
    act(plain(AX), "ioa", "ju", T.ju[:], io[:, 0:AX], scale=UP, bias=(0.5 - K) * UP)
    act(plain(AX), "ioa", "jv", T.jv[:], io[:, 0:AX], scale=UP, bias=(0.5 - K + A) * UP)
    act(plain(HO), "tbp", "idu", T.idu[:, 0:HO], T.tb[:, OFF:SO], scale=UP, bias=(0.5 - SO) * UP)
    act(one, "ones", "idn", T.idu[:, HO:HO + K], ones[:, 0:K], scale=-1024 * UP)
    act(plain(P), "tbp", "ee0", T.ee0[:, OFF + XO:SO], T.tb[:, OFF + XO:SO], scale=UP, bias=(0.5 - SO) * UP)
    act(plain(512 - 4 * K), "ones", "ftz", T.ft[:, 4 * K:512], ones[:, 4 * K:512], scale=0.0)
    act(plain(4 * K), "ones", "mmz", T.mm[:, 4 * MC:4 * OFF], ones[:, 0:4 * K], scale=0.0)
    ts(one, "ioa", "ul", T.ul[:], io[:, 0:12], 16.0, AL.mult)
    ts(one, "ioa", "ol", T.ol[:], io[:, 0:12], 16.0, AL.mult, 15.0, AL.add)
    for t in range(R):
        zw = 4 * (XO if t == L else CO)
        iota(zw, "Z%d" % t, T["xb%d" % t][:, 0:zw], [[0, zw]], 0)
        if t:
            op("g", "idu idn", "ee%d en%d" % (t, t), (170, 2 * (P + K), 0, 0),
               lambda t=t: g.affine_select(T["ee%d" % t][:, OFF + XO:NO], T.idu[:, XO:HO + K], [[0, P + K]], AL.is_ge, 0.0, 0, 0))
        count("srx%d" % t, T.src[:, AX * t:AX * t + K], K, MC)
        if TUNE["adr"][t]:
            count("adx%d" % t, T.adr[:, AX * t:AX * t + K], K, MC)
    if max(TUNE["adr"]):
        iota(K, "z48", short("z48"), [[0, K]], 0)
    op("g", "ones", "eb", (170, 2 * 528, 0, 0), lambda: g.affine_select(T.eb[:], ones[:, 0:528], [[-1, 528]], AL.is_equal, 0.0, 3, 4))
    for b in range(4):
        quant(128, "eb", "qe%d" % b, T.qe[:, 128 * b:128 * b + 128], T.se[:, 128 * b:128 * b + 128], T.eb[:, 3 - b:515 - b])
    quant(128, "uu", "qu", T.qu[:], T.su[:], T.uu[:])
    cp(took(128), "qu ul", "qu2", T.qu2[:].bitcast(dt.uint32), T.qu[:].bitcast(dt.uint32).indirect(T.ul[:, 0:8]))
    act(took(128), "qu ul", "su2", T.su2[:], T.su[:].indirect(T.ul[:, 0:8]), AF.Copy)
    quant(128, "vv", "qv", T.qv[:], T.sv[:], T.vv[:])

    cp(one, "tgi", "tg16", T.tg16[:], T.tgi[:])
    cp(one, "adi", "ad16", T.ad16[:], T.adi[:])
    send(nxt, "ad16", "first rql%d" % L, T.rqa[:], T.ad16[:, 16 * L:16 * L + 16], "rq%d" % L, TUNE["first"])
    cp(put(P), "tbp tg16", "at at0 at1", T.at[:].indirect(T.tg16[:]), T.tb[:, OFF + XO:SO])
    act(took(P), "ioa iob tg16", "tgr", T.tgr[:, XO:HO], io[:, 0:MC].indirect(T.tg16[:]))
    for t in range(R):
        if TUNE["adr"][t]:
            act(took(A), "ioa iob ad16", "adr%d" % t, T.adr[:, AX * t + K:AX * t + AX], io[:, 0:MC].indirect(T.ad16[:, 16 * t:16 * t + 16]))

    def ahead(t):
        p16 = T.pre16[:, 16 * t:16 * t + 16]
        pre, pk = (T.pre[:], "pre") if t else (T.src[:, K:AX], "src0")
        act(took(A), "at ad16", pk, pre, T.at[:].indirect(T.ad16[:, 16 * t:16 * t + 16]))
        lane16(pk, "sP", "pre16_%d" % t, p16, pre, A)
        jn = "jv" if t == L else "ju"
        cp(put(A), jn + " pre16_%d" % t, "ee%d en%d" % (t, t), T["ee%d" % t][:].indirect(p16), T[jn][:, K:AX])

    def lists(t):
        j16, jk = T.j16[:, 4 * t:4 * t + 3], "j16_%d" % t
        src, sk, acc = T.src[:, AX * t:AX * t + AX], "src%d srx%d" % (t, t), T.jf[:, 3:4]
        real = T.src[:, AX * t + K:AX * t + AX]
        tk, win = ("ioa iob tbp tbn pre16_%d" % t, T.tb[:, 0:NO].indirect(T.pre16[:, 16 * t:16 * t + 16])) if t else ("at ad16", T.at[:].indirect(T.ad16[:, 0:16]))
        act(took(A), tk, "flg acc", T.flg[:], win, AF.Sign, scale=-1.0, bias=OFF - 0.5, accum_out=acc)
        if t:
            act(took(A), tk, "src%d" % t, real, win)
            count("tbn", T.tb[:, SO:NO], K, OFF + CO)
            if t < L:
                count("tbp", T.tb[:, OFF:SO], HO, OFF)
        act(one, "acc", "s2", S2X, acc, AF.Relu, scale=-1.0, bias=-2 * MID)
        act(one, "acc", "s0", col(S0), acc, AF.Relu, scale=-0.5, bias=-MID)
        scan(plain(A // 2), "flg ones", "cum", T.cum[:], T.flg[:], ones[:, 0:A], 0.0, AL.add, AL.add)
        ts(one, "km s0", "base", T.sb[:, BASE:BASE + 3], T.sc[:, KM:KM + 3], col(S0), AL.subtract, -MID, AL.min)
        hx = A // 2
        for s in range(3):
            ts(plain(hx), "cum s2 k21", "jx%d" % s, T.jx[:, A * s:A * s + A], T.cum[:], S2X, AL.add, T.sb[:, K21 + s:K21 + s + 1], AL.is_lt)
            scan(one, "jx%d base" % s, "jc%d" % s, T.jc[:, hx * s:hx * s + hx], T.jx[:, A * s:A * s + hx], T.jx[:, A * s + hx:A * s + A],
                 T.sb[:, BASE + s:BASE + s + 1], AL.add, AL.add)
        ts(one, "jc0 jc1 jc2", jk, j16, T.jc[:, hx - 1:3 * hx:hx], A / 2, AL.add)
        if TUNE["adr"][t]:
            act(took(K), "adr%d adx%d %s" % (t, t, jk), "a1", short("a1"), T.adr[:, AX * t:AX * t + AX].indirect(j16))
        else:
            act(took(K), sk + " " + jk, "a1", short("a1"), src.indirect(j16))
        ck, jn = ("caj", "jv") if t == L else ("cam", "ju")
        if t == L:
            act(took(K), "ioa " + jk, "caj", short("caj"), io[:, 0:AX].indirect(j16), bias=float(SO - K))
        else:
            lane4("a1", "sR", "req%d" % t, T["req%d" % t][:], short("a1"), K, CA)
            send(nxt, "first req%d" % t, "rql%d" % t, T["rql%d" % t][:], T["req%d" % t][:], "rq%d" % t)
        cp(put(K), ck + " " + jk, sk, src.indirect(j16), short(ck))
        lane4(sk, "sA", "src4", T.src4[:], real, A, CB)
        act(took(K), jn + " " + jk, "jr", short("jr"), T[jn][:].indirect(j16))
        if t < L:
            lane16("a1", "sa", "a16", T.a16[:, 0:3], short("a1"), K)
            cp(put(K), "slo a16", "at", T.at[:].indirect(T.a16[:, 0:3]), short("slo"))
            ahead(t + 1)

    def ranking(i, key, kk, step, w, a):
        ns, h = w // 16, w // 2
        mx, cm, dc, rf, rk, own = T["mx%d" % i], T["cm%d" % i], T["dc%d" % i], T["rf%d" % i], T["rk%d" % i], T["ow%d" % i]
        dk = "dc%d" % i
        more, mk, less = (0.0, "", 0.0) if i == 1 else (col(S0), " s0", 1.0)
        for s in range(ns):
            c, o, d = 16 * s, own[:, 16 * s + 15:16 * s + 16], dc[:, 16 * s + 15:16 * s + 16]
            rd = kk + (" ow2" if i == 2 else " ow1_%d" % (s // 4))
            ka, kb, o0 = "mx%da%d" % (i, s), "mx%db%d" % (i, s), w * s
            row, lrow, rrow = mx[:, o0:o0 + w], mx[:, o0:o0 + c], mx[:, o0 + c:o0 + w]
            if s < a:
                act(plain(w), rd, ka + " " + kb, row, key[:, step - 1:step * w:step], AF.Sign, scale=-1.0, bias=o)
                if s:
                    act(plain(c), "", ka + " rl%d_%d" % (i, s), lrow, lrow, AF.Sign, bias=0.5, accum_out=rf[:, ns + s:ns + s + 1])
                act(plain(w - c), "", kb + " rr%d_%d" % (i, s), rrow, rrow, AF.Sign, bias=-0.5, accum_out=rf[:, 2 * ns + s:2 * ns + s + 1])
                continue
            if s:
                ts(plain(c), rd, ka, lrow, key[:, step - 1:step * c:step], o, AL.is_le)
            ts(plain(w - c), rd, kb, rrow, key[:, step * c + step - 1:step * w:step], o, AL.is_lt)
            scan(one, "%s %s %s" % (ka, kb, dk), "cm%d_%d" % (i, s), cm[:, h * s:h * s + h], mx[:, o0:o0 + h], mx[:, o0 + h:o0 + w], d, AL.add, AL.add)
        done = []
        if a:
            if i == 2:
                act(one, "s0", "s1", T.jf[:, 7:8], col(S0), scale=2.0, bias=w - 2.0)
            act(one, dk + " s1", "ru%d" % i, rf[:, 0:a], dc[:, 15:16 * a:16], scale=2.0, bias=T.jf[:, 7:8] if i == 2 else float(w))
            if a > 1:
                tt(one, "ru%d " % i + " ".join("rl%d_%d" % (i, s) for s in range(1, a)), "ru%d" % i, rf[:, 1:a], rf[:, 1:a], rf[:, ns + 1:ns + a], AL.add)
            for s in range(a):
                ts(one, "ru%d rr%d_%d" % (i, i, s), "rk%da%d" % (i, s), rk[:, s:s + 1], rf[:, 2 * ns + s:2 * ns + s + 1], rf[:, s:s + 1], AL.add, 0.5, AL.mult)
                done.append("rk%da%d" % (i, s))
        if a < ns:
            ts(one, " ".join("cm%d_%d" % (i, s) for s in range(a, ns)) + mk, "rk%dc" % i, rk[:, a:ns], cm[:, h * a + h - 1:h * ns:h], more, AL.add, -less, AL.add)
            done.append("rk%dc" % i)
        return " ".join(done)

    h = P // 2
    ahead(0)
    lists(0)

    banks = [[5, 6, 7, 0], [1, 2, 3, 4]]
    for t in range(R):
        xb, xn, e = T["xb%d" % t], T["xb%d" % (t + 1)], T["ee%d" % t]
        ek, X, Xn = "ee%d" % t, "X%d_0 X%d_1" % (t, t), "X%d_0 X%d_1" % (t + 1, t + 1)
        H = " ".join("H%d_%d" % (t, b) for b in range(8))
        came = " ".join("C%d_%d" % (t, b) for b in range(4)) + " Z%d" % t
        pool = "%s %s %s" % (H, X, came)
        late = TUNE["late"][t]
        e0 = OFF + XO

        for i in range(2):
            c = slice(h * i, h * i + h)
            quant(h, "X%d_%d" % (t, i), "qx%d" % i, T.qx[:, c], T.sx[:, c], xb[:, 4 * (XO + h * i):4 * (XO + h * i + h)])
            mm("qu2 su2 qx%d" % i, 4 * i, h, T.qu2[:], T.su2[:], T.qx[:, c], T.sx[:, c])
            tt(plain(h), "ps%d %s" % (4 * i, ek), "k0_%d" % i, T.k0[:, c], T.ps[:, 2048 * i:2048 * i + h], e[:, e0 + h * i:e0 + h * i + h], AL.max)
            scan(plain(h), "k0_%d c4m" % i, "k1_%d" % i, T.k1[:, c], T.c4m[:], T.k0[:, c], BIG, AL.max, AL.min)
        if t < L:
            act(took(4 * K), "mm mmz rql%d" % t, "ft", T.ft[:, 0:4 * K], T.mm[:].indirect(T["rql%d" % t][:]), AF.Copy)
            qf, sf = T["qf%d" % t], T["sf%d" % t]
            quant(128, "ft ftz", "qf%d" % t, qf[:, K:K + 128], sf[:, K:K + 128], T.ft[:])
            send(prv, "qf%d" % t, "land%d" % t, qf[:, 0:K].bitcast(dt.uint8), qf[:, K:2 * K].bitcast(dt.uint8), "fa%d" % t)
            send(prv, "qf%d" % t, "land%d" % t, sf[:, 0:K], sf[:, K:2 * K], "fa%d" % t)
        if t == 0:
            for b in range(4):
                ts(one, "rql%d" % L, "rq4_%d" % b, T.rq4[:, 16 * b:16 * b + 16], T.rqa[:], 4.0, AL.mult, float(b), AL.add)
                act(took(A), "mm mmz rq4_%d" % b, "fa%d" % b, T.fa[:, b:4 * A:4], T.mm[:].indirect(T.rq4[:, 16 * b:16 * b + 16]), AF.Copy)
            quant(A, "fa0 fa1 fa2 fa3", "qa", T.qa[:], T.sa[:], T.fa[:])
            send(prv, "qa land0", "land%d" % L, T.la[:].bitcast(dt.uint8), T.qa[:].bitcast(dt.uint8), "fa%d" % L, lat=TUNE["long"])
            send(prv, "qa land0", "land%d" % L, T.lb[:], T.sa[:], "fa%d" % L, lat=TUNE["long"])
        for i in range(2):
            c = slice(64 * i, 64 * i + 64)
            tt(plain(N1), "k1_%d cl" % i, "ra1_%d" % i, T.ra1[:, c], T.k1[:, h * i + 3:h * i + h:4], T.cl[:, 0:64], AL.max)
            scan(one, "ra1_%d cr" % i, "ow1_%d" % i, T.ow1[:, c], T.cr[:, 0:64], T.ra1[:, c], BIG, AL.max, AL.min)
        tt(took(N1), "ow1 ol ra1", "dg1", T.dg1[:], T.ow1[:].indirect(T.ol[:, 0:S1]), T.ra1[:], AL.is_equal)
        scan(one, "dg1 r16", "dc1", T.dc1[:], T.r16[:, 0:N1], T.dg1[:], 0.0, AL.min, AL.add)
        rk = ranking(1, T.k1, "k1_0 k1_1", 4, N1, TUNE["sg1"][t])
        act(took(N1), "ioa " + rk, "fl", T.fl[:], io[:, 0:AX].indirect(T.rk1[:]), AF.Sign, scale=-1.0, bias=K + 0.5)
        scan(one, "fl ones", "cm", T.cm[:], T.fl[:], ones[:, 0:N1], 0.0, AL.add, AL.add)
        for s in range(3):
            act(plain(N1), "cm k21", "mx3_%d idf%d" % (s, s), T.mx3[:, N1 * s:N1 * s + N1], T.cm[:], AF.Sign, scale=-1.0,
                bias=T.sb[:, K21 + s:K21 + s + 1], accum_out=T.jf[:, 4 + s:5 + s])
            ts(one, "idf%d q4" % s, "c4p%d" % s, T.c4p[:, s:16:4], T.q4[:], T.jf[:, 4 + s:5 + s], AL.add, 2.0, AL.mult)
        ho = HO + A * (t == L)
        for b in range(4):
            eq, es, o = T.qe[:, 128 * b:128 * b + 128], T.se[:, 128 * b:128 * b + 128], 512 * (1 + b)
            if t == L:
                mm("qe%d land%d" % (b, t), 1 + b, A, eq, es, T.la[:], T.lb[:])
                act(plain(A), "ps%d" % (1 + b), "C%d_%d" % (t, b), xb[:, 4 * HO + b:4 * ho:4], T.ps[:, o:o + A], AF.Copy)
            else:
                mm("qe%d qf%d land%d" % (b, t, t), 1 + b, 128, eq, es, qf[:, 0:128], sf[:, 0:128])
                act(one, "ps%d" % (1 + b), "C%d_%d" % (t, b), xb[:, 4 * CO + b:4 * XO:4], T.ps[:, o:o + K], AF.Copy)
        for i in range(2):
            c = slice(128 * i, 128 * i + 128)
            act(took(512), "%s %s src4" % (X, came), "zz%d" % i, T.zz[:, 512 * i:512 * i + 512], xb[:, 0:4 * ho].indirect(T.src4[:, 32 * i:32 * i + 32]), AF.Copy)
            quant(128, "zz%d" % i, "qz%d" % i, T.qz[:, c], T.sz[:, c], T.zz[:, 512 * i:512 * i + 512])
            for b in range(4):
                mm("qw sw qz%d" % i, banks[i][b], 128, T.qw[:, 128 * b:128 * b + 128], T.sw[:, 128 * b:128 * b + 128], T.qz[:, c], T.sz[:, c])
                o = 512 * banks[i][b]
                act(plain(128), "ps%d" % banks[i][b], "H%d_%d" % (t, 4 * i + b), xb[:, 4 * ho + 512 * i + b:4 * ho + 512 * i + 512:4], T.ps[:, o:o + 128], AF.Relu, scale=0.03125)
        lk = "c4p0 c4p1 c4p2"
        for b in range(4):
            lb = T.c4p[:, 4 * b:4 * b + 3]
            tt(took(K), "k0_0 k0_1 cl " + lk, "ra2_%d" % b, T.ra2[:, b:N2:4], T.k0[:].indirect(lb), T.cl[:, b:N2:4], AL.max)
            act(took(K), "k0_0 k0_1 " + lk, "k2_%d" % b, T.k2[:, b:N2:4], T.k0[:].indirect(lb))
            if b:
                act(one, "plr_0", "plr_%d" % b, T.plr[:, b:N2:4], T.plr[:, 0:N2:4], bias=float(b))
            else:
                act(took(K), "ioa iob " + lk, "plr_0", T.plr[:, 0:N2:4], io[:, 0:P].indirect(lb), bias=float(e0))
        scan(plain(N2), "ra2 cr", "ow2", T.ow2[:], T.cr[:], T.ra2[:], BIG, AL.max, AL.min)
        tt(took(N2), "ow2 ol ra2", "dg2", T.dg2[:], T.ow2[:].indirect(T.ol[:]), T.ra2[:], AL.is_equal)
        scan(plain(96), "dg2 r16", "dc2", T.dc2[:], T.r16[:, 0:N2], T.dg2[:], 0.0, AL.min, AL.add)
        rk = ranking(2, T.k2, "k2", 1, N2, TUNE["sg2"][t])
        cp(put(N2), "plr " + rk, "tbn", T.tb[:, SO:TW].indirect(T.rk2[:]), T.plr[:])

        def gather_x():
            xp = TUNE["xp"]
            w = P // xp
            for i in range(2):
                lane4(ek, "sE", "e4_%d" % i, T.e4[:, 64 * i:64 * i + 64], e[:, e0 + h * i:e0 + h * i + h], h, CE, h * i, str(i))
                alias["X%d_%d" % (t + 1, i)] = ["Xp%d_%d" % (t + 1, j) for j in range(xp) if j * 2 // xp == i]
            for i in range(xp):
                move(i >= xp - TUNE["xv"][t], took(4 * w), "%s e4_%d" % (pool, i * 2 // xp), "Xp%d_%d" % (t + 1, i),
                     xn[:, 4 * (XO + w * i):4 * (XO + w * i + w)], xb[:].indirect(T.e4[:, w // 4 * i:w // 4 * (i + 1)]))

        if not late:
            gather_x()
            lane4("jr", "sH", "hv4", T.hv4[:], short("jr"), K, CE)
            act(took(4 * K), pool + " hv4", "hv", T.hv[:], xb[:].indirect(T.hv4[:]), AF.Copy)
        vr, v16 = T.tb[:, SO:NO], T.v16[:, 0:3]
        lane16("tbn", "sV", "v16", v16, vr, K, float(OFF))
        if not late:
            lane4("tbn", "sW", "v4", T.v4[:], vr, K, CB)
            cp(put(4 * K), "hv v4", Xn + (" Z%d " % (t + 1) + " ".join("C%d_%d" % (t + 1, b) for b in range(4)) if t < L else ""), xn[:, 0:4 * HO].indirect(T.v4[:]), T.hv[:])
        byold = t < L and not TUNE["adr"][t + 1]
        if t == 0 or byold:
            act(took(K), "tgr tgra v16", "old", short("old"), T.tgr[:].indirect(v16))
        if t == 0:
            lane16("old", "so", "o16", T.o16[:, 0:3], short("old"), K)
            cp(put(K), "old o16", "at", T.at[:].indirect(T.o16[:, 0:3]), short("old"))
            cp(put(K), "tbn a16", "at", T.at[:].indirect(T.a16[:, 0:3]), vr)
        cp(put(K), "a1 v16", "tgr tgra", T.tgr[:].indirect(v16), short("a1"))
        if t < L:
            en = T["ee%d" % (t + 1)]
            tt(took(K), "en%d idu v16" % (t + 1), "ve", short("ve"), T.idu[:, 0:HO].indirect(v16), en[:, SO:NO], AL.max)
            zk = "old" if byold else "z48"
            cp(put(K), zk + " v16", "tbp", T.tb[:, OFF:SO].indirect(v16), short(zk))
            cp(put(K), "ve v16", "ee%d" % (t + 1), en[:, OFF:SO].indirect(v16), short("ve"))
            if late:
                cp(put(K), "jr v16", ek, e[:, OFF:SO].indirect(v16), short("jr"))
                gather_x()
            lists(t + 1)

    xb, fin = T["xb%d" % R], TUNE["fin"]
    w = P // fin
    for i in range(fin):
        c, half = slice(w * i, w * i + w), i * 2 // fin
        quant(w, "X%d_%d" % (R, half), "qx%d qy%d" % (half, i) if i * 2 % fin == 0 else "qy%d" % i, T.qx[:, c], T.sx[:, c], xb[:, 4 * (XO + w * i):4 * (XO + w * i + w)])
        mm("qv qy%d" % i, 1 + i, w, T.qv[:], T.sv[:], T.qx[:, c], T.sx[:, c])
        move(i % 2, plain(w), "ps%d" % (1 + i), "ys%d" % i, T.ys[:, c], T.ps[:, 512 * (1 + i):512 * (1 + i) + w])
        dma("a" if i % 2 == 0 else "s", "ys%d" % i, "y%d" % i, T.y[:, c], T.ys[:, c], 1800.0)
    for i in range(2):
        dma("s", " ".join("qy%d" % j for j in range(fin) if j * 2 // fin == i), "oc%d" % i, T.oc[:, 4 * h * i:4 * h * i + 4 * h],
            T.qx[:, h * i:h * i + h].bitcast(dt.uint8), 2000.0)
    for k in range(4):
        dma("s", " ".join("qy%d" % j for j in range(fin)), "osc%d" % k, T.osc[4 * k:4 * k + 4, :], T.sx[32 * k:32 * k + 4, :])
    dma("s", "tgr", "ot", T.ot[:], T.tgr[0:128:16, XO:HO])

    ops = [(q, [x for k in rd for x in alias.get(k, [k])], [x for k in wr for x in alias.get(k, [k])], a, b, f) for q, rd, wr, a, b, f in ops]
    known = {q: {} for q in Q}
    total, wrote, readers = {}, {}, {}
    for t in range(R):
        for key, sem, src, writes in (("rql%d" % t, "rq%d" % t, prv, 1), ("land%d" % t, "fa%d" % t, nxt, 2)):
            total[sem] = writes * len(topo.engines(src, core))
            wrote[key] = (sem, total[sem], {sem: total[sem]})
    ndma = 0
    for i in arrange(ops, nload):
        q, rd, wr, _, _, fn = ops[i]
        if fn[0] == "send":
            wr = []
        toks = [wrote[k] for k in rd + wr if k in wrote]
        for k in wr:
            toks += readers.get(k, [])
        for sem, val, clock in sorted(toks, key=lambda z: -z[1]):
            if known[q].get(sem, 0) < val:
                Q[q].wait_ge(T.sem[sem], val)
                for s, x in clock.items():
                    if known[q].get(s, 0) < x:
                        known[q][s] = x
        if fn[0] == "send":
            dst = fn[1]
            rid, pid, _ = topo.addr(dst)
            g.remote_dma(fn[2], fn[3], T.sem[fn[4]], T.sem.sent, pid, rid, topo.mask(core, dst))
            total["sent"] = total.get("sent", 0) + len(topo.engines(core, dst))
            continue
        if fn[0] == "dma":
            sem, inc = "d%d" % ndma, 16
            ndma += 1
            Q[q].dma_start(fn[1], fn[2]).then_inc(T.sem[sem], 16)
        else:
            sem, inc = OWN[q], 1
            fn[1]().then_inc(T.sem[sem], 1)
        total[sem] = total.get(sem, 0) + inc
        clock = dict(known[q])
        clock[sem] = total[sem]
        tok = (sem, total[sem], clock)
        for k in rd:
            readers.setdefault(k, []).append(tok)
        for k in wr:
            wrote[k] = tok
            readers[k] = []
    for sem in sorted(total):
        if known["g"].get(sem, 0) < total[sem]:
            g.wait_ge(T.sem[sem], total[sem])
